import numpy as np
import ml_dtypes


def mxq(x, axis, fmt="e4m3"):
    dtype, down = {"e4m3": (ml_dtypes.float8_e4m3fn, 7), "e5m2": (ml_dtypes.float8_e5m2, 14)}[fmt]
    v = np.moveaxis(np.asarray(x, np.float32).astype(ml_dtypes.bfloat16).astype(np.float64), axis, -1)
    blocks = v.reshape(v.shape[:-1] + (-1, 32))
    amax = np.abs(blocks).max(-1, keepdims=True)
    byte = np.maximum(np.where(amax > 0, np.frexp(amax)[1] - 1 + 127, 0) - down, 1)
    scale = np.exp2(byte - 127.0)
    codes = (blocks / scale).astype(np.float32).astype(dtype).astype(np.float64)
    return np.moveaxis((codes * scale).reshape(v.shape), -1, axis)


WIDE = False


def mx_kscale(k):
    if not WIDE:
        return np.ones(k)
    levels = np.array([18, -18])
    if k % 512:
        return np.exp2(np.random.permutation(np.resize(levels, k // 32))).repeat(32)
    a = np.empty((k // 512, 16))
    for p in range(k // 512):
        a[p, :8] = np.random.permutation(np.resize(levels, 8))
        for g in range(8):
            far = levels[np.abs(levels - a[p, g]) >= 10]
            a[p, g + 8] = far[np.random.randint(len(far))]
    return np.exp2(a.ravel()).repeat(32)


def f64(x):
    return np.asarray(x).astype(np.float64)


def striped(idx):
    return np.tile(np.asarray(idx).reshape(-1, 16).T, (8, 1)).astype(np.uint16)


def unstriped(offs):
    return offs[:16].T.reshape(-1).astype(np.int64)


E2M1 = np.array([0.0, 0.5, 1.0, 1.5, 2.0, 3.0, 4.0, 6.0, -0.0, -0.5, -1.0, -1.5, -2.0, -3.0, -4.0, -6.0])


def pack_weight(w, fmt):
    k, n = w.shape
    w = f64(np.asarray(w, np.float32).astype(ml_dtypes.bfloat16)).reshape(k // 32, 32, n)
    amax = np.abs(w).max(1)
    if fmt == "e4m3":
        byte = np.frexp(amax)[1] - 1 + 127 - 7
    else:
        mant, ex = np.frexp(amax / 6.0)
        byte = np.where(mant > 0.5, ex, ex - 1) + 127
    byte = np.clip(np.where(amax > 0, byte, 1), 1, 254)
    scaled = (w * np.exp2(127.0 - byte)[:, None, :]).reshape(k, n).astype(np.float32)
    by_word = np.ascontiguousarray(scaled.reshape(k // 512, 128, 4, n).transpose(0, 1, 3, 2))
    if fmt == "e4m3":
        words = by_word.astype(ml_dtypes.float8_e4m3fn).view(np.uint8)
    else:
        c = by_word.astype(ml_dtypes.float4_e2m1fn).view(np.uint8) & 0xF
        words = (c[..., 0::2] | (c[..., 1::2] << 4)).reshape(k // 512, 128, 2 * n)
    return np.ascontiguousarray(words), np.ascontiguousarray(byte.astype(np.uint8).reshape(k // 512, 16, n))


def unpack_weight(words, scales, fmt):
    g, _, n = scales.shape
    words = np.ascontiguousarray(words).reshape(g, 128, n, -1)
    if fmt == "e4m3":
        vals = words.view(ml_dtypes.float8_e4m3fn).astype(np.float64)
    else:
        nib = np.empty((g, 128, n, 4), np.uint8)
        nib[..., 0::2] = words & 0xF
        nib[..., 1::2] = words >> 4
        vals = E2M1[nib]
    vals = vals * np.repeat(np.exp2(scales.astype(np.float64) - 127.0), 8, axis=1)[..., None]
    return vals.transpose(0, 1, 3, 2).reshape(g * 512, n)


def planes(y):
    n, m = y.shape
    v = y.astype(np.float32).astype(ml_dtypes.bfloat16).astype(np.float64).reshape(n // 32, 32, m)
    top = np.abs(v).max(1)
    byte = np.clip(np.where(top > 0, np.frexp(top)[1] - 1 + 127 - 7, 1), 1, 254)
    codes = (v * np.exp2(127.0 - byte)[:, None, :]).reshape(n, m).astype(np.float32).astype(ml_dtypes.float8_e4m3fn).view(np.uint8)
    words = codes.reshape(n // 512, 128, 4, m).transpose(0, 1, 3, 2)
    return np.ascontiguousarray(words), np.ascontiguousarray(byte.astype(np.uint8).reshape(n // 512, 16, m))


def setup_inputs():
    n = np.random.standard_normal
    uni = np.random.uniform
    idx = np.random.permutation(2048)[:512]
    f_d = mx_kscale(512)
    f_e = mx_kscale(512)
    f_i = np.ones(2048)
    f_i[idx] = mx_kscale(512)
    vT_ = pack_weight(n((512, 2048)) / np.sqrt(512) / f_e[:, None], "e4m3")
    return {
        "qT": (0.35 * n((512, 1024)) * f_d[:, None]).astype(np.float32),
        "kT": (n((512, 2048)) / np.sqrt(512) / f_d[:, None] * f_i[None, :]).astype(np.float32),
        "doT": (n((512, 1024)) * f_e[:, None]).astype(np.float32),
        "vT_words": vT_[0],
        "vT_scales": vT_[1],
        "us": (uni(0.75, 1.3, (1024, 1))).astype(np.float32),
        "ts": np.tile(uni(0.75, 1.3, 2048) / f_i, (128, 1)).astype(np.float32),
        "tv": np.tile(uni(0.75, 1.3, 2048), (128, 1)).astype(np.float32),
        "wt": (uni(0.75, 1.3, (1024, 1))).astype(np.float32),
        "offs": striped(idx),
    }


def reference(qT, kT, doT, vT_words, vT_scales, us, ts, tv, wt, offs):
    idx = unstriped(offs)
    kT_i = f64(kT)[:, idx]
    vT = unpack_weight(vT_words, vT_scales, "e4m3")
    vT_i = vT[:, idx]
    ts_i = f64(ts)[:1][:, idx]
    tv_i = f64(tv)[:1][:, idx]
    a = mxq(f64(qT), 0, "e4m3").T @ mxq(kT_i, 0, "e4m3")
    z = f64(us) * ts_i * a
    m = (z).max(-1, keepdims=True)
    x = np.exp(z - m)
    tot = (x).sum(-1, keepdims=True)
    p = x / tot
    b = mxq(f64(doT), 0, "e5m2").T @ vT_i
    dp = f64(wt) * tv_i * b
    delta = (p * dp).sum(-1, keepdims=True)
    g = f64(us) * ts_i * p * (dp - delta)
    out_0 = mxq(g, 1, "e5m2") @ mxq(kT_i, 1, "e4m3").T
    return (out_0,) + planes(out_0)

@@ -1,0 +1,379 @@
+from contextlib import ExitStack
+
+import concourse.mybir as mybir
+from concourse.masks import make_identity
+
+F32 = mybir.dt.float32
+BF16 = mybir.dt.bfloat16
+I32 = mybir.dt.int32
+U32 = mybir.dt.uint32
+U16 = mybir.dt.uint16
+U8 = mybir.dt.uint8
+E4M3 = mybir.dt.float8_e4m3fn_x4
+E5M2 = mybir.dt.float8_e5m2_x4
+ALU = mybir.AluOpType
+ACT = mybir.ActivationFunctionType
+AXIS = mybir.AxisListType
+
+P = 128
+PACK = 4
+PASS = P * PACK
+TOKENS = 2048
+SLOTS = 512
+FEATURES = 512
+QUERIES = 1024
+HALVES = QUERIES // PASS
+TILES = QUERIES // P
+
+FLOPS = 3 * 2 * QUERIES * SLOTS * FEATURES
+
+MX_BANKS = 2
+ROW_BANKS = 4
+GRAD_BANKS = 2
+K_SPLIT = 512
+Q0_SPLIT = 128
+DO0_SPLIT = 128
+Q1_SPLIT = 512
+DO1_SPLIT = 0
+OUT0_SPLIT = 0
+OUT1_SPLIT = 384
+VS_TAG = ""
+DO_FIRST = 1
+PIECE = 256
+AHEAD = 2
+Q1_AT = 3
+KT_AT = 0
+SC1_AT = 0
+SC_RATE = 1
+GROUP = 2
+Q0_PIECES = 2
+GATE_ON_SCALAR = 0
+KT_TAG = ""
+LAG = 2
+DO1_STEP = 0
+OUT0_LAG = 0
+SHIFT_ON_VECTOR = (4, 5, 6, 7)
+
+
+def tile_attend_gsma_q_pl_kernel(
+    tc, qT, kT, doT, vT_words, vT_scales, us, ts, tv, wt, offs, out_0, out_1, out_2
+):
+    nc = tc.nc
+    with ExitStack() as ctx:
+        keep = ctx.enter_context(tc.tile_pool(name="keep", bufs=1))
+        work = ctx.enter_context(tc.tile_pool(name="work", bufs=3))
+        psum = ctx.enter_context(tc.psum_pool(name="psum", bufs=2))
+
+        offsets = keep.tile([P, SLOTS // 16], U16, name="offsets")
+        nc.sync.dma_start(offsets[:], offs)
+        ts_row = keep.tile([1, TOKENS], F32, name="ts_row")
+        tv_row = keep.tile([1, TOKENS], F32, name="tv_row")
+        us_sb = keep.tile([P, HALVES, PACK], F32, name="us_sb")
+        wt_sb = keep.tile([P, HALVES, PACK], F32, name="wt_sb")
+        nc.sync.dma_start(ts_row[:], ts[0:1, :])
+        nc.sync.dma_start(tv_row[:], tv[0:1, :])
+        k_planes = kT.rearrange("(p t) c -> t p c", t=PACK)
+        k_win = [keep.tile([P, TOKENS], F32, name=f"k_win{t}") for t in range(PACK)]
+        nc.sync.dma_start(k_win[0][:], k_planes[0])
+        nc.sync.dma_start(us_sb[:], us.rearrange("(h p t) o -> p h (t o)", h=HALVES, t=PACK))
+        nc.sync.dma_start(wt_sb[:], wt.rearrange("(h p t) o -> p h (t o)", h=HALVES, t=PACK))
+        nc.sync.dma_start(k_win[1][:], k_planes[1])
+        nc.sync.dma_start(k_win[2][:], k_planes[2])
+        vs_win = keep.tile([P, TOKENS], U8, name="vs_win")
+        nc.gpsimd.memset(vs_win[:].bitcast(I32), 0)
+        for quad in range(4):
+            nc.sync.dma_start(
+                vs_win[32 * quad : 32 * quad + 4, :].bitcast(I32),
+                vT_scales[0, 4 * quad : 4 * quad + 4, :].bitcast(I32),
+            )
+        nc.sync.dma_start(k_win[3][:], k_planes[3])
+
+        q_first = [keep.tile([P, PACK, PASS // 2], F32, name=f"q_first{i}", align_bytes=64) for i in range(2)]
+        do_raw = [keep.tile([P, PACK, PASS], F32, name="do_raw0")]
+        vw_win = keep.tile([P, TOKENS], I32, name="vw_win")
+        q_rows = qT.rearrange("(p j) (h r) -> h p j r", j=PACK, h=HALVES)
+        do_rows = doT.rearrange("(p j) (h r) -> h p j r", j=PACK, h=HALVES)
+        for i in range(2):
+            nc.sync.dma_start(q_first[i][:], q_rows[0][:, :, i * PASS // 2 : (i + 1) * PASS // 2])
+        if DO_FIRST:
+            nc.sync.dma_start(do_raw[0][:], do_rows[0])
+        nc.sync.dma_start(vw_win[:], vT_words[0].rearrange("p c l -> p (c l)").bitcast(I32))
+        if not DO_FIRST:
+            nc.sync.dma_start(do_raw[0][:], do_rows[0])
+
+        ident = keep.tile([P, P], F32, name="ident")
+        make_identity(nc, ident[:])
+        ts_win = keep.tile([P, TOKENS], F32, name="ts_win")
+        tv_win = keep.tile([P, TOKENS], F32, name="tv_win")
+        nc.vector.memset(ts_win[:], 0.0)
+        nc.vector.memset(tv_win[:], 0.0)
+        warm = keep.tile([P, 1], F32, name="warm")
+        nc.scalar.activation(warm[:], ident[:, 0:1], ACT.Exp)
+        nc.scalar.activation(ts_win[0:1, :], ts_row[:], ACT.Copy)
+        nc.scalar.activation(tv_win[0:1, :], tv_row[:], ACT.Copy)
+
+        def pick(window, name):
+            picked = keep.tile([P, SLOTS], F32, name=name + "_picked")
+            nc.vector.tensor_copy(picked[:], window[:].indirect(offsets[:]))
+            return picked
+
+        def columns_of(view, name):
+            turned = psum.tile([P, PACK, P], F32, name=name + "_turned", tag="dp", bufs=ROW_BANKS)
+            for t in range(PACK):
+                nc.tensor.transpose(turned[:, t, :], view[:, t, :], ident[:])
+            columns = keep.tile([P, PACK], F32, name=name + "_columns")
+            nc.scalar.copy(columns[:], turned[:, :, 0])
+            return columns
+
+        k_picked = keep.tile([P, PACK, SLOTS], BF16, name="k_picked", align_bytes=64)
+
+        def gather_keys(t):
+            nc.vector.tensor_copy(k_picked[:, t, :], k_win[t][:].indirect(offsets[:]))
+
+        def turn_keys(pair):
+            bank = psum.tile([P, 2, 2, P], F32, name=f"kt_bank{pair}", tag="grad", bufs=GRAD_BANKS)
+            for e in range(2):
+                words = k_picked[:, 2 * pair + e, :].bitcast(F32).rearrange("p (s u) -> p u s", u=2)
+                for u in range(2):
+                    nc.tensor.transpose(bank[:, e, u, :], words[:, u, :], ident[:])
+            nc.scalar.copy(kt_woven[:, :, 2 * pair : 2 * pair + 2, :], bank[:].rearrange("s e u p -> s p e u"))
+
+        gather_keys(0)
+        ts_picked = pick(ts_win, "ts")
+        ts_place = columns_of(ts_picked[:].rearrange("p (s t) -> p t s", t=PACK), "ts_place")
+        spread = psum.tile([P, PACK, P], F32, name="ts_spread", tag="dp", bufs=ROW_BANKS)
+        for u in range(PACK):
+            nc.tensor.transpose(spread[:, u, :], ts_place[:, u : u + 1].to_broadcast([P, P]), ident[:])
+        ts_rows = keep.tile([P, PACK, P], F32, name="ts_rows")
+        nc.scalar.copy(ts_rows[:], spread[:])
+        tv_block = columns_of(pick(tv_win, "tv")[:].rearrange("p (j s) -> p j s", j=PACK), "tv_block")
+        uswt = keep.tile([P, HALVES, PACK], F32, name="uswt")
+        nc.vector.tensor_tensor(uswt[:], us_sb[:], wt_sb[:], ALU.mult)
+        gather_keys(1)
+        gather_keys(2)
+        gather_keys(3)
+        q_second = keep.tile([P, PACK, PASS], F32, name="q_raw1", tag="k_win0")
+        do_raw.append(keep.tile([P, PACK, PASS], F32, name="do_raw1", tag="k_win1"))
+        nc.sync.dma_start(q_second[:], q_rows[1])
+        nc.sync.dma_start(do_raw[1][:], do_rows[1])
+
+        def weave(src_tile, name, split):
+            woven = keep.tile([P, PASS, PACK], BF16, name=name + "_woven", align_bytes=64)
+            src = src_tile[:].rearrange("p t (c i) -> p c t i", i=4)
+            dst = woven[:].rearrange("p (c i) t -> p c t i", i=4)
+            if split > 0:
+                nc.vector.tensor_copy(dst[:, : split // 4], src[:, : split // 4])
+            for c in range(split, PASS, PIECE):
+                part = slice(c // 4, min(c + PIECE, PASS) // 4)
+                nc.scalar.copy(dst[:, part], src[:, part])
+            return woven[:].rearrange("p c t -> p (c t)")
+
+        def weave_dealt(raw, name, split):
+            woven = keep.tile([P, PACK, P, PACK], BF16, name=name + "_woven", align_bytes=64)
+            src = raw[:].rearrange("p j (m t) -> p m j t", t=PACK)
+            dst = woven[:].rearrange("p t m j -> p m j t")
+            if split > 0:
+                nc.vector.tensor_copy(dst[:, : split // 4], src[:, : split // 4])
+            for c in range(split, PASS, PIECE):
+                part = slice(c // 4, min(c + PIECE, PASS) // 4)
+                nc.scalar.copy(dst[:, part], src[:, part])
+            return woven[:].rearrange("p t m j -> p (t m j)")
+
+        def quantise(name, source, fmt, tag="", pieces=1):
+            codes = keep.tile([P, PASS], U32, name=name + "_codes", align_bytes=64, tag=tag)
+            scales = keep.tile([P, PASS], U8, name=name + "_scales", align_bytes=64)
+            width = PASS // pieces
+            for i in range(pieces):
+                cols = slice(i * width, (i + 1) * width)
+                nc.vector.quantize_mx(
+                    out=codes[:, cols].bitcast(fmt), scales=scales[:, cols],
+                    in_=source[:, i * width * PACK : (i + 1) * width * PACK],
+                )
+            return codes, scales
+
+        k_woven = weave(k_picked, "k", K_SPLIT)
+        q_dealt = keep.tile([P, PACK, P, PACK], BF16, name="q0_woven", align_bytes=64)
+        for i in range(2):
+            nc.scalar.copy(
+                q_dealt[:].rearrange("p t m j -> p m j t")[:, i * P // 2 : (i + 1) * P // 2],
+                q_first[i][:].rearrange("p j (m t) -> p m j t", t=PACK),
+            )
+        q_woven = q_dealt[:].rearrange("p t m j -> p (t m j)")
+        k_codes, k_scales = quantise("k", k_woven, E4M3)
+        q_mx = [quantise("q0", q_woven, E4M3, pieces=Q0_PIECES)]
+        kt_woven = keep.tile([P, P, PACK, 2], F32, name="kt_woven", align_bytes=64, tag="q_first1")
+        turn_keys(0)
+        turn_keys(1)
+        v_scales = keep.tile([P, SLOTS], U8, name="v_scales", align_bytes=64, tag=VS_TAG)
+        nc.vector.tensor_copy(v_scales[:], vs_win[:].indirect(offsets[:]))
+
+
+        result = [keep.tile([P, PACK, FEATURES], F32, name=f"result{h}", tag=f"k_win{2 + h}") for h in range(HALVES)]
+        out_rows = out_0.rearrange("(h p t) d -> h t p d", h=HALVES, t=PACK)
+        totals = [keep.tile([P, GROUP], F32, name=f"totals{i}") for i in range(TILES // GROUP)]
+        state = {}
+
+        def slot_major(name, codes, scales, moving, fmt, token_scale):
+            scaled = []
+            for j in range(PACK):
+                cols = slice(j * P, (j + 1) * P)
+                bank = psum.tile([P, PASS], F32, name=name + "_bank", tag="mx", bufs=MX_BANKS)
+                nc.tensor.matmul_mx(
+                    out=bank[:], lhsT=codes[:, cols].bitcast(E4M3), lhsT_scale=scales[:, cols],
+                    rhs=moving[0][:].bitcast(fmt), rhs_scale=moving[1][:], start=True, stop=True,
+                )
+                block = keep.tile([P, PACK, P], F32, name=f"{name}_block{j}")
+                nc.scalar.activation(
+                    block[:], bank[:].rearrange("s (m t) -> s t m", t=PACK), ACT.Copy, scale=token_scale[:, j : j + 1]
+                )
+                scaled.append(block)
+            return scaled
+
+        def turn(blocks, t, tag, bufs):
+            bank = psum.tile([P, PACK, P], F32, name=tag + "_bank", tag=tag, bufs=bufs)
+            for j in range(PACK):
+                nc.tensor.transpose(bank[:, j, :], blocks[j][:, t, :], ident[:])
+            return bank[:].rearrange("r j (s u) -> r u (j s)", u=PACK)
+
+        def scores(n):
+            h, t = divmod(n, PACK)
+            cols = slice(t * P, (t + 1) * P)
+            bank = psum.tile([P, SLOTS], F32, name="score_bank", tag="dp", bufs=ROW_BANKS)
+            nc.tensor.matmul_mx(
+                out=bank[:], lhsT=q_mx[h][0][:, cols].bitcast(E4M3), lhsT_scale=q_mx[h][1][:, cols],
+                rhs=k_codes[:].bitcast(E4M3), rhs_scale=k_scales[:], start=True, stop=True,
+            )
+            z = work.tile([P, PACK, P], F32, name="z")
+            nc.vector.scalar_tensor_tensor(
+                z[:], bank[:].rearrange("r (s u) -> r u s", u=PACK), us_sb[:, h, t : t + 1], ts_rows[:],
+                ALU.mult, ALU.mult,
+            )
+            state[("z", n)] = z
+
+        def softmax(n):
+            z = state[("z", n)][:].rearrange("r u s -> r (u s)")
+            neg_max = work.tile([P, 1], F32, name="neg_max")
+            nc.vector.tensor_reduce(neg_max[:], z, AXIS.X, ALU.max, negate=True)
+            x = work.tile([P, SLOTS], F32, name="x", bufs=TILES)
+            nc.scalar.activation(
+                x[:], z, ACT.Exp, bias=neg_max[:], accum_out=totals[n // GROUP][:, n % GROUP : n % GROUP + 1]
+            )
+            state[("x", n)] = x
+
+        def row_factors(i):
+            inverse = keep.tile([P, GROUP], F32, name=f"inverse{i}")
+            nc.vector.reciprocal(inverse[:], totals[i][:])
+            gate = keep.tile([P, GROUP], F32, name=f"gate{i}")
+            rows = uswt[:].rearrange("p h t -> p (h t)")[:, i * GROUP : (i + 1) * GROUP]
+            if GROUP == 1 and GATE_ON_SCALAR:
+                nc.scalar.activation(gate[:], inverse[:], ACT.Copy, scale=rows)
+            else:
+                nc.vector.tensor_tensor(gate[:], inverse[:], rows, ALU.mult)
+            neg_inverse = keep.tile([P, GROUP], F32, name=f"neg_inverse{i}")
+            nc.scalar.activation(neg_inverse[:], inverse[:], ACT.Copy, scale=-1.0)
+            for e in range(GROUP):
+                state[("rows", i * GROUP + e)] = (gate[:, e : e + 1], neg_inverse[:, e : e + 1])
+
+        def weighted(n):
+            h, t = divmod(n, PACK)
+            dp = turn(state[("b", h)], t, "dp", ROW_BANKS)
+            pdp = work.tile([P, PACK, P], F32, name="pdp")
+            delta = work.tile([P, 1], F32, name="delta")
+            nc.vector.scalar_tensor_tensor(
+                pdp[:], dp, state[("rows", n)][0],
+                state[("x", n)][:].rearrange("r (u s) -> r u s", u=PACK),
+                ALU.mult, ALU.mult, accum_out=delta[:],
+            )
+            state[("pdp", n)] = (pdp, delta)
+
+        def centre(n):
+            h, t = divmod(n, PACK)
+            pdp, delta = state[("pdp", n)]
+            shift = work.tile([P, SLOTS], F32, name="shift")
+            if n in SHIFT_ON_VECTOR:
+                nc.vector.tensor_scalar(
+                    shift[:], state[("x", n)][:], delta[:], state[("rows", n)][1], ALU.mult, ALU.mult
+                )
+            else:
+                factor = work.tile([P, 1], F32, name="factor")
+                nc.scalar.activation(factor[:], delta[:], ACT.Copy, scale=state[("rows", n)][1])
+                nc.scalar.activation(shift[:], state[("x", n)][:], ACT.Copy, scale=factor[:])
+            bank = psum.tile([P, PACK, P], F32, name="grad_bank", tag="grad", bufs=GRAD_BANKS)
+            for u in range(PACK):
+                nc.tensor.matmul(bank[:, u, :], pdp[:, u, :], ident[:], start=True, stop=False, is_transpose=True)
+                nc.tensor.matmul(
+                    bank[:, u, :], shift[:, u * P : (u + 1) * P], ident[:], start=False, stop=True, is_transpose=True
+                )
+            state[("grad", n)] = bank
+
+        def scale_gradient(n):
+            g = work.tile([P, P, PACK], BF16, name="g", align_bytes=64)
+            nc.vector.tensor_tensor(
+                g[:], state[("grad", n)][:].rearrange("s u r -> s r u"),
+                ts_place[:].unsqueeze(1).to_broadcast([P, P, PACK]), ALU.mult,
+            )
+            state[("g", n)] = g
+
+        def query_gradient(n):
+            h, t = divmod(n, PACK)
+            g_codes = work.tile([P, P], U32, name="g_codes", align_bytes=64)
+            g_scales = work.tile([P, P], U8, name="g_scales", align_bytes=64)
+            nc.vector.quantize_mx(
+                out=g_codes[:].bitcast(E5M2), scales=g_scales[:], in_=state[("g", n)][:].rearrange("s r u -> s (r u)")
+            )
+            bank = psum.tile([P, FEATURES], F32, name="out_bank", tag="mx", bufs=MX_BANKS)
+            nc.tensor.matmul_mx(
+                out=bank[:], lhsT=g_codes[:].bitcast(E5M2), lhsT_scale=g_scales[:],
+                rhs=state["kt"][0][:].bitcast(E4M3), rhs_scale=state["kt"][1][:], start=True, stop=True,
+            )
+            nc.scalar.copy(result[h][:, t, :], bank[:])
+            nc.sync.dma_start(out_rows[h, t], result[h][:, t, :])
+
+        def planes(h, woven):
+            codes, scales = quantise(f"plane{h}", woven, E4M3)
+            nc.sync.dma_start(out_1[h].rearrange("p c l -> p (c l)").bitcast(I32), codes[:].bitcast(I32))
+            for quad in range(4):
+                queue = nc.scalar if (h == HALVES - 1 and quad % 2 == 1) else nc.sync
+                queue.dma_start(
+                    out_2[h, 4 * quad : 4 * quad + 4, :].bitcast(I32),
+                    scales[32 * quad : 32 * quad + 4, :].bitcast(I32),
+                )
+
+        def live(n):
+            return 0 <= n < TILES
+
+        v_codes = keep.tile([P, SLOTS], U32, name="v_codes", align_bytes=64)
+        nc.vector.tensor_copy(v_codes[:], vw_win[:].bitcast(U32).indirect(offsets[:]))
+        do_mx = quantise("do0", weave(do_raw[0], "do0", DO0_SPLIT), E5M2)
+        state[("b", 0)] = slot_major("b0", v_codes, v_scales, do_mx, E5M2, tv_block)
+
+        def forward(n):
+            scores(n)
+            softmax(n)
+            if n % GROUP == GROUP - 1:
+                row_factors(n // GROUP)
+
+        for n in range(PACK):
+            forward(n)
+            if n == Q1_AT:
+                q_mx.append(quantise("q1", weave_dealt(q_second, "q1", Q1_SPLIT), E4M3))
+        done = PACK
+        for step in range(TILES + LAG):
+            if step == KT_AT:
+                state["kt"] = quantise("kt", kt_woven[:].rearrange("s p t u -> s (p t u)").bitcast(BF16), E4M3, KT_TAG)
+            if step == DO1_STEP:
+                do_mx = quantise("do1", weave(do_raw[1], "do1", DO1_SPLIT), E5M2)
+                state[("b", 1)] = slot_major("b1", v_codes, v_scales, do_mx, E5M2, tv_block)
+            if live(step):
+                weighted(step)
+                centre(step)
+            if live(step - LAG):
+                scale_gradient(step - LAG)
+                query_gradient(step - LAG)
+            if step >= SC1_AT:
+                for n in range(done, min(TILES, done + SC_RATE)):
+                    forward(n)
+                done = min(TILES, done + SC_RATE)
+            if step == PACK - 1 + LAG + OUT0_LAG:
+                planes(0, weave(result[0], "result0", OUT0_SPLIT))
+        planes(1, weave(result[1], "result1", OUT1_SPLIT))

@@ -35,24 +35,33 @@ Q0_SPLIT = 128
 DO0_SPLIT = 128
 Q1_SPLIT = 512
 DO1_SPLIT = 0
-OUT0_SPLIT = 0
-OUT1_SPLIT = 384
-VS_TAG = ""
-DO_FIRST = 1
-PIECE = 256
+OUT0_SPLIT = 256
+OUT1_SPLIT = 320
+VS_TAG = "q0_woven"
+ORDER = "dvqe"
+V_AT = 0
+PIECE = 128
 AHEAD = 2
 Q1_AT = 3
 KT_AT = 0
 SC1_AT = 0
 SC_RATE = 1
+B_HALVES = ()
+SHIFT_ON_POOL = ()
+FIRST = 4
+DO1_AT = 4
+B1_AT = 4
+REPEAT = (1,2,3,4,5,6)
+FUSED = ()
+LATE_B1 = 0
 GROUP = 2
-Q0_PIECES = 2
+Q0_PIECES = 1
 GATE_ON_SCALAR = 0
 KT_TAG = ""
 LAG = 2
 DO1_STEP = 0
-OUT0_LAG = 0
-SHIFT_ON_VECTOR = (4, 5, 6, 7)
+OUT0_LAG = 4
+SHIFT_ON_VECTOR = (4,5,6,7)
 
 
 def tile_attend_gsma_q_pl_kernel(
@@ -66,7 +75,7 @@ def tile_attend_gsma_q_pl_kernel(
 
         offsets = keep.tile([P, SLOTS // 16], U16, name="offsets")
         nc.sync.dma_start(offsets[:], offs)
-        ts_row = keep.tile([1, TOKENS], F32, name="ts_row")
+        ts_row = keep.tile([1, TOKENS], F32, name="ts_row", tag="k_win_r0")
         tv_row = keep.tile([1, TOKENS], F32, name="tv_row")
         us_sb = keep.tile([P, HALVES, PACK], F32, name="us_sb")
         wt_sb = keep.tile([P, HALVES, PACK], F32, name="wt_sb")
@@ -89,17 +98,22 @@ def tile_attend_gsma_q_pl_kernel(
         nc.sync.dma_start(k_win[3][:], k_planes[3])
 
         q_first = [keep.tile([P, PACK, PASS // 2], F32, name=f"q_first{i}", align_bytes=64) for i in range(2)]
-        do_raw = [keep.tile([P, PACK, PASS], F32, name="do_raw0")]
+        do_raw = [keep.tile([P, PACK, PASS], F32, name=f"do_raw{h}") for h in range(HALVES)]
         vw_win = keep.tile([P, TOKENS], I32, name="vw_win")
         q_rows = qT.rearrange("(p j) (h r) -> h p j r", j=PACK, h=HALVES)
         do_rows = doT.rearrange("(p j) (h r) -> h p j r", j=PACK, h=HALVES)
         for i in range(2):
             nc.sync.dma_start(q_first[i][:], q_rows[0][:, :, i * PASS // 2 : (i + 1) * PASS // 2])
-        if DO_FIRST:
-            nc.sync.dma_start(do_raw[0][:], do_rows[0])
-        nc.sync.dma_start(vw_win[:], vT_words[0].rearrange("p c l -> p (c l)").bitcast(I32))
-        if not DO_FIRST:
-            nc.sync.dma_start(do_raw[0][:], do_rows[0])
+        q_second = keep.tile([P, PACK, PASS], F32, name="q_raw1")
+        for which in ORDER:
+            if which == "d":
+                nc.sync.dma_start(do_raw[0][:], do_rows[0])
+            if which == "v":
+                nc.sync.dma_start(vw_win[:], vT_words[0].rearrange("p c l -> p (c l)").bitcast(I32))
+            if which == "q":
+                nc.sync.dma_start(q_second[:], q_rows[1])
+            if which == "e":
+                nc.sync.dma_start(do_raw[1][:], do_rows[1])
 
         ident = keep.tile([P, P], F32, name="ident")
         make_identity(nc, ident[:])
@@ -117,11 +131,11 @@ def tile_attend_gsma_q_pl_kernel(
             nc.vector.tensor_copy(picked[:], window[:].indirect(offsets[:]))
             return picked
 
-        def columns_of(view, name):
+        def columns_of(view, name, tag=""):
             turned = psum.tile([P, PACK, P], F32, name=name + "_turned", tag="dp", bufs=ROW_BANKS)
             for t in range(PACK):
                 nc.tensor.transpose(turned[:, t, :], view[:, t, :], ident[:])
-            columns = keep.tile([P, PACK], F32, name=name + "_columns")
+            columns = keep.tile([P, PACK], F32, name=name + "_columns", tag=tag, align_bytes=64)
             nc.scalar.copy(columns[:], turned[:, :, 0])
             return columns
 
@@ -139,30 +153,29 @@ def tile_attend_gsma_q_pl_kernel(
             nc.scalar.copy(kt_woven[:, :, 2 * pair : 2 * pair + 2, :], bank[:].rearrange("s e u p -> s p e u"))
 
         gather_keys(0)
-        ts_picked = pick(ts_win, "ts")
-        ts_place = columns_of(ts_picked[:].rearrange("p (s t) -> p t s", t=PACK), "ts_place")
-        spread = psum.tile([P, PACK, P], F32, name="ts_spread", tag="dp", bufs=ROW_BANKS)
-        for u in range(PACK):
-            nc.tensor.transpose(spread[:, u, :], ts_place[:, u : u + 1].to_broadcast([P, P]), ident[:])
+        ts_block = columns_of(pick(ts_win, "ts")[:].rearrange("p (j s) -> p j s", j=PACK), "ts")
+        spread = psum.tile([P, PACK, P], F32, name="ts_spread", tag="mx", bufs=MX_BANKS)
+        for j in range(PACK):
+            nc.tensor.transpose(spread[:, j, :], ts_block[:, j : j + 1].to_broadcast([P, P]), ident[:])
         ts_rows = keep.tile([P, PACK, P], F32, name="ts_rows")
-        nc.scalar.copy(ts_rows[:], spread[:])
-        tv_block = columns_of(pick(tv_win, "tv")[:].rearrange("p (j s) -> p j s", j=PACK), "tv_block")
+        nc.scalar.copy(ts_rows[:], spread[:].rearrange("r j (s u) -> r u (j s)", u=PACK))
+        neg_us = keep.tile([P, HALVES, PACK], F32, name="neg_us")
+        if B_HALVES:
+            nc.vector.tensor_scalar(neg_us[:], us_sb[:], -1.0, None, ALU.mult)
         uswt = keep.tile([P, HALVES, PACK], F32, name="uswt")
         nc.vector.tensor_tensor(uswt[:], us_sb[:], wt_sb[:], ALU.mult)
         gather_keys(1)
+        tv_block = columns_of(pick(tv_win, "tv")[:].rearrange("p (j s) -> p j s", j=PACK), "tv_block")
         gather_keys(2)
         gather_keys(3)
-        q_second = keep.tile([P, PACK, PASS], F32, name="q_raw1", tag="k_win0")
-        do_raw.append(keep.tile([P, PACK, PASS], F32, name="do_raw1", tag="k_win1"))
-        nc.sync.dma_start(q_second[:], q_rows[1])
-        nc.sync.dma_start(do_raw[1][:], do_rows[1])
 
-        def weave(src_tile, name, split):
+        def weave(src_tile, name, split, vpiece=PASS):
             woven = keep.tile([P, PASS, PACK], BF16, name=name + "_woven", align_bytes=64)
             src = src_tile[:].rearrange("p t (c i) -> p c t i", i=4)
             dst = woven[:].rearrange("p (c i) t -> p c t i", i=4)
-            if split > 0:
-                nc.vector.tensor_copy(dst[:, : split // 4], src[:, : split // 4])
+            for c in range(0, split, vpiece):
+                part = slice(c // 4, min(c + vpiece, split) // 4)
+                nc.vector.tensor_copy(dst[:, part], src[:, part])
             for c in range(split, PASS, PIECE):
                 part = slice(c // 4, min(c + PIECE, PASS) // 4)
                 nc.scalar.copy(dst[:, part], src[:, part])
@@ -194,21 +207,28 @@ def tile_attend_gsma_q_pl_kernel(
         k_woven = weave(k_picked, "k", K_SPLIT)
         q_dealt = keep.tile([P, PACK, P, PACK], BF16, name="q0_woven", align_bytes=64)
         for i in range(2):
-            nc.scalar.copy(
-                q_dealt[:].rearrange("p t m j -> p m j t")[:, i * P // 2 : (i + 1) * P // 2],
-                q_first[i][:].rearrange("p j (m t) -> p m j t", t=PACK),
-            )
+            if 0 in B_HALVES:
+                nc.scalar.copy(
+                    q_dealt[:].rearrange("p a b t -> p (a b) t").rearrange("p (c i) t -> p c t i", i=4)[:, i * P // 2 : (i + 1) * P // 2],
+                    q_first[i][:].rearrange("p t (c i) -> p c t i", i=4),
+                )
+            else:
+                nc.scalar.copy(
+                    q_dealt[:].rearrange("p t m j -> p m j t")[:, i * P // 2 : (i + 1) * P // 2],
+                    q_first[i][:].rearrange("p j (m t) -> p m j t", t=PACK),
+                )
         q_woven = q_dealt[:].rearrange("p t m j -> p (t m j)")
         k_codes, k_scales = quantise("k", k_woven, E4M3)
         q_mx = [quantise("q0", q_woven, E4M3, pieces=Q0_PIECES)]
         kt_woven = keep.tile([P, P, PACK, 2], F32, name="kt_woven", align_bytes=64, tag="q_first1")
         turn_keys(0)
         turn_keys(1)
+        ts_place = columns_of(ts_rows[:], "ts_place", "q_first0")
         v_scales = keep.tile([P, SLOTS], U8, name="v_scales", align_bytes=64, tag=VS_TAG)
         nc.vector.tensor_copy(v_scales[:], vs_win[:].indirect(offsets[:]))
 
 
-        result = [keep.tile([P, PACK, FEATURES], F32, name=f"result{h}", tag=f"k_win{2 + h}") for h in range(HALVES)]
+        result = [keep.tile([P, PACK, FEATURES], F32, name=f"result{h}", tag=f"k_win{h}") for h in range(HALVES)]
         out_rows = out_0.rearrange("(h p t) d -> h t p d", h=HALVES, t=PACK)
         totals = [keep.tile([P, GROUP], F32, name=f"totals{i}") for i in range(TILES // GROUP)]
         state = {}
@@ -222,7 +242,7 @@ def tile_attend_gsma_q_pl_kernel(
                     out=bank[:], lhsT=codes[:, cols].bitcast(E4M3), lhsT_scale=scales[:, cols],
                     rhs=moving[0][:].bitcast(fmt), rhs_scale=moving[1][:], start=True, stop=True,
                 )
-                block = keep.tile([P, PACK, P], F32, name=f"{name}_block{j}")
+                block = keep.tile([P, PACK, P], F32, name=f"{name}_block{j}", tag=f"{name}_block{j}")
                 nc.scalar.activation(
                     block[:], bank[:].rearrange("s (m t) -> s t m", t=PACK), ACT.Copy, scale=token_scale[:, j : j + 1]
                 )
@@ -260,6 +280,21 @@ def tile_attend_gsma_q_pl_kernel(
             )
             state[("x", n)] = x
 
+        def softmax_turned(n):
+            h, t = divmod(n, PACK)
+            turned = turn(state[("a", h)], t, "dp", ROW_BANKS)
+            neg_z = work.tile([P, PACK, P], F32, name="z")
+            neg_max = work.tile([P, 1], F32, name="neg_max")
+            nc.vector.tensor_scalar(
+                neg_z[:], turned, neg_us[:, h, t : t + 1], None, ALU.mult, ALU.min, accum_out=neg_max[:]
+            )
+            x = work.tile([P, SLOTS], F32, name="x", bufs=TILES)
+            nc.scalar.activation(
+                x[:], neg_z[:].rearrange("r u s -> r (u s)"), ACT.Exp, bias=neg_max[:], scale=-1.0,
+                accum_out=totals[n // GROUP][:, n % GROUP : n % GROUP + 1],
+            )
+            state[("x", n)] = x
+
         def row_factors(i):
             inverse = keep.tile([P, GROUP], F32, name=f"inverse{i}")
             nc.vector.reciprocal(inverse[:], totals[i][:])
@@ -290,8 +325,23 @@ def tile_attend_gsma_q_pl_kernel(
             h, t = divmod(n, PACK)
             pdp, delta = state[("pdp", n)]
             shift = work.tile([P, SLOTS], F32, name="shift")
+            if n in FUSED:
+                factor = work.tile([P, 1], F32, name="factor")
+                nc.scalar.activation(factor[:], delta[:], ACT.Copy, scale=state[("rows", n)][1])
+                nc.vector.scalar_tensor_tensor(
+                    shift[:], state[("x", n)][:], factor[:], pdp[:].rearrange("r u s -> r (u s)"), ALU.mult, ALU.add
+                )
+                bank = psum.tile([P, PACK, P], F32, name="grad_bank", tag="grad", bufs=GRAD_BANKS)
+                for u in range(PACK):
+                    nc.tensor.transpose(bank[:, u, :], shift[:, u * P : (u + 1) * P], ident[:])
+                state[("grad", n)] = bank
+                return
             if n in SHIFT_ON_VECTOR:
                 nc.vector.tensor_scalar(
+                    shift[:], state[("x", n)][:], delta[:], state[("rows", n)][1], ALU.mult, ALU.mult
+                )
+            elif n in SHIFT_ON_POOL:
+                nc.gpsimd.tensor_scalar(
                     shift[:], state[("x", n)][:], delta[:], state[("rows", n)][1], ALU.mult, ALU.mult
                 )
             else:
@@ -322,10 +372,11 @@ def tile_attend_gsma_q_pl_kernel(
                 out=g_codes[:].bitcast(E5M2), scales=g_scales[:], in_=state[("g", n)][:].rearrange("s r u -> s (r u)")
             )
             bank = psum.tile([P, FEATURES], F32, name="out_bank", tag="mx", bufs=MX_BANKS)
-            nc.tensor.matmul_mx(
-                out=bank[:], lhsT=g_codes[:].bitcast(E5M2), lhsT_scale=g_scales[:],
-                rhs=state["kt"][0][:].bitcast(E4M3), rhs_scale=state["kt"][1][:], start=True, stop=True,
-            )
+            for again in range(2 if n in REPEAT else 1):
+                nc.tensor.matmul_mx(
+                    out=bank[:], lhsT=g_codes[:].bitcast(E5M2), lhsT_scale=g_scales[:],
+                    rhs=state["kt"][0][:].bitcast(E4M3), rhs_scale=state["kt"][1][:], start=True, stop=True,
+                )
             nc.scalar.copy(result[h][:, t, :], bank[:])
             nc.sync.dma_start(out_rows[h, t], result[h][:, t, :])
 
@@ -342,38 +393,47 @@ def tile_attend_gsma_q_pl_kernel(
         def live(n):
             return 0 <= n < TILES
 
-        v_codes = keep.tile([P, SLOTS], U32, name="v_codes", align_bytes=64)
-        nc.vector.tensor_copy(v_codes[:], vw_win[:].bitcast(U32).indirect(offsets[:]))
-        do_mx = quantise("do0", weave(do_raw[0], "do0", DO0_SPLIT), E5M2)
-        state[("b", 0)] = slot_major("b0", v_codes, v_scales, do_mx, E5M2, tv_block)
-
         def forward(n):
-            scores(n)
-            softmax(n)
+            if n // PACK in B_HALVES:
+                softmax_turned(n)
+            else:
+                scores(n)
+                softmax(n)
             if n % GROUP == GROUP - 1:
                 row_factors(n // GROUP)
 
-        for n in range(PACK):
-            forward(n)
+        if 0 in B_HALVES:
+            state[("a", 0)] = slot_major("a0", k_codes, k_scales, q_mx[0], E4M3, ts_block)
+        do_mx = [quantise("do0", weave(do_raw[0], "do0", DO0_SPLIT), E5M2)]
+        v_codes = keep.tile([P, SLOTS], U32, name="v_codes", align_bytes=64)
+        nc.vector.tensor_copy(v_codes[:], vw_win[:].bitcast(U32).indirect(offsets[:]))
+        state[("b", 0)] = slot_major("b0", v_codes, v_scales, do_mx[0], E5M2, tv_block)
+        for n in range(TILES):
             if n == Q1_AT:
-                q_mx.append(quantise("q1", weave_dealt(q_second, "q1", Q1_SPLIT), E4M3))
-        done = PACK
+                if 1 in B_HALVES:
+                    q_mx.append(quantise("q1", weave(q_second, "q1", Q1_SPLIT), E4M3))
+                    state[("a", 1)] = slot_major("a1", k_codes, k_scales, q_mx[1], E4M3, ts_block)
+                else:
+                    q_mx.append(quantise("q1", weave_dealt(q_second, "q1", Q1_SPLIT), E4M3))
+            if n == DO1_AT and LATE_B1 < 0:
+                do_mx.append(quantise("do1", weave(do_raw[1], "do1", DO1_SPLIT), E5M2))
+            if n == B1_AT and LATE_B1 < 0:
+                state[("b", 1)] = slot_major("b1", v_codes, v_scales, do_mx[1], E5M2, tv_block)
+            if n < FIRST:
+                forward(n)
+        state["kt"] = quantise("kt", kt_woven[:].rearrange("s p t u -> s (p t u)").bitcast(BF16), E4M3, KT_TAG)
         for step in range(TILES + LAG):
-            if step == KT_AT:
-                state["kt"] = quantise("kt", kt_woven[:].rearrange("s p t u -> s (p t u)").bitcast(BF16), E4M3, KT_TAG)
-            if step == DO1_STEP:
-                do_mx = quantise("do1", weave(do_raw[1], "do1", DO1_SPLIT), E5M2)
-                state[("b", 1)] = slot_major("b1", v_codes, v_scales, do_mx, E5M2, tv_block)
+            if step == LATE_B1:
+                do_mx.append(quantise("do1", weave(do_raw[1], "do1", DO1_SPLIT), E5M2))
+                state[("b", 1)] = slot_major("b1", v_codes, v_scales, do_mx[1], E5M2, tv_block)
             if live(step):
                 weighted(step)
                 centre(step)
             if live(step - LAG):
                 scale_gradient(step - LAG)
                 query_gradient(step - LAG)
-            if step >= SC1_AT:
-                for n in range(done, min(TILES, done + SC_RATE)):
-                    forward(n)
-                done = min(TILES, done + SC_RATE)
-            if step == PACK - 1 + LAG + OUT0_LAG:
-                planes(0, weave(result[0], "result0", OUT0_SPLIT))
+            if live(FIRST + step):
+                forward(FIRST + step)
+            if step == min(PACK - 1 + LAG + OUT0_LAG, TILES + LAG - 1):
+                planes(0, weave(result[0], "result0", OUT0_SPLIT, 128))
         planes(1, weave(result[1], "result1", OUT1_SPLIT))

@@ -30,38 +30,24 @@ FLOPS = 3 * 2 * QUERIES * SLOTS * FEATURES
 MX_BANKS = 2
 ROW_BANKS = 4
 GRAD_BANKS = 2
-K_SPLIT = 512
-Q0_SPLIT = 128
-DO0_SPLIT = 128
+SCORE_TAG = "dp"
+PAIRED = ()
+SHIFT_ON_VECTOR = (4, 5, 6, 7)
+REPEAT = ()
+GROUP = 2
+PIECE = 128
+Q0_ON_VECTOR = 0
+Q0_PIECES = 4
+DO0_SPLIT = 0
 Q1_SPLIT = 512
 DO1_SPLIT = 0
 OUT0_SPLIT = 256
 OUT1_SPLIT = 320
-VS_TAG = "q0_woven"
-ORDER = "dvqe"
-V_AT = 0
-PIECE = 128
-AHEAD = 2
-Q1_AT = 3
-KT_AT = 0
-SC1_AT = 0
-SC_RATE = 1
-B_HALVES = ()
-SHIFT_ON_POOL = ()
-FIRST = 4
-DO1_AT = 4
-B1_AT = 4
-REPEAT = (1,2,3,4,5,6)
-FUSED = ()
-LATE_B1 = 0
-GROUP = 2
-Q0_PIECES = 1
-GATE_ON_SCALAR = 0
-KT_TAG = ""
+XT_BUFS = 4
 LAG = 2
-DO1_STEP = 0
-OUT0_LAG = 4
-SHIFT_ON_VECTOR = (4,5,6,7)
+G_LAG = 1
+DO1_AT = 1
+Z_BUFS = 2
 
 
 def tile_attend_gsma_q_pl_kernel(
@@ -73,73 +59,69 @@ def tile_attend_gsma_q_pl_kernel(
         work = ctx.enter_context(tc.tile_pool(name="work", bufs=3))
         psum = ctx.enter_context(tc.psum_pool(name="psum", bufs=2))
 
+        k_planes = kT.rearrange("(p t) c -> t p c", t=PACK)
+        k_win = [keep.tile([P, TOKENS], F32, name=f"k_win{t}", align_bytes=64) for t in range(PACK)]
         offsets = keep.tile([P, SLOTS // 16], U16, name="offsets")
-        nc.sync.dma_start(offsets[:], offs)
-        ts_row = keep.tile([1, TOKENS], F32, name="ts_row", tag="k_win_r0")
-        tv_row = keep.tile([1, TOKENS], F32, name="tv_row")
+        ts_row = keep.tile([1, TOKENS], F32, name="ts_row", align_bytes=64)
+        tv_row = keep.tile([1, TOKENS], F32, name="tv_row", tag="row1")
         us_sb = keep.tile([P, HALVES, PACK], F32, name="us_sb")
         wt_sb = keep.tile([P, HALVES, PACK], F32, name="wt_sb")
+        ts_win = keep.tile([P, TOKENS], F32, name="ts_win")
+        nc.gpsimd.memset(ts_win[:], 0.0)
+        vs_win = keep.tile([P, TOKENS], U8, name="vs_win")
+        warm = keep.tile([P, 1], F32, name="warm")
+        seed = keep.tile([P, 1], F32, name="seed")
+        nc.vector.memset(seed[:], 0.0)
+        nc.vector.memset(vs_win[:].bitcast(I32), 0)
         nc.sync.dma_start(ts_row[:], ts[0:1, :])
-        nc.sync.dma_start(tv_row[:], tv[0:1, :])
-        k_planes = kT.rearrange("(p t) c -> t p c", t=PACK)
-        k_win = [keep.tile([P, TOKENS], F32, name=f"k_win{t}") for t in range(PACK)]
         nc.sync.dma_start(k_win[0][:], k_planes[0])
+        nc.sync.dma_start(offsets[:], offs)
+        nc.scalar.dma_start(tv_row[:], tv[0:1, :])
+        nc.scalar.activation(warm[:], seed[:], ACT.Exp)
         nc.sync.dma_start(us_sb[:], us.rearrange("(h p t) o -> p h (t o)", h=HALVES, t=PACK))
         nc.sync.dma_start(wt_sb[:], wt.rearrange("(h p t) o -> p h (t o)", h=HALVES, t=PACK))
         nc.sync.dma_start(k_win[1][:], k_planes[1])
-        nc.sync.dma_start(k_win[2][:], k_planes[2])
-        vs_win = keep.tile([P, TOKENS], U8, name="vs_win")
-        nc.gpsimd.memset(vs_win[:].bitcast(I32), 0)
         for quad in range(4):
             nc.sync.dma_start(
                 vs_win[32 * quad : 32 * quad + 4, :].bitcast(I32),
                 vT_scales[0, 4 * quad : 4 * quad + 4, :].bitcast(I32),
             )
+        nc.sync.dma_start(k_win[2][:], k_planes[2])
         nc.sync.dma_start(k_win[3][:], k_planes[3])
-
         q_first = [keep.tile([P, PACK, PASS // 2], F32, name=f"q_first{i}", align_bytes=64) for i in range(2)]
-        do_raw = [keep.tile([P, PACK, PASS], F32, name=f"do_raw{h}") for h in range(HALVES)]
-        vw_win = keep.tile([P, TOKENS], I32, name="vw_win")
         q_rows = qT.rearrange("(p j) (h r) -> h p j r", j=PACK, h=HALVES)
         do_rows = doT.rearrange("(p j) (h r) -> h p j r", j=PACK, h=HALVES)
         for i in range(2):
             nc.sync.dma_start(q_first[i][:], q_rows[0][:, :, i * PASS // 2 : (i + 1) * PASS // 2])
-        q_second = keep.tile([P, PACK, PASS], F32, name="q_raw1")
-        for which in ORDER:
-            if which == "d":
-                nc.sync.dma_start(do_raw[0][:], do_rows[0])
-            if which == "v":
-                nc.sync.dma_start(vw_win[:], vT_words[0].rearrange("p c l -> p (c l)").bitcast(I32))
-            if which == "q":
-                nc.sync.dma_start(q_second[:], q_rows[1])
-            if which == "e":
-                nc.sync.dma_start(do_raw[1][:], do_rows[1])
+        do_raw = [keep.tile([P, PACK, PASS], F32, name="do_raw0"), keep.tile([P, PACK, PASS], F32, name="do_raw1", tag="row1")]
+        vw_win = keep.tile([P, TOKENS], I32, name="vw_win", align_bytes=64)
+        q_second = keep.tile([P, PACK, PASS], F32, name="q_raw1", tag="row0")
+        nc.sync.dma_start(do_raw[0][:], do_rows[0])
+        nc.sync.dma_start(vw_win[:], vT_words[0].rearrange("p c l -> p (c l)").bitcast(I32))
 
         ident = keep.tile([P, P], F32, name="ident")
         make_identity(nc, ident[:])
-        ts_win = keep.tile([P, TOKENS], F32, name="ts_win")
         tv_win = keep.tile([P, TOKENS], F32, name="tv_win")
-        nc.vector.memset(ts_win[:], 0.0)
         nc.vector.memset(tv_win[:], 0.0)
-        warm = keep.tile([P, 1], F32, name="warm")
-        nc.scalar.activation(warm[:], ident[:, 0:1], ACT.Exp)
-        nc.scalar.activation(ts_win[0:1, :], ts_row[:], ACT.Copy)
+        nc.vector.tensor_copy(ts_win[0:1, :], ts_row[:])
         nc.scalar.activation(tv_win[0:1, :], tv_row[:], ACT.Copy)
+        nc.sync.dma_start(q_second[:], q_rows[1])
+        nc.sync.dma_start(do_raw[1][:], do_rows[1])
 
-        def pick(window, name):
-            picked = keep.tile([P, SLOTS], F32, name=name + "_picked")
+        def pick(window, name, tag):
+            picked = keep.tile([P, SLOTS], F32, name=name + "_picked", tag=tag, align_bytes=64)
             nc.vector.tensor_copy(picked[:], window[:].indirect(offsets[:]))
             return picked
 
-        def columns_of(view, name, tag=""):
+        def columns_of(view, name):
             turned = psum.tile([P, PACK, P], F32, name=name + "_turned", tag="dp", bufs=ROW_BANKS)
             for t in range(PACK):
                 nc.tensor.transpose(turned[:, t, :], view[:, t, :], ident[:])
-            columns = keep.tile([P, PACK], F32, name=name + "_columns", tag=tag, align_bytes=64)
+            columns = keep.tile([P, PACK], F32, name=name + "_columns")
             nc.scalar.copy(columns[:], turned[:, :, 0])
             return columns
 
-        k_picked = keep.tile([P, PACK, SLOTS], BF16, name="k_picked", align_bytes=64)
+        k_picked = keep.tile([P, PACK, SLOTS], BF16, name="k_picked", align_bytes=64, tag="ts_row")
 
         def gather_keys(t):
             nc.vector.tensor_copy(k_picked[:, t, :], k_win[t][:].indirect(offsets[:]))
@@ -152,25 +134,27 @@ def tile_attend_gsma_q_pl_kernel(
                     nc.tensor.transpose(bank[:, e, u, :], words[:, u, :], ident[:])
             nc.scalar.copy(kt_woven[:, :, 2 * pair : 2 * pair + 2, :], bank[:].rearrange("s e u p -> s p e u"))
 
+        ts_block = columns_of(pick(ts_win, "ts", "")[:].rearrange("p (j s) -> p j s", j=PACK), "ts")
         gather_keys(0)
-        ts_block = columns_of(pick(ts_win, "ts")[:].rearrange("p (j s) -> p j s", j=PACK), "ts")
         spread = psum.tile([P, PACK, P], F32, name="ts_spread", tag="mx", bufs=MX_BANKS)
         for j in range(PACK):
             nc.tensor.transpose(spread[:, j, :], ts_block[:, j : j + 1].to_broadcast([P, P]), ident[:])
         ts_rows = keep.tile([P, PACK, P], F32, name="ts_rows")
-        nc.scalar.copy(ts_rows[:], spread[:].rearrange("r j (s u) -> r u (j s)", u=PACK))
-        neg_us = keep.tile([P, HALVES, PACK], F32, name="neg_us")
-        if B_HALVES:
-            nc.vector.tensor_scalar(neg_us[:], us_sb[:], -1.0, None, ALU.mult)
-        uswt = keep.tile([P, HALVES, PACK], F32, name="uswt")
-        nc.vector.tensor_tensor(uswt[:], us_sb[:], wt_sb[:], ALU.mult)
+        ts_nat = keep.tile([P, SLOTS], F32, name="ts_nat")
+        if len(PAIRED) > 0:
+            nc.scalar.copy(ts_nat[:], spread[:].rearrange("r j s -> r (j s)"))
+        if len(PAIRED) < TILES:
+            nc.scalar.copy(ts_rows[:], spread[:].rearrange("r j (s u) -> r u (j s)", u=PACK))
+            ts_place = columns_of(ts_rows[:], "ts_place")
         gather_keys(1)
-        tv_block = columns_of(pick(tv_win, "tv")[:].rearrange("p (j s) -> p j s", j=PACK), "tv_block")
+        tv_block = columns_of(pick(tv_win, "tv", "k_win1")[:].rearrange("p (j s) -> p j s", j=PACK), "tv_block")
+        v_scales = keep.tile([P, SLOTS], U8, name="v_scales", align_bytes=64, tag="k_win0")
+        nc.vector.tensor_copy(v_scales[:], vs_win[:].indirect(offsets[:]))
         gather_keys(2)
         gather_keys(3)
 
-        def weave(src_tile, name, split, vpiece=PASS):
-            woven = keep.tile([P, PASS, PACK], BF16, name=name + "_woven", align_bytes=64)
+        def weave(src_tile, name, split, vpiece=PASS, tag=""):
+            woven = keep.tile([P, PASS, PACK], BF16, name=name + "_woven", align_bytes=64, tag=tag)
             src = src_tile[:].rearrange("p t (c i) -> p c t i", i=4)
             dst = woven[:].rearrange("p (c i) t -> p c t i", i=4)
             for c in range(0, split, vpiece):
@@ -181,19 +165,20 @@ def tile_attend_gsma_q_pl_kernel(
                 nc.scalar.copy(dst[:, part], src[:, part])
             return woven[:].rearrange("p c t -> p (c t)")
 
-        def weave_dealt(raw, name, split):
-            woven = keep.tile([P, PACK, P, PACK], BF16, name=name + "_woven", align_bytes=64)
+        def weave_dealt(raw, name, split, tag):
+            woven = keep.tile([P, PASS * PACK], BF16, name=name + "_woven", align_bytes=64, tag=tag)
+            woven = woven[:]
             src = raw[:].rearrange("p j (m t) -> p m j t", t=PACK)
-            dst = woven[:].rearrange("p t m j -> p m j t")
+            dst = woven.rearrange("p (t m j) -> p m j t", t=PACK, j=PACK)
             if split > 0:
                 nc.vector.tensor_copy(dst[:, : split // 4], src[:, : split // 4])
             for c in range(split, PASS, PIECE):
                 part = slice(c // 4, min(c + PIECE, PASS) // 4)
                 nc.scalar.copy(dst[:, part], src[:, part])
-            return woven[:].rearrange("p t m j -> p (t m j)")
+            return woven
 
-        def quantise(name, source, fmt, tag="", pieces=1):
-            codes = keep.tile([P, PASS], U32, name=name + "_codes", align_bytes=64, tag=tag)
+        def quantise(name, source, fmt, pieces=1):
+            codes = keep.tile([P, PASS], U32, name=name + "_codes", align_bytes=64)
             scales = keep.tile([P, PASS], U8, name=name + "_scales", align_bytes=64)
             width = PASS // pieces
             for i in range(pieces):
@@ -204,164 +189,152 @@ def tile_attend_gsma_q_pl_kernel(
                 )
             return codes, scales
 
-        k_woven = weave(k_picked, "k", K_SPLIT)
+        k_woven = weave(k_picked, "k", PASS, PASS // 2)
         q_dealt = keep.tile([P, PACK, P, PACK], BF16, name="q0_woven", align_bytes=64)
-        for i in range(2):
-            if 0 in B_HALVES:
-                nc.scalar.copy(
-                    q_dealt[:].rearrange("p a b t -> p (a b) t").rearrange("p (c i) t -> p c t i", i=4)[:, i * P // 2 : (i + 1) * P // 2],
-                    q_first[i][:].rearrange("p t (c i) -> p c t i", i=4),
-                )
-            else:
-                nc.scalar.copy(
-                    q_dealt[:].rearrange("p t m j -> p m j t")[:, i * P // 2 : (i + 1) * P // 2],
-                    q_first[i][:].rearrange("p j (m t) -> p m j t", t=PACK),
-                )
-        q_woven = q_dealt[:].rearrange("p t m j -> p (t m j)")
-        k_codes, k_scales = quantise("k", k_woven, E4M3)
-        q_mx = [quantise("q0", q_woven, E4M3, pieces=Q0_PIECES)]
+        dealt = q_dealt[:].rearrange("p t m j -> p m j t")
+        nc.scalar.copy(dealt[:, : P // 2], q_first[0][:].rearrange("p j (m t) -> p m j t", t=PACK))
+        late = q_first[1][:].rearrange("p j (m t) -> p m j t", t=PACK)
+        cut = (PASS // 2 - Q0_ON_VECTOR) // PACK
+        nc.scalar.copy(dealt[:, P // 2 : P // 2 + cut], late[:, :cut])
+        k_codes, k_scales = quantise("k", k_woven, E4M3, pieces=2)
+        if Q0_ON_VECTOR > 0:
+            nc.vector.tensor_copy(dealt[:, P // 2 + cut :], late[:, cut:])
+        q_mx = [quantise("q0", q_dealt[:].rearrange("p t m j -> p (t m j)"), E4M3, pieces=Q0_PIECES)]
+        uswt = keep.tile([P, 2, TILES], F32, name="uswt", tag="vs_win")
+        nc.vector.tensor_tensor(
+            uswt[:, 0], us_sb[:].rearrange("p h t -> p (h t)"), wt_sb[:].rearrange("p h t -> p (h t)"), ALU.mult
+        )
+        nc.vector.memset(uswt[:, 1], -1.0)
         kt_woven = keep.tile([P, P, PACK, 2], F32, name="kt_woven", align_bytes=64, tag="q_first1")
         turn_keys(0)
         turn_keys(1)
-        ts_place = columns_of(ts_rows[:], "ts_place", "q_first0")
-        v_scales = keep.tile([P, SLOTS], U8, name="v_scales", align_bytes=64, tag=VS_TAG)
-        nc.vector.tensor_copy(v_scales[:], vs_win[:].indirect(offsets[:]))
 
-
-        result = [keep.tile([P, PACK, FEATURES], F32, name=f"result{h}", tag=f"k_win{h}") for h in range(HALVES)]
+        result = [keep.tile([P, PACK, FEATURES], F32, name=f"result{h}", tag=f"k_win{h + 2}", align_bytes=64) for h in range(HALVES)]
         out_rows = out_0.rearrange("(h p t) d -> h t p d", h=HALVES, t=PACK)
         totals = [keep.tile([P, GROUP], F32, name=f"totals{i}") for i in range(TILES // GROUP)]
         state = {}
 
-        def slot_major(name, codes, scales, moving, fmt, token_scale):
-            scaled = []
+        def values_product(h, moving, tag):
+            blocks = keep.tile([P, PACK, PACK, P], F32, name=f"d_blocks{h}", tag=tag)
             for j in range(PACK):
                 cols = slice(j * P, (j + 1) * P)
-                bank = psum.tile([P, PASS], F32, name=name + "_bank", tag="mx", bufs=MX_BANKS)
+                bank = psum.tile([P, PASS], F32, name="b_bank", tag="mx", bufs=MX_BANKS)
                 nc.tensor.matmul_mx(
-                    out=bank[:], lhsT=codes[:, cols].bitcast(E4M3), lhsT_scale=scales[:, cols],
-                    rhs=moving[0][:].bitcast(fmt), rhs_scale=moving[1][:], start=True, stop=True,
+                    out=bank[:], lhsT=v_codes[:, cols].bitcast(E4M3), lhsT_scale=v_scales[:, cols],
+                    rhs=moving[0][:].bitcast(E5M2), rhs_scale=moving[1][:], start=True, stop=True,
                 )
-                block = keep.tile([P, PACK, P], F32, name=f"{name}_block{j}", tag=f"{name}_block{j}")
                 nc.scalar.activation(
-                    block[:], bank[:].rearrange("s (m t) -> s t m", t=PACK), ACT.Copy, scale=token_scale[:, j : j + 1]
+                    blocks[:, j], bank[:].rearrange("s (m t) -> s t m", t=PACK), ACT.Copy, scale=tv_block[:, j : j + 1]
                 )
-                scaled.append(block)
-            return scaled
+            state[("b", h)] = blocks
 
-        def turn(blocks, t, tag, bufs):
-            bank = psum.tile([P, PACK, P], F32, name=tag + "_bank", tag=tag, bufs=bufs)
-            for j in range(PACK):
-                nc.tensor.transpose(bank[:, j, :], blocks[j][:, t, :], ident[:])
-            return bank[:].rearrange("r j (s u) -> r u (j s)", u=PACK)
+        def by_place(view, n):
+            if n in PAIRED:
+                return view
+            return view.rearrange("r (s u) -> r u s", u=PACK)
+
+        def as_laid(tile, n):
+            if n in PAIRED:
+                return tile[:]
+            return tile[:].rearrange("r (u s) -> r u s", u=PACK)
 
         def scores(n):
             h, t = divmod(n, PACK)
             cols = slice(t * P, (t + 1) * P)
-            bank = psum.tile([P, SLOTS], F32, name="score_bank", tag="dp", bufs=ROW_BANKS)
+            bank = psum.tile([P, SLOTS], F32, name="score_bank", tag=SCORE_TAG, bufs=ROW_BANKS if SCORE_TAG == "dp" else MX_BANKS)
             nc.tensor.matmul_mx(
                 out=bank[:], lhsT=q_mx[h][0][:, cols].bitcast(E4M3), lhsT_scale=q_mx[h][1][:, cols],
                 rhs=k_codes[:].bitcast(E4M3), rhs_scale=k_scales[:], start=True, stop=True,
             )
-            z = work.tile([P, PACK, P], F32, name="z")
+            z = work.tile([P, SLOTS], F32, name="z", bufs=Z_BUFS)
             nc.vector.scalar_tensor_tensor(
-                z[:], bank[:].rearrange("r (s u) -> r u s", u=PACK), us_sb[:, h, t : t + 1], ts_rows[:],
+                as_laid(z, n), by_place(bank[:], n), us_sb[:, h, t : t + 1], ts_nat[:] if n in PAIRED else ts_rows[:],
                 ALU.mult, ALU.mult,
             )
             state[("z", n)] = z
 
         def softmax(n):
-            z = state[("z", n)][:].rearrange("r u s -> r (u s)")
+            z = state[("z", n)][:]
             neg_max = work.tile([P, 1], F32, name="neg_max")
             nc.vector.tensor_reduce(neg_max[:], z, AXIS.X, ALU.max, negate=True)
-            x = work.tile([P, SLOTS], F32, name="x", bufs=TILES)
+            if n == 0:
+                state["x0"] = keep.tile([P, PACK, SLOTS], F32, name="x_first", tag="do_raw0")
+            x = state["x0"][:, n] if n < PACK else work.tile([P, SLOTS], F32, name="x", bufs=PACK)
             nc.scalar.activation(
                 x[:], z, ACT.Exp, bias=neg_max[:], accum_out=totals[n // GROUP][:, n % GROUP : n % GROUP + 1]
             )
             state[("x", n)] = x
-
-        def softmax_turned(n):
-            h, t = divmod(n, PACK)
-            turned = turn(state[("a", h)], t, "dp", ROW_BANKS)
-            neg_z = work.tile([P, PACK, P], F32, name="z")
-            neg_max = work.tile([P, 1], F32, name="neg_max")
-            nc.vector.tensor_scalar(
-                neg_z[:], turned, neg_us[:, h, t : t + 1], None, ALU.mult, ALU.min, accum_out=neg_max[:]
-            )
-            x = work.tile([P, SLOTS], F32, name="x", bufs=TILES)
-            nc.scalar.activation(
-                x[:], neg_z[:].rearrange("r u s -> r (u s)"), ACT.Exp, bias=neg_max[:], scale=-1.0,
-                accum_out=totals[n // GROUP][:, n % GROUP : n % GROUP + 1],
-            )
-            state[("x", n)] = x
+            if n % GROUP == GROUP - 1:
+                row_factors(n // GROUP)
 
         def row_factors(i):
             inverse = keep.tile([P, GROUP], F32, name=f"inverse{i}")
             nc.vector.reciprocal(inverse[:], totals[i][:])
-            gate = keep.tile([P, GROUP], F32, name=f"gate{i}")
-            rows = uswt[:].rearrange("p h t -> p (h t)")[:, i * GROUP : (i + 1) * GROUP]
-            if GROUP == 1 and GATE_ON_SCALAR:
-                nc.scalar.activation(gate[:], inverse[:], ACT.Copy, scale=rows)
-            else:
-                nc.vector.tensor_tensor(gate[:], inverse[:], rows, ALU.mult)
-            neg_inverse = keep.tile([P, GROUP], F32, name=f"neg_inverse{i}")
-            nc.scalar.activation(neg_inverse[:], inverse[:], ACT.Copy, scale=-1.0)
+            gate = keep.tile([P, 2, GROUP], F32, name=f"gate{i}")
+            nc.vector.tensor_tensor(
+                gate[:], inverse[:].unsqueeze(1).to_broadcast([P, 2, GROUP]),
+                uswt[:, :, i * GROUP : (i + 1) * GROUP], ALU.mult,
+            )
             for e in range(GROUP):
-                state[("rows", i * GROUP + e)] = (gate[:, e : e + 1], neg_inverse[:, e : e + 1])
+                state[("rows", i * GROUP + e)] = (
+                    gate[:, 0, e : e + 1], (inverse[:] if i * GROUP + e in PAIRED else gate[:, 1])[:, e : e + 1]
+                )
 
-        def weighted(n):
+        def weights(n):
+            if n not in PAIRED:
+                return
+            xt = work.tile([P, SLOTS], F32, name="xt", bufs=XT_BUFS)
+            nc.vector.scalar_tensor_tensor(xt[:], state[("x", n)][:], state[("rows", n)][0], ts_nat[:], ALU.mult, ALU.mult)
+            state[("xt", n)] = xt
+
+        def row_sum(n):
             h, t = divmod(n, PACK)
-            dp = turn(state[("b", h)], t, "dp", ROW_BANKS)
-            pdp = work.tile([P, PACK, P], F32, name="pdp")
+            bank = psum.tile([P, PACK, P], F32, name="dp_bank", tag="dp", bufs=ROW_BANKS)
+            for j in range(PACK):
+                nc.tensor.transpose(bank[:, j, :], state[("b", h)][:, j, t, :], ident[:])
+            dp = bank[:].rearrange("r j s -> r (j s)")
+            pdp = work.tile([P, SLOTS], F32, name="pdp")
             delta = work.tile([P, 1], F32, name="delta")
             nc.vector.scalar_tensor_tensor(
-                pdp[:], dp, state[("rows", n)][0],
-                state[("x", n)][:].rearrange("r (u s) -> r u s", u=PACK),
-                ALU.mult, ALU.mult, accum_out=delta[:],
+                as_laid(pdp, n), by_place(dp, n), state[("rows", n)][1 if n in PAIRED else 0],
+                as_laid(state[("x", n)], n), ALU.mult, ALU.mult, accum_out=delta[:],
             )
-            state[("pdp", n)] = (pdp, delta)
-
-        def centre(n):
-            h, t = divmod(n, PACK)
-            pdp, delta = state[("pdp", n)]
-            shift = work.tile([P, SLOTS], F32, name="shift")
-            if n in FUSED:
-                factor = work.tile([P, 1], F32, name="factor")
-                nc.scalar.activation(factor[:], delta[:], ACT.Copy, scale=state[("rows", n)][1])
-                nc.vector.scalar_tensor_tensor(
-                    shift[:], state[("x", n)][:], factor[:], pdp[:].rearrange("r u s -> r (u s)"), ALU.mult, ALU.add
-                )
-                bank = psum.tile([P, PACK, P], F32, name="grad_bank", tag="grad", bufs=GRAD_BANKS)
-                for u in range(PACK):
-                    nc.tensor.transpose(bank[:, u, :], shift[:, u * P : (u + 1) * P], ident[:])
-                state[("grad", n)] = bank
+            state[("pdp", n)] = (dp, pdp, delta)
+            if n in PAIRED:
                 return
+            shift = work.tile([P, SLOTS], F32, name="shift")
             if n in SHIFT_ON_VECTOR:
-                nc.vector.tensor_scalar(
-                    shift[:], state[("x", n)][:], delta[:], state[("rows", n)][1], ALU.mult, ALU.mult
-                )
-            elif n in SHIFT_ON_POOL:
-                nc.gpsimd.tensor_scalar(
-                    shift[:], state[("x", n)][:], delta[:], state[("rows", n)][1], ALU.mult, ALU.mult
-                )
+                nc.vector.tensor_scalar(shift[:], state[("x", n)][:], delta[:], state[("rows", n)][1], ALU.mult, ALU.mult)
             else:
                 factor = work.tile([P, 1], F32, name="factor")
                 nc.scalar.activation(factor[:], delta[:], ACT.Copy, scale=state[("rows", n)][1])
                 nc.scalar.activation(shift[:], state[("x", n)][:], ACT.Copy, scale=factor[:])
-            bank = psum.tile([P, PACK, P], F32, name="grad_bank", tag="grad", bufs=GRAD_BANKS)
+            grad = psum.tile([P, PACK, P], F32, name="grad_bank", tag="grad", bufs=GRAD_BANKS)
             for u in range(PACK):
-                nc.tensor.matmul(bank[:, u, :], pdp[:, u, :], ident[:], start=True, stop=False, is_transpose=True)
-                nc.tensor.matmul(
-                    bank[:, u, :], shift[:, u * P : (u + 1) * P], ident[:], start=False, stop=True, is_transpose=True
-                )
-            state[("grad", n)] = bank
+                cols = slice(u * P, (u + 1) * P)
+                nc.tensor.matmul(grad[:, u, :], pdp[:, cols], ident[:], start=True, stop=False, is_transpose=True)
+                nc.tensor.matmul(grad[:, u, :], shift[:, cols], ident[:], start=False, stop=True, is_transpose=True)
+            state[("grad", n)] = grad
 
-        def scale_gradient(n):
+        def gradient(n):
             g = work.tile([P, P, PACK], BF16, name="g", align_bytes=64)
-            nc.vector.tensor_tensor(
-                g[:], state[("grad", n)][:].rearrange("s u r -> s r u"),
-                ts_place[:].unsqueeze(1).to_broadcast([P, P, PACK]), ALU.mult,
-            )
+            if n in PAIRED:
+                dp, pdp, delta = state[("pdp", n)]
+                rows = work.tile([P, SLOTS], BF16, name="g_rows", align_bytes=64)
+                nc.vector.scalar_tensor_tensor(rows[:], dp, delta[:], state[("xt", n)][:], ALU.subtract, ALU.mult)
+                bank = psum.tile([P, 2, P], F32, name="pair_bank", tag="grad", bufs=GRAD_BANKS)
+                words = rows[:].bitcast(F32).rearrange("r (s u) -> r u s", u=2)
+                for u in range(2):
+                    nc.tensor.transpose(bank[:, u, :], words[:, u, :], ident[:])
+                nc.scalar.copy(
+                    g[:].rearrange("s r u -> s (r u)").bitcast(F32).rearrange("s (r u) -> s r u", u=2),
+                    bank[:].rearrange("s u r -> s r u"),
+                )
+            else:
+                nc.vector.tensor_tensor(
+                    g[:], state[("grad", n)][:].rearrange("s u r -> s r u"),
+                    ts_place[:].unsqueeze(1).to_broadcast([P, P, PACK]), ALU.mult,
+                )
             state[("g", n)] = g
 
         def query_gradient(n):
@@ -393,47 +366,40 @@ def tile_attend_gsma_q_pl_kernel(
         def live(n):
             return 0 <= n < TILES
 
-        def forward(n):
-            if n // PACK in B_HALVES:
-                softmax_turned(n)
-            else:
-                scores(n)
-                softmax(n)
-            if n % GROUP == GROUP - 1:
-                row_factors(n // GROUP)
-
-        if 0 in B_HALVES:
-            state[("a", 0)] = slot_major("a0", k_codes, k_scales, q_mx[0], E4M3, ts_block)
-        do_mx = [quantise("do0", weave(do_raw[0], "do0", DO0_SPLIT), E5M2)]
+        do_woven = weave(do_raw[0], "do0", DO0_SPLIT)
+        scores(0)
+        scores(1)
+        softmax(0)
+        softmax(1)
         v_codes = keep.tile([P, SLOTS], U32, name="v_codes", align_bytes=64)
         nc.vector.tensor_copy(v_codes[:], vw_win[:].bitcast(U32).indirect(offsets[:]))
-        state[("b", 0)] = slot_major("b0", v_codes, v_scales, do_mx[0], E5M2, tv_block)
-        for n in range(TILES):
-            if n == Q1_AT:
-                if 1 in B_HALVES:
-                    q_mx.append(quantise("q1", weave(q_second, "q1", Q1_SPLIT), E4M3))
-                    state[("a", 1)] = slot_major("a1", k_codes, k_scales, q_mx[1], E4M3, ts_block)
-                else:
-                    q_mx.append(quantise("q1", weave_dealt(q_second, "q1", Q1_SPLIT), E4M3))
-            if n == DO1_AT and LATE_B1 < 0:
-                do_mx.append(quantise("do1", weave(do_raw[1], "do1", DO1_SPLIT), E5M2))
-            if n == B1_AT and LATE_B1 < 0:
-                state[("b", 1)] = slot_major("b1", v_codes, v_scales, do_mx[1], E5M2, tv_block)
-            if n < FIRST:
-                forward(n)
-        state["kt"] = quantise("kt", kt_woven[:].rearrange("s p t u -> s (p t u)").bitcast(BF16), E4M3, KT_TAG)
-        for step in range(TILES + LAG):
-            if step == LATE_B1:
-                do_mx.append(quantise("do1", weave(do_raw[1], "do1", DO1_SPLIT), E5M2))
-                state[("b", 1)] = slot_major("b1", v_codes, v_scales, do_mx[1], E5M2, tv_block)
-            if live(step):
-                weighted(step)
-                centre(step)
-            if live(step - LAG):
-                scale_gradient(step - LAG)
-                query_gradient(step - LAG)
-            if live(FIRST + step):
-                forward(FIRST + step)
-            if step == min(PACK - 1 + LAG + OUT0_LAG, TILES + LAG - 1):
-                planes(0, weave(result[0], "result0", OUT0_SPLIT, 128))
-        planes(1, weave(result[1], "result1", OUT1_SPLIT))
+        values_product(0, quantise("do0", do_woven, E5M2), "ts_win")
+        scores(2)
+        scores(3)
+        softmax(2)
+        softmax(3)
+        state["kt"] = quantise("kt", kt_woven[:].rearrange("s p t u -> s (p t u)").bitcast(BF16), E4M3)
+        q_mx.append(quantise("q1", weave_dealt(q_second, "q1", Q1_SPLIT, ""), E4M3))
+        row_sum(0)
+        for step in range(TILES + 2):
+            if step == 0:
+                do_woven = weave(do_raw[1], "do1", DO1_SPLIT)
+            if live(step + 1):
+                row_sum(step + 1)
+            if live(step + PACK):
+                scores(step + PACK)
+            if step in PAIRED:
+                weights(step)
+            if live(step - 1) and step - 1 not in PAIRED:
+                gradient(step - 1)
+            if live(step + PACK):
+                softmax(step + PACK)
+            if step in PAIRED:
+                gradient(step)
+            for n in range(TILES):
+                if step == n + (1 if n in PAIRED else 2):
+                    query_gradient(n)
+            if step == DO1_AT:
+                values_product(1, quantise("do1", do_woven, E5M2), "tv_win")
+        planes(0, weave(result[0], "result0", OUT0_SPLIT, 128, tag="q0_woven"))
+        planes(1, weave(result[1], "result1", OUT1_SPLIT, tag="q_first0"))

@@ -67,11 +67,11 @@ def tile_attend_gsma_q_pl_kernel(
         us_sb = keep.tile([P, HALVES, PACK], F32, name="us_sb")
         wt_sb = keep.tile([P, HALVES, PACK], F32, name="wt_sb")
         ts_win = keep.tile([P, TOKENS], F32, name="ts_win")
-        nc.gpsimd.memset(ts_win[:], 0.0)
         vs_win = keep.tile([P, TOKENS], U8, name="vs_win")
         warm = keep.tile([P, 1], F32, name="warm")
         seed = keep.tile([P, 1], F32, name="seed")
         nc.vector.memset(seed[:], 0.0)
+        nc.vector.memset(ts_win[:].bitcast(I32), 0)
         nc.vector.memset(vs_win[:].bitcast(I32), 0)
         nc.sync.dma_start(ts_row[:], ts[0:1, :])
         nc.sync.dma_start(k_win[0][:], k_planes[0])
@@ -102,8 +102,8 @@ def tile_attend_gsma_q_pl_kernel(
         ident = keep.tile([P, P], F32, name="ident")
         make_identity(nc, ident[:])
         tv_win = keep.tile([P, TOKENS], F32, name="tv_win")
-        nc.vector.memset(tv_win[:], 0.0)
-        nc.vector.tensor_copy(ts_win[0:1, :], ts_row[:])
+        nc.vector.memset(tv_win[:].bitcast(I32), 0)
+        nc.scalar.activation(ts_win[0:1, :], ts_row[:], ACT.Copy)
         nc.scalar.activation(tv_win[0:1, :], tv_row[:], ACT.Copy)
         nc.sync.dma_start(q_second[:], q_rows[1])
         nc.sync.dma_start(do_raw[1][:], do_rows[1])
@@ -121,7 +121,7 @@ def tile_attend_gsma_q_pl_kernel(
             nc.scalar.copy(columns[:], turned[:, :, 0])
             return columns
 
-        k_picked = keep.tile([P, PACK, SLOTS], BF16, name="k_picked", align_bytes=64, tag="ts_row")
+        k_picked = keep.tile([P, PACK, SLOTS], BF16, name="k_picked", align_bytes=64)
 
         def gather_keys(t):
             nc.vector.tensor_copy(k_picked[:, t, :], k_win[t][:].indirect(offsets[:]))
@@ -134,8 +134,8 @@ def tile_attend_gsma_q_pl_kernel(
                     nc.tensor.transpose(bank[:, e, u, :], words[:, u, :], ident[:])
             nc.scalar.copy(kt_woven[:, :, 2 * pair : 2 * pair + 2, :], bank[:].rearrange("s e u p -> s p e u"))
 
-        ts_block = columns_of(pick(ts_win, "ts", "")[:].rearrange("p (j s) -> p j s", j=PACK), "ts")
         gather_keys(0)
+        ts_block = columns_of(pick(ts_win, "ts", "")[:].rearrange("p (j s) -> p j s", j=PACK), "ts")
         spread = psum.tile([P, PACK, P], F32, name="ts_spread", tag="mx", bufs=MX_BANKS)
         for j in range(PACK):
             nc.tensor.transpose(spread[:, j, :], ts_block[:, j : j + 1].to_broadcast([P, P]), ident[:])

@@ -32,22 +32,24 @@ ROW_BANKS = 4
 GRAD_BANKS = 2
 SCORE_TAG = "dp"
 PAIRED = ()
-SHIFT_ON_VECTOR = (4, 5, 6, 7)
+SHIFT_ON_VECTOR = (0, 1, 2, 3, 4, 5, 6, 7)
 REPEAT = ()
 GROUP = 2
 PIECE = 128
 Q0_ON_VECTOR = 0
 Q0_PIECES = 4
 DO0_SPLIT = 0
-Q1_SPLIT = 512
+Q1_SPLIT = 0
 DO1_SPLIT = 0
 OUT0_SPLIT = 256
-OUT1_SPLIT = 320
+OUT1_SPLIT = 384
 XT_BUFS = 4
 LAG = 2
 G_LAG = 1
-DO1_AT = 1
+DO1_AT = 0
 Z_BUFS = 2
+EARLY = 0
+AHEAD = 1
 
 
 def tile_attend_gsma_q_pl_kernel(
@@ -68,16 +70,12 @@ def tile_attend_gsma_q_pl_kernel(
         wt_sb = keep.tile([P, HALVES, PACK], F32, name="wt_sb")
         ts_win = keep.tile([P, TOKENS], F32, name="ts_win")
         vs_win = keep.tile([P, TOKENS], U8, name="vs_win")
-        warm = keep.tile([P, 1], F32, name="warm")
-        seed = keep.tile([P, 1], F32, name="seed")
-        nc.vector.memset(seed[:], 0.0)
         nc.vector.memset(ts_win[:].bitcast(I32), 0)
         nc.vector.memset(vs_win[:].bitcast(I32), 0)
         nc.sync.dma_start(ts_row[:], ts[0:1, :])
         nc.sync.dma_start(k_win[0][:], k_planes[0])
         nc.sync.dma_start(offsets[:], offs)
         nc.scalar.dma_start(tv_row[:], tv[0:1, :])
-        nc.scalar.activation(warm[:], seed[:], ACT.Exp)
         nc.sync.dma_start(us_sb[:], us.rearrange("(h p t) o -> p h (t o)", h=HALVES, t=PACK))
         nc.sync.dma_start(wt_sb[:], wt.rearrange("(h p t) o -> p h (t o)", h=HALVES, t=PACK))
         nc.sync.dma_start(k_win[1][:], k_planes[1])
@@ -113,11 +111,11 @@ def tile_attend_gsma_q_pl_kernel(
             nc.vector.tensor_copy(picked[:], window[:].indirect(offsets[:]))
             return picked
 
-        def columns_of(view, name):
+        def columns_of(view, name, tag=""):
             turned = psum.tile([P, PACK, P], F32, name=name + "_turned", tag="dp", bufs=ROW_BANKS)
             for t in range(PACK):
                 nc.tensor.transpose(turned[:, t, :], view[:, t, :], ident[:])
-            columns = keep.tile([P, PACK], F32, name=name + "_columns")
+            columns = keep.tile([P, PACK], F32, name=name + "_columns", tag=tag, align_bytes=64)
             nc.scalar.copy(columns[:], turned[:, :, 0])
             return columns
 
@@ -147,7 +145,7 @@ def tile_attend_gsma_q_pl_kernel(
             nc.scalar.copy(ts_rows[:], spread[:].rearrange("r j (s u) -> r u (j s)", u=PACK))
             ts_place = columns_of(ts_rows[:], "ts_place")
         gather_keys(1)
-        tv_block = columns_of(pick(tv_win, "tv", "k_win1")[:].rearrange("p (j s) -> p j s", j=PACK), "tv_block")
+        tv_picked = pick(tv_win, "tv", "k_win1")
         v_scales = keep.tile([P, SLOTS], U8, name="v_scales", align_bytes=64, tag="k_win0")
         nc.vector.tensor_copy(v_scales[:], vs_win[:].indirect(offsets[:]))
         gather_keys(2)
@@ -177,8 +175,8 @@ def tile_attend_gsma_q_pl_kernel(
                 nc.scalar.copy(dst[:, part], src[:, part])
             return woven
 
-        def quantise(name, source, fmt, pieces=1):
-            codes = keep.tile([P, PASS], U32, name=name + "_codes", align_bytes=64)
+        def quantise(name, source, fmt, pieces=1, tag=""):
+            codes = keep.tile([P, PASS], U32, name=name + "_codes", align_bytes=64, tag=tag)
             scales = keep.tile([P, PASS], U8, name=name + "_scales", align_bytes=64)
             width = PASS // pieces
             for i in range(pieces):
@@ -196,6 +194,7 @@ def tile_attend_gsma_q_pl_kernel(
         late = q_first[1][:].rearrange("p j (m t) -> p m j t", t=PACK)
         cut = (PASS // 2 - Q0_ON_VECTOR) // PACK
         nc.scalar.copy(dealt[:, P // 2 : P // 2 + cut], late[:, :cut])
+        tv_block = columns_of(tv_picked[:].rearrange("p (j s) -> p j s", j=PACK), "tv_block", "q_first0")
         k_codes, k_scales = quantise("k", k_woven, E4M3, pieces=2)
         if Q0_ON_VECTOR > 0:
             nc.vector.tensor_copy(dealt[:, P // 2 + cut :], late[:, cut:])
@@ -214,8 +213,7 @@ def tile_attend_gsma_q_pl_kernel(
         totals = [keep.tile([P, GROUP], F32, name=f"totals{i}") for i in range(TILES // GROUP)]
         state = {}
 
-        def values_product(h, moving, tag):
-            blocks = keep.tile([P, PACK, PACK, P], F32, name=f"d_blocks{h}", tag=tag)
+        def values_product(h, moving, blocks):
             for j in range(PACK):
                 cols = slice(j * P, (j + 1) * P)
                 bank = psum.tile([P, PASS], F32, name="b_bank", tag="mx", bufs=MX_BANKS)
@@ -246,7 +244,7 @@ def tile_attend_gsma_q_pl_kernel(
                 out=bank[:], lhsT=q_mx[h][0][:, cols].bitcast(E4M3), lhsT_scale=q_mx[h][1][:, cols],
                 rhs=k_codes[:].bitcast(E4M3), rhs_scale=k_scales[:], start=True, stop=True,
             )
-            z = work.tile([P, SLOTS], F32, name="z", bufs=Z_BUFS)
+            z = work.tile([P, SLOTS], F32, name="z", tag=f"z{h}", bufs=Z_BUFS)
             nc.vector.scalar_tensor_tensor(
                 as_laid(z, n), by_place(bank[:], n), us_sb[:, h, t : t + 1], ts_nat[:] if n in PAIRED else ts_rows[:],
                 ALU.mult, ALU.mult,
@@ -258,8 +256,13 @@ def tile_attend_gsma_q_pl_kernel(
             neg_max = work.tile([P, 1], F32, name="neg_max")
             nc.vector.tensor_reduce(neg_max[:], z, AXIS.X, ALU.max, negate=True)
             if n == 0:
-                state["x0"] = keep.tile([P, PACK, SLOTS], F32, name="x_first", tag="do_raw0")
-            x = state["x0"][:, n] if n < PACK else work.tile([P, SLOTS], F32, name="x", bufs=PACK)
+                state["x0"] = keep.tile([P, 2, SLOTS], F32, name="x_first", tag="do_raw0")
+            if n < 2:
+                x = state["x0"][:, n]
+            elif n < PACK:
+                x = state["mid"][:, PACK + n - 2]
+            else:
+                x = work.tile([P, SLOTS], F32, name="x", bufs=PACK)
             nc.scalar.activation(
                 x[:], z, ACT.Exp, bias=neg_max[:], accum_out=totals[n // GROUP][:, n % GROUP : n % GROUP + 1]
             )
@@ -350,18 +353,33 @@ def tile_attend_gsma_q_pl_kernel(
                     out=bank[:], lhsT=g_codes[:].bitcast(E5M2), lhsT_scale=g_scales[:],
                     rhs=state["kt"][0][:].bitcast(E4M3), rhs_scale=state["kt"][1][:], start=True, stop=True,
                 )
-            nc.scalar.copy(result[h][:, t, :], bank[:])
+            if n == TILES - 1:
+                nc.scalar.copy(result[h][:, t, : PASS // 2], bank[:, : PASS // 2])
+                nc.scalar.copy(result[h][:, t, PASS // 2 :], bank[:, PASS // 2 :])
+            else:
+                nc.scalar.copy(result[h][:, t, :], bank[:])
             nc.sync.dma_start(out_rows[h, t], result[h][:, t, :])
 
+        plane_scales = keep.tile([P, HALVES, FEATURES], U8, name="plane_scales", align_bytes=64)
+
         def planes(h, woven):
-            codes, scales = quantise(f"plane{h}", woven, E4M3)
-            nc.sync.dma_start(out_1[h].rearrange("p c l -> p (c l)").bitcast(I32), codes[:].bitcast(I32))
-            for quad in range(4):
-                queue = nc.scalar if (h == HALVES - 1 and quad % 2 == 1) else nc.sync
-                queue.dma_start(
-                    out_2[h, 4 * quad : 4 * quad + 4, :].bitcast(I32),
-                    scales[32 * quad : 32 * quad + 4, :].bitcast(I32),
+            codes = keep.tile([P, FEATURES], U32, name=f"plane{h}_codes", align_bytes=64)
+            width = FEATURES // (1 + h)
+            for c in range(0, FEATURES, width):
+                nc.vector.quantize_mx(
+                    out=codes[:, c : c + width].bitcast(E4M3), scales=plane_scales[:, h, c : c + width],
+                    in_=woven[:, c * PACK : (c + width) * PACK],
                 )
+                nc.sync.dma_start(
+                    out_1[h].rearrange("p c l -> p (c l)").bitcast(I32)[:, c : c + width],
+                    codes[:, c : c + width].bitcast(I32),
+                )
+
+        def store_scales():
+            rows = out_2.rearrange("h f c -> f h c").bitcast(I32)
+            for quad in range(4):
+                queue = nc.scalar if quad % 2 == 0 else nc.sync
+                queue.dma_start(rows[4 * quad : 4 * quad + 4], plane_scales[32 * quad : 32 * quad + 4].bitcast(I32))
 
         def live(n):
             return 0 <= n < TILES
@@ -373,33 +391,42 @@ def tile_attend_gsma_q_pl_kernel(
         softmax(1)
         v_codes = keep.tile([P, SLOTS], U32, name="v_codes", align_bytes=64)
         nc.vector.tensor_copy(v_codes[:], vw_win[:].bitcast(U32).indirect(offsets[:]))
-        values_product(0, quantise("do0", do_woven, E5M2), "ts_win")
+        do_mx = quantise("do0", do_woven, E5M2)
+        q_woven = weave_dealt(q_second, "q1", Q1_SPLIT, "")
+        state["mid"] = keep.tile([P, PACK + 2, SLOTS], F32, name="mid", tag="row0")
+        values_product(0, do_mx, state["mid"][:, :PACK].rearrange("s j (t m) -> s j t m", t=PACK))
         scores(2)
         scores(3)
         softmax(2)
         softmax(3)
-        state["kt"] = quantise("kt", kt_woven[:].rearrange("s p t u -> s (p t u)").bitcast(BF16), E4M3)
-        q_mx.append(quantise("q1", weave_dealt(q_second, "q1", Q1_SPLIT, ""), E4M3))
-        row_sum(0)
+        q_mx.append(quantise("q1", q_woven, E4M3, pieces=2))
+        state["kt"] = quantise("kt", kt_woven[:].rearrange("s p t u -> s (p t u)").bitcast(BF16), E4M3, tag="q1_woven")
+        for n in range(PACK, PACK + EARLY):
+            scores(n)
+        for n in range(PACK, PACK + EARLY):
+            softmax(n)
+        for n in range(AHEAD):
+            row_sum(n)
         for step in range(TILES + 2):
             if step == 0:
                 do_woven = weave(do_raw[1], "do1", DO1_SPLIT)
-            if live(step + 1):
-                row_sum(step + 1)
-            if live(step + PACK):
-                scores(step + PACK)
+            if live(step + AHEAD):
+                row_sum(step + AHEAD)
+            if live(step + PACK + EARLY):
+                scores(step + PACK + EARLY)
             if step in PAIRED:
                 weights(step)
             if live(step - 1) and step - 1 not in PAIRED:
                 gradient(step - 1)
-            if live(step + PACK):
-                softmax(step + PACK)
+            if live(step + PACK + EARLY):
+                softmax(step + PACK + EARLY)
             if step in PAIRED:
                 gradient(step)
             for n in range(TILES):
                 if step == n + (1 if n in PAIRED else 2):
                     query_gradient(n)
             if step == DO1_AT:
-                values_product(1, quantise("do1", do_woven, E5M2), "tv_win")
+                values_product(1, quantise("do1", do_woven, E5M2), keep.tile([P, PACK, PACK, P], F32, name="d_blocks1", tag="tv_win"))
         planes(0, weave(result[0], "result0", OUT0_SPLIT, 128, tag="q0_woven"))
-        planes(1, weave(result[1], "result1", OUT1_SPLIT, tag="q_first0"))
+        planes(1, weave(result[1], "result1", OUT1_SPLIT, PASS // 2, tag="q_first0"))
+        store_scales()

@@ -32,7 +32,7 @@ ROW_BANKS = 4
 GRAD_BANKS = 2
 SCORE_TAG = "dp"
 PAIRED = ()
-SHIFT_ON_VECTOR = (0, 1, 2, 3, 4, 5, 6, 7)
+SHIFT_ON_VECTOR = (4, 5, 6, 7)
 REPEAT = ()
 GROUP = 2
 PIECE = 128
@@ -41,7 +41,7 @@ Q0_PIECES = 4
 DO0_SPLIT = 0
 Q1_SPLIT = 0
 DO1_SPLIT = 0
-OUT0_SPLIT = 256
+OUT0_SPLIT = 128
 OUT1_SPLIT = 384
 XT_BUFS = 4
 LAG = 2

@@ -27,29 +27,27 @@ TILES = QUERIES // P
 
 FLOPS = 3 * 2 * QUERIES * SLOTS * FEATURES
 
-MX_BANKS = 2
-ROW_BANKS = 4
-GRAD_BANKS = 2
-SCORE_TAG = "dp"
-PAIRED = ()
-SHIFT_ON_VECTOR = (4, 5, 6, 7)
-REPEAT = ()
-GROUP = 2
+BANKS = 2
+XV_PIECES = 2
+XV_V = ()
+TS_ROW = 4
+TV_ROW = 8
+Q0_CUTS = (0, 256, 512)
+DO0_V = 0
+Q1_V = 0
+DO1_V = 0
+OUT0_V = 0
+P0_AT = 8
+OUT1_V = 384
 PIECE = 128
-Q0_ON_VECTOR = 0
-Q0_PIECES = 4
-DO0_SPLIT = 0
-Q1_SPLIT = 0
-DO1_SPLIT = 0
-OUT0_SPLIT = 128
-OUT1_SPLIT = 384
-XT_BUFS = 4
-LAG = 2
-G_LAG = 1
-DO1_AT = 0
-Z_BUFS = 2
-EARLY = 0
-AHEAD = 1
+SHIFT_V = (0, 1, 6, 7)
+LEAD = 3
+FACT = 2
+PAIRS = 0
+WARM = ()
+Q1_AT = 0
+DO1_AT = 1
+OUT0_AT = 6
 
 
 def tile_attend_gsma_q_pl_kernel(
@@ -62,118 +60,103 @@ def tile_attend_gsma_q_pl_kernel(
         psum = ctx.enter_context(tc.psum_pool(name="psum", bufs=2))
 
         k_planes = kT.rearrange("(p t) c -> t p c", t=PACK)
-        k_win = [keep.tile([P, TOKENS], F32, name=f"k_win{t}", align_bytes=64) for t in range(PACK)]
+        q_rows = qT.rearrange("(p j) (h r) -> h p j r", j=PACK, h=HALVES)
+        do_rows = doT.rearrange("(p j) (h r) -> h p j r", j=PACK, h=HALVES)
         offsets = keep.tile([P, SLOTS // 16], U16, name="offsets")
-        ts_row = keep.tile([1, TOKENS], F32, name="ts_row", align_bytes=64)
-        tv_row = keep.tile([1, TOKENS], F32, name="tv_row", tag="row1")
-        us_sb = keep.tile([P, HALVES, PACK], F32, name="us_sb")
-        wt_sb = keep.tile([P, HALVES, PACK], F32, name="wt_sb")
-        ts_win = keep.tile([P, TOKENS], F32, name="ts_win")
+        k_win = [keep.tile([P, TOKENS], F32, name=f"k_win{t}", align_bytes=64) for t in range(PACK)]
         vs_win = keep.tile([P, TOKENS], U8, name="vs_win")
+        ts_win = keep.tile([P, TOKENS], F32, name="ts_win", align_bytes=64)
+        tv_win = keep.tile([P, TOKENS], F32, name="tv_win", align_bytes=64)
         nc.vector.memset(ts_win[:].bitcast(I32), 0)
+        nc.vector.memset(tv_win[:].bitcast(I32), 0)
         nc.vector.memset(vs_win[:].bitcast(I32), 0)
-        nc.sync.dma_start(ts_row[:], ts[0:1, :])
-        nc.sync.dma_start(k_win[0][:], k_planes[0])
         nc.sync.dma_start(offsets[:], offs)
-        nc.scalar.dma_start(tv_row[:], tv[0:1, :])
-        nc.sync.dma_start(us_sb[:], us.rearrange("(h p t) o -> p h (t o)", h=HALVES, t=PACK))
-        nc.sync.dma_start(wt_sb[:], wt.rearrange("(h p t) o -> p h (t o)", h=HALVES, t=PACK))
-        nc.sync.dma_start(k_win[1][:], k_planes[1])
+        nc.scalar.dma_start(ts_win[TS_ROW : TS_ROW + 1, :], ts[0:1, :])
+        nc.scalar.dma_start(tv_win[TV_ROW : TV_ROW + 1, :], tv[0:1, :])
         for quad in range(4):
-            nc.sync.dma_start(
+            nc.scalar.dma_start(
                 vs_win[32 * quad : 32 * quad + 4, :].bitcast(I32),
                 vT_scales[0, 4 * quad : 4 * quad + 4, :].bitcast(I32),
             )
-        nc.sync.dma_start(k_win[2][:], k_planes[2])
-        nc.sync.dma_start(k_win[3][:], k_planes[3])
-        q_first = [keep.tile([P, PACK, PASS // 2], F32, name=f"q_first{i}", align_bytes=64) for i in range(2)]
-        q_rows = qT.rearrange("(p j) (h r) -> h p j r", j=PACK, h=HALVES)
-        do_rows = doT.rearrange("(p j) (h r) -> h p j r", j=PACK, h=HALVES)
-        for i in range(2):
-            nc.sync.dma_start(q_first[i][:], q_rows[0][:, :, i * PASS // 2 : (i + 1) * PASS // 2])
-        do_raw = [keep.tile([P, PACK, PASS], F32, name="do_raw0"), keep.tile([P, PACK, PASS], F32, name="do_raw1", tag="row1")]
+        for t in range(PACK):
+            nc.sync.dma_start(k_win[t][:], k_planes[t])
+        q_first = []
+        for i in range(len(Q0_CUTS) - 1):
+            q_first.append(keep.tile([P, PACK, Q0_CUTS[i + 1] - Q0_CUTS[i]], F32, name=f"q_first{i}", align_bytes=64))
+            nc.sync.dma_start(q_first[i][:], q_rows[0][:, :, Q0_CUTS[i] : Q0_CUTS[i + 1]])
+        us_sb = keep.tile([P, HALVES, PACK], F32, name="us_sb")
+        nc.sync.dma_start(us_sb[:], us.rearrange("(h p t) o -> p h (t o)", h=HALVES, t=PACK))
+        do_raw = [keep.tile([P, PACK, PASS], F32, name=f"do_raw{h}", align_bytes=64) for h in range(HALVES)]
         vw_win = keep.tile([P, TOKENS], I32, name="vw_win", align_bytes=64)
-        q_second = keep.tile([P, PACK, PASS], F32, name="q_raw1", tag="row0")
+        q_second = keep.tile([P, PACK, PASS], F32, name="q_second", align_bytes=64)
         nc.sync.dma_start(do_raw[0][:], do_rows[0])
         nc.sync.dma_start(vw_win[:], vT_words[0].rearrange("p c l -> p (c l)").bitcast(I32))
-
-        ident = keep.tile([P, P], F32, name="ident")
-        make_identity(nc, ident[:])
-        tv_win = keep.tile([P, TOKENS], F32, name="tv_win")
-        nc.vector.memset(tv_win[:].bitcast(I32), 0)
-        nc.scalar.activation(ts_win[0:1, :], ts_row[:], ACT.Copy)
-        nc.scalar.activation(tv_win[0:1, :], tv_row[:], ACT.Copy)
         nc.sync.dma_start(q_second[:], q_rows[1])
         nc.sync.dma_start(do_raw[1][:], do_rows[1])
 
-        def pick(window, name, tag):
-            picked = keep.tile([P, SLOTS], F32, name=name + "_picked", tag=tag, align_bytes=64)
-            nc.vector.tensor_copy(picked[:], window[:].indirect(offsets[:]))
+        ident = keep.tile([P, P], F32, name="ident")
+        make_identity(nc, ident[:])
+
+        def pick(window, name, dtype):
+            picked = keep.tile([P, SLOTS], dtype, name=name, align_bytes=64)
+            nc.vector.tensor_copy(picked[:], window.indirect(offsets[:]))
             return picked
 
-        def columns_of(view, name, tag=""):
-            turned = psum.tile([P, PACK, P], F32, name=name + "_turned", tag="dp", bufs=ROW_BANKS)
+        def columns_of(view, row, name):
+            turned = psum.tile([P, PACK, P], F32, name=name + "_turned", tag="score", bufs=BANKS)
             for t in range(PACK):
                 nc.tensor.transpose(turned[:, t, :], view[:, t, :], ident[:])
-            columns = keep.tile([P, PACK], F32, name=name + "_columns", tag=tag, align_bytes=64)
-            nc.scalar.copy(columns[:], turned[:, :, 0])
+            columns = keep.tile([P, PACK], F32, name=name + "_columns")
+            nc.scalar.activation(columns[:], turned[:, :, row], ACT.Copy)
             return columns
 
         k_picked = keep.tile([P, PACK, SLOTS], BF16, name="k_picked", align_bytes=64)
+        kt_woven = keep.tile([P, P, PACK, 2], F32, name="kt_woven", align_bytes=64)
 
         def gather_keys(t):
             nc.vector.tensor_copy(k_picked[:, t, :], k_win[t][:].indirect(offsets[:]))
 
-        def turn_keys(pair):
-            bank = psum.tile([P, 2, 2, P], F32, name=f"kt_bank{pair}", tag="grad", bufs=GRAD_BANKS)
+        def turn_keys(pair, copy):
+            bank = psum.tile([P, 2, 2, P], F32, name=f"kt_bank{pair}", tag="grad", bufs=BANKS)
             for e in range(2):
                 words = k_picked[:, 2 * pair + e, :].bitcast(F32).rearrange("p (s u) -> p u s", u=2)
                 for u in range(2):
                     nc.tensor.transpose(bank[:, e, u, :], words[:, u, :], ident[:])
-            nc.scalar.copy(kt_woven[:, :, 2 * pair : 2 * pair + 2, :], bank[:].rearrange("s e u p -> s p e u"))
+            copy(kt_woven[:, :, 2 * pair : 2 * pair + 2, :], bank[:].rearrange("s e u p -> s p e u"))
 
+        def token_rows(window, row, name):
+            columns = columns_of(pick(window[:], name + "_picked", F32)[:].rearrange("p (j s) -> p j s", j=PACK), row, name)
+            spread = psum.tile([P, PACK, P], F32, name=name + "_spread", tag="out", bufs=BANKS)
+            for j in range(PACK):
+                nc.tensor.transpose(spread[:, j, :], columns[:, j : j + 1].to_broadcast([P, P]), ident[:])
+            rows = keep.tile([P, PACK, P], F32, name=name + "_rows")
+            nc.scalar.copy(rows[:], spread[:].rearrange("r j (s u) -> r u (j s)", u=PACK))
+            return rows
+
+        ts_rows = token_rows(ts_win, TS_ROW, "ts")
         gather_keys(0)
-        ts_block = columns_of(pick(ts_win, "ts", "")[:].rearrange("p (j s) -> p j s", j=PACK), "ts")
-        spread = psum.tile([P, PACK, P], F32, name="ts_spread", tag="mx", bufs=MX_BANKS)
-        for j in range(PACK):
-            nc.tensor.transpose(spread[:, j, :], ts_block[:, j : j + 1].to_broadcast([P, P]), ident[:])
-        ts_rows = keep.tile([P, PACK, P], F32, name="ts_rows")
-        ts_nat = keep.tile([P, SLOTS], F32, name="ts_nat")
-        if len(PAIRED) > 0:
-            nc.scalar.copy(ts_nat[:], spread[:].rearrange("r j s -> r (j s)"))
-        if len(PAIRED) < TILES:
-            nc.scalar.copy(ts_rows[:], spread[:].rearrange("r j (s u) -> r u (j s)", u=PACK))
-            ts_place = columns_of(ts_rows[:], "ts_place")
+        tv_rows = token_rows(tv_win, TV_ROW, "tv")[:].rearrange("r u s -> r (u s)")
+        ts_place = columns_of(ts_rows[:], 0, "ts_place")
         gather_keys(1)
-        tv_picked = pick(tv_win, "tv", "k_win1")
-        v_scales = keep.tile([P, SLOTS], U8, name="v_scales", align_bytes=64, tag="k_win0")
-        nc.vector.tensor_copy(v_scales[:], vs_win[:].indirect(offsets[:]))
+        turn_keys(0, nc.scalar.copy)
+        v_scales = pick(vs_win[:], "v_scales", U8)
         gather_keys(2)
         gather_keys(3)
 
-        def weave(src_tile, name, split, vpiece=PASS, tag=""):
+        def shares(dst, src, width, on_vector, vpiece):
+            for c in range(0, on_vector, vpiece):
+                part = slice(c // 4, min(c + vpiece, on_vector) // 4)
+                nc.vector.tensor_copy(dst[:, part], src[:, part])
+            for c in range(on_vector, width, PIECE):
+                part = slice(c // 4, min(c + PIECE, width) // 4)
+                nc.scalar.copy(dst[:, part], src[:, part])
+
+        def weave(src_tile, name, on_vector, vpiece=PASS, tag=""):
             woven = keep.tile([P, PASS, PACK], BF16, name=name + "_woven", align_bytes=64, tag=tag)
             src = src_tile[:].rearrange("p t (c i) -> p c t i", i=4)
             dst = woven[:].rearrange("p (c i) t -> p c t i", i=4)
-            for c in range(0, split, vpiece):
-                part = slice(c // 4, min(c + vpiece, split) // 4)
-                nc.vector.tensor_copy(dst[:, part], src[:, part])
-            for c in range(split, PASS, PIECE):
-                part = slice(c // 4, min(c + PIECE, PASS) // 4)
-                nc.scalar.copy(dst[:, part], src[:, part])
+            shares(dst, src, PASS, on_vector, vpiece)
             return woven[:].rearrange("p c t -> p (c t)")
-
-        def weave_dealt(raw, name, split, tag):
-            woven = keep.tile([P, PASS * PACK], BF16, name=name + "_woven", align_bytes=64, tag=tag)
-            woven = woven[:]
-            src = raw[:].rearrange("p j (m t) -> p m j t", t=PACK)
-            dst = woven.rearrange("p (t m j) -> p m j t", t=PACK, j=PACK)
-            if split > 0:
-                nc.vector.tensor_copy(dst[:, : split // 4], src[:, : split // 4])
-            for c in range(split, PASS, PIECE):
-                part = slice(c // 4, min(c + PIECE, PASS) // 4)
-                nc.scalar.copy(dst[:, part], src[:, part])
-            return woven
 
         def quantise(name, source, fmt, pieces=1, tag=""):
             codes = keep.tile([P, PASS], U32, name=name + "_codes", align_bytes=64, tag=tag)
@@ -190,64 +173,61 @@ def tile_attend_gsma_q_pl_kernel(
         k_woven = weave(k_picked, "k", PASS, PASS // 2)
         q_dealt = keep.tile([P, PACK, P, PACK], BF16, name="q0_woven", align_bytes=64)
         dealt = q_dealt[:].rearrange("p t m j -> p m j t")
-        nc.scalar.copy(dealt[:, : P // 2], q_first[0][:].rearrange("p j (m t) -> p m j t", t=PACK))
-        late = q_first[1][:].rearrange("p j (m t) -> p m j t", t=PACK)
-        cut = (PASS // 2 - Q0_ON_VECTOR) // PACK
-        nc.scalar.copy(dealt[:, P // 2 : P // 2 + cut], late[:, :cut])
-        tv_block = columns_of(tv_picked[:].rearrange("p (j s) -> p j s", j=PACK), "tv_block", "q_first0")
+        for i in range(len(q_first)):
+            nc.scalar.copy(
+                dealt[:, Q0_CUTS[i] // PACK : Q0_CUTS[i + 1] // PACK], q_first[i][:].rearrange("p j (m t) -> p m j t", t=PACK)
+            )
+        wt_sb = keep.tile([P, HALVES, PACK], F32, name="wt_sb", tag="q_first1", align_bytes=64)
+        nc.scalar.dma_start(wt_sb[:], wt.rearrange("(h p t) o -> p h (t o)", h=HALVES, t=PACK))
         k_codes, k_scales = quantise("k", k_woven, E4M3, pieces=2)
-        if Q0_ON_VECTOR > 0:
-            nc.vector.tensor_copy(dealt[:, P // 2 + cut :], late[:, cut:])
-        q_mx = [quantise("q0", q_dealt[:].rearrange("p t m j -> p (t m j)"), E4M3, pieces=Q0_PIECES)]
-        uswt = keep.tile([P, 2, TILES], F32, name="uswt", tag="vs_win")
-        nc.vector.tensor_tensor(
-            uswt[:, 0], us_sb[:].rearrange("p h t -> p (h t)"), wt_sb[:].rearrange("p h t -> p (h t)"), ALU.mult
-        )
-        nc.vector.memset(uswt[:, 1], -1.0)
-        kt_woven = keep.tile([P, P, PACK, 2], F32, name="kt_woven", align_bytes=64, tag="q_first1")
-        turn_keys(0)
-        turn_keys(1)
+        turn_keys(1, nc.vector.tensor_copy)
+        q_mx = [quantise("q0", q_dealt[:].rearrange("p t m j -> p (t m j)"), E4M3, pieces=PACK)]
+        kt_mx = quantise("kt", kt_woven[:].rearrange("s p t u -> s (p t u)").bitcast(BF16), E4M3, tag="q0_woven")
 
         result = [keep.tile([P, PACK, FEATURES], F32, name=f"result{h}", tag=f"k_win{h + 2}", align_bytes=64) for h in range(HALVES)]
         out_rows = out_0.rearrange("(h p t) d -> h t p d", h=HALVES, t=PACK)
-        totals = [keep.tile([P, GROUP], F32, name=f"totals{i}") for i in range(TILES // GROUP)]
+        uswt = keep.tile([P, TILES, 2], F32, name="uswt")
+        nc.vector.memset(uswt[:, :, 1], -1.0)
         state = {}
 
-        def values_product(h, moving, blocks):
-            for j in range(PACK):
-                cols = slice(j * P, (j + 1) * P)
-                bank = psum.tile([P, PASS], F32, name="b_bank", tag="mx", bufs=MX_BANKS)
-                nc.tensor.matmul_mx(
-                    out=bank[:], lhsT=v_codes[:, cols].bitcast(E4M3), lhsT_scale=v_scales[:, cols],
-                    rhs=moving[0][:].bitcast(E5M2), rhs_scale=moving[1][:], start=True, stop=True,
-                )
-                nc.scalar.activation(
-                    blocks[:, j], bank[:].rearrange("s (m t) -> s t m", t=PACK), ACT.Copy, scale=tv_block[:, j : j + 1]
-                )
-            state[("b", h)] = blocks
-
-        def by_place(view, n):
-            if n in PAIRED:
-                return view
-            return view.rearrange("r (s u) -> r u s", u=PACK)
-
-        def as_laid(tile, n):
-            if n in PAIRED:
-                return tile[:]
-            return tile[:].rearrange("r (u s) -> r u s", u=PACK)
-
-        def scores(n):
+        def values_pass(n):
             h, t = divmod(n, PACK)
             cols = slice(t * P, (t + 1) * P)
-            bank = psum.tile([P, SLOTS], F32, name="score_bank", tag=SCORE_TAG, bufs=ROW_BANKS if SCORE_TAG == "dp" else MX_BANKS)
+            bank = psum.tile([P, SLOTS], F32, name="b_bank", tag="value", bufs=BANKS)
+            nc.tensor.matmul_mx(
+                out=bank[:], lhsT=do_mx[h][0][:, cols].bitcast(E5M2), lhsT_scale=do_mx[h][1][:, cols],
+                rhs=v_codes[:].bitcast(E4M3), rhs_scale=v_scales[:], start=True, stop=True,
+            )
+            state[("b", n)] = bank
+
+        def deal(raw, name, on_vector):
+            woven = keep.tile([P, PACK, P, PACK], BF16, name=name + "_woven", align_bytes=64)
+            shares(woven[:].rearrange("p t m j -> p m j t"), raw[:].rearrange("p j (m t) -> p m j t", t=PACK), PASS, on_vector, PASS)
+            return woven[:].rearrange("p t m j -> p (t m j)")
+
+        def by_place(view):
+            return view.rearrange("r (s u) -> r u s", u=PACK)
+
+        def as_laid(tile):
+            return tile[:].rearrange("r (u s) -> r u s", u=PACK)
+
+        def score_pass(n):
+            h, t = divmod(n, PACK)
+            cols = slice(t * P, (t + 1) * P)
+            bank = psum.tile([P, SLOTS], F32, name="score_bank", tag="score", bufs=BANKS)
             nc.tensor.matmul_mx(
                 out=bank[:], lhsT=q_mx[h][0][:, cols].bitcast(E4M3), lhsT_scale=q_mx[h][1][:, cols],
                 rhs=k_codes[:].bitcast(E4M3), rhs_scale=k_scales[:], start=True, stop=True,
             )
-            z = work.tile([P, SLOTS], F32, name="z", tag=f"z{h}", bufs=Z_BUFS)
+            state[("a", n)] = bank
+
+        def scores(n):
+            h, t = divmod(n, PACK)
+            if n == 2:
+                state["z_late"] = keep.tile([P, 2, SLOTS], F32, name="z_late", tag="vw_win", align_bytes=64)
+            z = state["z_late"][:, n - 2] if n in (2, 3) else work.tile([P, SLOTS], F32, name="z", bufs=2)
             nc.vector.scalar_tensor_tensor(
-                as_laid(z, n), by_place(bank[:], n), us_sb[:, h, t : t + 1], ts_nat[:] if n in PAIRED else ts_rows[:],
-                ALU.mult, ALU.mult,
+                as_laid(z), by_place(state[("a", n)][:]), us_sb[:, h, t : t + 1], ts_rows[:], ALU.mult, ALU.mult
             )
             state[("z", n)] = z
 
@@ -255,90 +235,77 @@ def tile_attend_gsma_q_pl_kernel(
             z = state[("z", n)][:]
             neg_max = work.tile([P, 1], F32, name="neg_max")
             nc.vector.tensor_reduce(neg_max[:], z, AXIS.X, ALU.max, negate=True)
-            if n == 0:
-                state["x0"] = keep.tile([P, 2, SLOTS], F32, name="x_first", tag="do_raw0")
-            if n < 2:
-                x = state["x0"][:, n]
-            elif n < PACK:
-                x = state["mid"][:, PACK + n - 2]
+            if n == 2:
+                x = keep.tile([P, SLOTS], F32, name="x_late", tag="q_second", align_bytes=64)
             else:
                 x = work.tile([P, SLOTS], F32, name="x", bufs=PACK)
-            nc.scalar.activation(
-                x[:], z, ACT.Exp, bias=neg_max[:], accum_out=totals[n // GROUP][:, n % GROUP : n % GROUP + 1]
-            )
-            state[("x", n)] = x
-            if n % GROUP == GROUP - 1:
-                row_factors(n // GROUP)
+            total = work.tile([P, 1], F32, name="total", bufs=PACK + 1)
+            nc.scalar.activation(x[:], z, ACT.Exp, bias=neg_max[:], accum_out=total[:])
+            state[("x", n)] = (x, None, total)
+            if n > 1:
+                value_weights(n)
 
-        def row_factors(i):
-            inverse = keep.tile([P, GROUP], F32, name=f"inverse{i}")
-            nc.vector.reciprocal(inverse[:], totals[i][:])
-            gate = keep.tile([P, 2, GROUP], F32, name=f"gate{i}")
-            nc.vector.tensor_tensor(
-                gate[:], inverse[:].unsqueeze(1).to_broadcast([P, 2, GROUP]),
-                uswt[:, :, i * GROUP : (i + 1) * GROUP], ALU.mult,
-            )
-            for e in range(GROUP):
-                state[("rows", i * GROUP + e)] = (
-                    gate[:, 0, e : e + 1], (inverse[:] if i * GROUP + e in PAIRED else gate[:, 1])[:, e : e + 1]
-                )
+        def value_weights(n):
+            x, none, total = state[("x", n)]
+            if n == 0:
+                xv = keep.tile([P, SLOTS], F32, name="xv_first", tag="do0_woven", align_bytes=64)
+            else:
+                xv = work.tile([P, SLOTS], F32, name="xv", bufs=PACK)
+            if n in XV_V:
+                nc.vector.tensor_tensor(xv[:], x[:], tv_rows, ALU.mult)
+            else:
+                for c in range(0, SLOTS, SLOTS // XV_PIECES):
+                    cols = slice(c, c + SLOTS // XV_PIECES)
+                    nc.gpsimd.tensor_tensor(xv[:, cols], x[:, cols], tv_rows[:, cols], ALU.mult)
+            state[("x", n)] = (x, xv, total)
 
-        def weights(n):
-            if n not in PAIRED:
-                return
-            xt = work.tile([P, SLOTS], F32, name="xt", bufs=XT_BUFS)
-            nc.vector.scalar_tensor_tensor(xt[:], state[("x", n)][:], state[("rows", n)][0], ts_nat[:], ALU.mult, ALU.mult)
-            state[("xt", n)] = xt
+        def row_factors(n):
+            inverse = work.tile([P, 1], F32, name="inverse", bufs=PACK + 1)
+            nc.vector.reciprocal(inverse[:], state[("x", n)][2][:])
+            gate = work.tile([P, 2], F32, name="gate", bufs=PACK + 1)
+            nc.scalar.activation(gate[:], uswt[:, n, :], ACT.Copy, scale=inverse[:])
+            state[("rows", n)] = (gate[:, 0:1], gate[:, 1:2])
 
         def row_sum(n):
-            h, t = divmod(n, PACK)
-            bank = psum.tile([P, PACK, P], F32, name="dp_bank", tag="dp", bufs=ROW_BANKS)
-            for j in range(PACK):
-                nc.tensor.transpose(bank[:, j, :], state[("b", h)][:, j, t, :], ident[:])
-            dp = bank[:].rearrange("r j s -> r (j s)")
             pdp = work.tile([P, SLOTS], F32, name="pdp")
             delta = work.tile([P, 1], F32, name="delta")
             nc.vector.scalar_tensor_tensor(
-                as_laid(pdp, n), by_place(dp, n), state[("rows", n)][1 if n in PAIRED else 0],
-                as_laid(state[("x", n)], n), ALU.mult, ALU.mult, accum_out=delta[:],
+                as_laid(pdp), by_place(state[("b", n)][:]), state[("rows", n)][0], as_laid(state[("x", n)][1]),
+                ALU.mult, ALU.mult, accum_out=delta[:],
             )
-            state[("pdp", n)] = (dp, pdp, delta)
-            if n in PAIRED:
-                return
+            grad = psum.tile([P, PACK, P], F32, name="grad_bank", tag="grad", bufs=BANKS)
+            for u in range(PACK):
+                nc.tensor.matmul(grad[:, u, :], pdp[:, u * P : (u + 1) * P], ident[:], start=u == 0, stop=False, is_transpose=True)
+            state[("grad", n)] = grad
+            state[("delta", n)] = delta
+
+        def centre(n):
+            delta = state[("delta", n)]
             shift = work.tile([P, SLOTS], F32, name="shift")
-            if n in SHIFT_ON_VECTOR:
-                nc.vector.tensor_scalar(shift[:], state[("x", n)][:], delta[:], state[("rows", n)][1], ALU.mult, ALU.mult)
+            if n in SHIFT_V:
+                nc.vector.tensor_scalar(shift[:], state[("x", n)][0][:], delta[:], state[("rows", n)][1], ALU.mult, ALU.mult)
             else:
                 factor = work.tile([P, 1], F32, name="factor")
                 nc.scalar.activation(factor[:], delta[:], ACT.Copy, scale=state[("rows", n)][1])
-                nc.scalar.activation(shift[:], state[("x", n)][:], ACT.Copy, scale=factor[:])
-            grad = psum.tile([P, PACK, P], F32, name="grad_bank", tag="grad", bufs=GRAD_BANKS)
+                nc.scalar.activation(shift[:], state[("x", n)][0][:], ACT.Copy, scale=factor[:])
             for u in range(PACK):
-                cols = slice(u * P, (u + 1) * P)
-                nc.tensor.matmul(grad[:, u, :], pdp[:, cols], ident[:], start=True, stop=False, is_transpose=True)
-                nc.tensor.matmul(grad[:, u, :], shift[:, cols], ident[:], start=False, stop=True, is_transpose=True)
-            state[("grad", n)] = grad
+                nc.tensor.matmul(
+                    state[("grad", n)][:, u, :], shift[:, u * P : (u + 1) * P], ident[:], start=False, stop=u == PACK - 1, is_transpose=True
+                )
 
         def gradient(n):
             g = work.tile([P, P, PACK], BF16, name="g", align_bytes=64)
-            if n in PAIRED:
-                dp, pdp, delta = state[("pdp", n)]
-                rows = work.tile([P, SLOTS], BF16, name="g_rows", align_bytes=64)
-                nc.vector.scalar_tensor_tensor(rows[:], dp, delta[:], state[("xt", n)][:], ALU.subtract, ALU.mult)
-                bank = psum.tile([P, 2, P], F32, name="pair_bank", tag="grad", bufs=GRAD_BANKS)
-                words = rows[:].bitcast(F32).rearrange("r (s u) -> r u s", u=2)
-                for u in range(2):
-                    nc.tensor.transpose(bank[:, u, :], words[:, u, :], ident[:])
-                nc.scalar.copy(
-                    g[:].rearrange("s r u -> s (r u)").bitcast(F32).rearrange("s (r u) -> s r u", u=2),
-                    bank[:].rearrange("s u r -> s r u"),
-                )
-            else:
-                nc.vector.tensor_tensor(
-                    g[:], state[("grad", n)][:].rearrange("s u r -> s r u"),
-                    ts_place[:].unsqueeze(1).to_broadcast([P, P, PACK]), ALU.mult,
-                )
+            nc.vector.tensor_tensor(
+                g[:], state[("grad", n)][:].rearrange("s u r -> s r u"),
+                ts_place[:].unsqueeze(1).to_broadcast([P, P, PACK]), ALU.mult,
+            )
             state[("g", n)] = g
+
+        def result_pass(bank, codes, scales):
+            nc.tensor.matmul_mx(
+                out=bank[:], lhsT=codes[:].bitcast(E5M2), lhsT_scale=scales[:],
+                rhs=kt_mx[0][:].bitcast(E4M3), rhs_scale=kt_mx[1][:], start=True, stop=True,
+            )
 
         def query_gradient(n):
             h, t = divmod(n, PACK)
@@ -347,12 +314,11 @@ def tile_attend_gsma_q_pl_kernel(
             nc.vector.quantize_mx(
                 out=g_codes[:].bitcast(E5M2), scales=g_scales[:], in_=state[("g", n)][:].rearrange("s r u -> s (r u)")
             )
-            bank = psum.tile([P, FEATURES], F32, name="out_bank", tag="mx", bufs=MX_BANKS)
-            for again in range(2 if n in REPEAT else 1):
-                nc.tensor.matmul_mx(
-                    out=bank[:], lhsT=g_codes[:].bitcast(E5M2), lhsT_scale=g_scales[:],
-                    rhs=state["kt"][0][:].bitcast(E4M3), rhs_scale=state["kt"][1][:], start=True, stop=True,
-                )
+            bank = psum.tile([P, FEATURES], F32, name="out_bank", tag="out", bufs=BANKS)
+            if n in WARM:
+                result_pass(bank, *state["last"])
+            result_pass(bank, g_codes, g_scales)
+            state["last"] = (g_codes, g_scales)
             if n == TILES - 1:
                 nc.scalar.copy(result[h][:, t, : PASS // 2], bank[:, : PASS // 2])
                 nc.scalar.copy(result[h][:, t, PASS // 2 :], bank[:, PASS // 2 :])
@@ -384,49 +350,84 @@ def tile_attend_gsma_q_pl_kernel(
         def live(n):
             return 0 <= n < TILES
 
-        do_woven = weave(do_raw[0], "do0", DO0_SPLIT)
+        score_pass(0)
+        score_pass(1)
         scores(0)
         scores(1)
+        score_pass(2)
+        score_pass(3)
+        do_woven = deal(do_raw[0], "do0", DO0_V)
         softmax(0)
         softmax(1)
-        v_codes = keep.tile([P, SLOTS], U32, name="v_codes", align_bytes=64)
-        nc.vector.tensor_copy(v_codes[:], vw_win[:].bitcast(U32).indirect(offsets[:]))
-        do_mx = quantise("do0", do_woven, E5M2)
-        q_woven = weave_dealt(q_second, "q1", Q1_SPLIT, "")
-        state["mid"] = keep.tile([P, PACK + 2, SLOTS], F32, name="mid", tag="row0")
-        values_product(0, do_mx, state["mid"][:, :PACK].rearrange("s j (t m) -> s j t m", t=PACK))
+        nc.vector.tensor_tensor(
+            uswt[:, :, 0], us_sb[:].rearrange("p h t -> p (h t)"), wt_sb[:].rearrange("p h t -> p (h t)"), ALU.mult
+        )
+        v_codes = pick(vw_win[:].bitcast(U32), "v_codes", U32)
+        row_factors(0)
+        do_mx = [quantise("do0", do_woven, E5M2)]
+        value_weights(0)
+        value_weights(1)
+        values_pass(0)
+        values_pass(1)
+        row_factors(1)
         scores(2)
         scores(3)
+        q_woven = deal(q_second, "q1", Q1_V)
         softmax(2)
         softmax(3)
-        q_mx.append(quantise("q1", q_woven, E4M3, pieces=2))
-        state["kt"] = quantise("kt", kt_woven[:].rearrange("s p t u -> s (p t u)").bitcast(BF16), E4M3, tag="q1_woven")
-        for n in range(PACK, PACK + EARLY):
-            scores(n)
-        for n in range(PACK, PACK + EARLY):
-            softmax(n)
-        for n in range(AHEAD):
-            row_sum(n)
-        for step in range(TILES + 2):
-            if step == 0:
-                do_woven = weave(do_raw[1], "do1", DO1_SPLIT)
-            if live(step + AHEAD):
-                row_sum(step + AHEAD)
-            if live(step + PACK + EARLY):
-                scores(step + PACK + EARLY)
-            if step in PAIRED:
-                weights(step)
-            if live(step - 1) and step - 1 not in PAIRED:
+        first = keep.tile([P, PASS, PACK], BF16, name="result0_woven", align_bytes=64, tag="k_woven")
+
+        def weave_first(piece, copy):
+            part = slice(piece * PIECE // 4, (piece + 1) * PIECE // 4)
+            copy(first[:].rearrange("p (c i) t -> p c t i", i=4)[:, part], result[0][:].rearrange("p t (c i) -> p c t i", i=4)[:, part])
+
+        for step in range(TILES + 1):
+            ahead = step + LEAD
+            fresh = PACK <= ahead < TILES
+            if live(step):
+                row_sum(step)
+            if 2 <= step + FACT < TILES:
+                row_factors(step + FACT)
+            if live(step) and step not in SHIFT_V:
+                centre(step)
+            if step == Q1_AT:
+                q_mx.append(quantise("q1", q_woven, E4M3))
+                do_woven = deal(do_raw[1], "do1", DO1_V)
+            if step == OUT0_AT:
+                for piece in range(OUT0_V, PACK):
+                    weave_first(piece, nc.scalar.copy)
+            if OUT0_AT <= step and 2 * (step - OUT0_AT) < OUT0_V:
+                weave_first(2 * (step - OUT0_AT), nc.vector.tensor_copy)
+            if step == P0_AT:
+                planes(0, first[:].rearrange("p c t -> p (c t)"))
+            if fresh:
+                scores(ahead)
+            if live(step) and step in SHIFT_V and step >= OUT0_AT:
+                centre(step)
+            if live(step - 1):
                 gradient(step - 1)
-            if live(step + PACK + EARLY):
-                softmax(step + PACK + EARLY)
-            if step in PAIRED:
-                gradient(step)
-            for n in range(TILES):
-                if step == n + (1 if n in PAIRED else 2):
-                    query_gradient(n)
+            if live(step) and step in SHIFT_V and step < OUT0_AT:
+                centre(step)
+            if OUT0_AT <= step and 2 * (step - OUT0_AT) + 1 < OUT0_V:
+                weave_first(2 * (step - OUT0_AT) + 1, nc.vector.tensor_copy)
+            if fresh:
+                softmax(ahead)
+            if live(step - 1):
+                query_gradient(step - 1)
             if step == DO1_AT:
-                values_product(1, quantise("do1", do_woven, E5M2), keep.tile([P, PACK, PACK, P], F32, name="d_blocks1", tag="tv_win"))
-        planes(0, weave(result[0], "result0", OUT0_SPLIT, 128, tag="q0_woven"))
-        planes(1, weave(result[1], "result1", OUT1_SPLIT, PASS // 2, tag="q_first0"))
+                do_mx.append(quantise("do1", do_woven, E5M2))
+            if PACK <= ahead + 1 < TILES:
+                score_pass(ahead + 1)
+            if live(step + 2):
+                values_pass(step + 2)
+        last = keep.tile([P, PASS, PACK], BF16, name="result1_woven", align_bytes=64, tag="q1_woven")
+        if PAIRS:
+            src = result[1][:].rearrange("p t (c i) -> p c t i", i=4)
+            dst = last[:].rearrange("p (c i) t -> p c t i", i=4)
+            nc.vector.tensor_copy(dst[:, :, :2], src[:, :, :2])
+            for c in range(0, PASS // 4, PASS // 8):
+                nc.vector.tensor_copy(dst[:, c : c + PASS // 8, 2:], src[:, c : c + PASS // 8, 2:])
+        else:
+            shares(last[:].rearrange("p (c i) t -> p c t i", i=4), result[1][:].rearrange("p t (c i) -> p c t i", i=4), PASS, OUT1_V, PASS // 2)
+        planes(1, last[:].rearrange("p c t -> p (c t)"))
         store_scales()

@@ -1,7 +1,6 @@
 from contextlib import ExitStack
 
 import concourse.mybir as mybir
-from concourse.masks import make_identity
 
 F32 = mybir.dt.float32
 BF16 = mybir.dt.bfloat16
@@ -30,8 +29,6 @@ FLOPS = 3 * 2 * QUERIES * SLOTS * FEATURES
 BANKS = 2
 XV_PIECES = 2
 XV_V = ()
-TS_ROW = 4
-TV_ROW = 8
 Q0_CUTS = (0, 256, 512)
 DO0_V = 0
 Q1_V = 0
@@ -67,18 +64,19 @@ def tile_attend_gsma_q_pl_kernel(
         vs_win = keep.tile([P, TOKENS], U8, name="vs_win")
         ts_win = keep.tile([P, TOKENS], F32, name="ts_win", align_bytes=64)
         tv_win = keep.tile([P, TOKENS], F32, name="tv_win", align_bytes=64)
-        nc.vector.memset(ts_win[:].bitcast(I32), 0)
-        nc.vector.memset(tv_win[:].bitcast(I32), 0)
+        ts_flat = keep.tile([P, P], F32, name="ts_flat")
+        tv_flat = keep.tile([P, P], F32, name="tv_flat")
         nc.vector.memset(vs_win[:].bitcast(I32), 0)
         nc.sync.dma_start(offsets[:], offs)
-        nc.scalar.dma_start(ts_win[TS_ROW : TS_ROW + 1, :], ts[0:1, :])
-        nc.scalar.dma_start(tv_win[TV_ROW : TV_ROW + 1, :], tv[0:1, :])
+        nc.scalar.dma_start(ts_flat[:], ts[0 : P * P // TOKENS, :].rearrange("r (j n) -> (r j) n", n=P))
+        nc.scalar.dma_start(tv_flat[:], tv[0 : P * P // TOKENS, :].rearrange("r (j n) -> (r j) n", n=P))
+        nc.sync.dma_start(k_win[0][:], k_planes[0])
         for quad in range(4):
-            nc.scalar.dma_start(
+            nc.sync.dma_start(
                 vs_win[32 * quad : 32 * quad + 4, :].bitcast(I32),
                 vT_scales[0, 4 * quad : 4 * quad + 4, :].bitcast(I32),
             )
-        for t in range(PACK):
+        for t in range(1, PACK):
             nc.sync.dma_start(k_win[t][:], k_planes[t])
         q_first = []
         for i in range(len(Q0_CUTS) - 1):
@@ -91,24 +89,42 @@ def tile_attend_gsma_q_pl_kernel(
         q_second = keep.tile([P, PACK, PASS], F32, name="q_second", align_bytes=64)
         nc.sync.dma_start(do_raw[0][:], do_rows[0])
         nc.sync.dma_start(vw_win[:], vT_words[0].rearrange("p c l -> p (c l)").bitcast(I32))
+        wt_sb = keep.tile([P, HALVES, PACK], F32, name="wt_sb")
+        nc.sync.dma_start(wt_sb[:], wt.rearrange("(h p t) o -> p h (t o)", h=HALVES, t=PACK))
         nc.sync.dma_start(q_second[:], q_rows[1])
         nc.sync.dma_start(do_raw[1][:], do_rows[1])
 
         ident = keep.tile([P, P], F32, name="ident")
-        make_identity(nc, ident[:])
+        ones = keep.tile([P, P], F32, name="ones")
+        ramp = keep.tile([P, P], F32, name="ramp", align_bytes=64)
+        ramp_turned = keep.tile([P, P], F32, name="ramp_turned", align_bytes=64)
+        nc.vector.memset(ones[:], 1.0)
+        nc.vector.memset(ident[:], 0.0)
+        nc.vector.tensor_tensor_scan(ramp[:], ones[:], ones[:], 0.0, ALU.mult, ALU.add)
+        nc.vector.transpose(ramp_turned[:], ramp[:])
+        for quad in range(4):
+            block = slice(32 * quad, 32 * quad + 32)
+            nc.vector.tensor_tensor(ident[block, block], ramp[block, block], ramp_turned[block, block], ALU.is_equal)
 
-        def pick(window, name, dtype):
-            picked = keep.tile([P, SLOTS], dtype, name=name, align_bytes=64)
+        def pick(window, name, dtype, tag=""):
+            picked = keep.tile([P, SLOTS], dtype, name=name, align_bytes=64, tag=tag)
             nc.vector.tensor_copy(picked[:], window.indirect(offsets[:]))
             return picked
 
-        def columns_of(view, row, name):
-            turned = psum.tile([P, PACK, P], F32, name=name + "_turned", tag="score", bufs=BANKS)
-            for t in range(PACK):
-                nc.tensor.transpose(turned[:, t, :], view[:, t, :], ident[:])
-            columns = keep.tile([P, PACK], F32, name=name + "_columns")
-            nc.scalar.activation(columns[:], turned[:, :, row], ACT.Copy)
-            return columns
+        def fill_window(window, flat, name):
+            turned = psum.tile([P, P], F32, name=name + "_turned", tag="out", bufs=BANKS)
+            nc.tensor.transpose(turned[:], flat[:], ident[:])
+            columns = keep.tile([P, TOKENS // P], F32, name=name + "_columns")
+            nc.scalar.copy(columns[:], turned[:, : TOKENS // P])
+            for b in range(TOKENS // PASS):
+                spread = psum.tile([P, PACK, P], F32, name=name + "_spread", tag=("score", "value")[b % 2], bufs=BANKS)
+                for j in range(PACK):
+                    column = columns[:, PACK * b + j : PACK * b + j + 1]
+                    nc.tensor.transpose(spread[:, j, :], column.to_broadcast([P, P]), ident[:])
+                nc.scalar.copy(window[:, b * PASS : (b + 1) * PASS], spread[:].rearrange("r j n -> r (j n)"))
+
+        fill_window(ts_win, ts_flat, "ts")
+        fill_window(tv_win, tv_flat, "tv")
 
         k_picked = keep.tile([P, PACK, SLOTS], BF16, name="k_picked", align_bytes=64)
         kt_woven = keep.tile([P, P, PACK, 2], F32, name="kt_woven", align_bytes=64)
@@ -124,23 +140,23 @@ def tile_attend_gsma_q_pl_kernel(
                     nc.tensor.transpose(bank[:, e, u, :], words[:, u, :], ident[:])
             copy(kt_woven[:, :, 2 * pair : 2 * pair + 2, :], bank[:].rearrange("s e u p -> s p e u"))
 
-        def token_rows(window, row, name):
-            columns = columns_of(pick(window[:], name + "_picked", F32)[:].rearrange("p (j s) -> p j s", j=PACK), row, name)
-            spread = psum.tile([P, PACK, P], F32, name=name + "_spread", tag="out", bufs=BANKS)
-            for j in range(PACK):
-                nc.tensor.transpose(spread[:, j, :], columns[:, j : j + 1].to_broadcast([P, P]), ident[:])
+        def token_rows(window, name):
             rows = keep.tile([P, PACK, P], F32, name=name + "_rows")
-            nc.scalar.copy(rows[:], spread[:].rearrange("r j (s u) -> r u (j s)", u=PACK))
+            nc.scalar.copy(rows[:], pick(window[:], name + "_picked", F32)[:].rearrange("r (s u) -> r u s", u=PACK))
             return rows
 
-        ts_rows = token_rows(ts_win, TS_ROW, "ts")
         gather_keys(0)
-        tv_rows = token_rows(tv_win, TV_ROW, "tv")[:].rearrange("r u s -> r (u s)")
-        ts_place = columns_of(ts_rows[:], 0, "ts_place")
+        ts_rows = token_rows(ts_win, "ts")
+        turned = psum.tile([P, PACK, P], F32, name="ts_place_turned", tag="out", bufs=BANKS)
+        for u in range(PACK):
+            nc.tensor.transpose(turned[:, u, :], ts_rows[:, u, :], ident[:])
+        ts_place = keep.tile([P, PACK], F32, name="ts_place")
+        nc.scalar.activation(ts_place[:], turned[:, :, 0], ACT.Copy)
         gather_keys(1)
+        tv_rows = token_rows(tv_win, "tv")[:].rearrange("r u s -> r (u s)")
         turn_keys(0, nc.scalar.copy)
-        v_scales = pick(vs_win[:], "v_scales", U8)
         gather_keys(2)
+        v_scales = pick(vs_win[:], "v_scales", U8)
         gather_keys(3)
 
         def shares(dst, src, width, on_vector, vpiece):
@@ -177,14 +193,12 @@ def tile_attend_gsma_q_pl_kernel(
             nc.scalar.copy(
                 dealt[:, Q0_CUTS[i] // PACK : Q0_CUTS[i + 1] // PACK], q_first[i][:].rearrange("p j (m t) -> p m j t", t=PACK)
             )
-        wt_sb = keep.tile([P, HALVES, PACK], F32, name="wt_sb", tag="q_first1", align_bytes=64)
-        nc.scalar.dma_start(wt_sb[:], wt.rearrange("(h p t) o -> p h (t o)", h=HALVES, t=PACK))
         k_codes, k_scales = quantise("k", k_woven, E4M3, pieces=2)
         turn_keys(1, nc.vector.tensor_copy)
         q_mx = [quantise("q0", q_dealt[:].rearrange("p t m j -> p (t m j)"), E4M3, pieces=PACK)]
         kt_mx = quantise("kt", kt_woven[:].rearrange("s p t u -> s (p t u)").bitcast(BF16), E4M3, tag="q0_woven")
 
-        result = [keep.tile([P, PACK, FEATURES], F32, name=f"result{h}", tag=f"k_win{h + 2}", align_bytes=64) for h in range(HALVES)]
+        result = [keep.tile([P, PACK, FEATURES], F32, name=f"result{h}", tag=f"k_win{h}", align_bytes=64) for h in range(HALVES)]
         out_rows = out_0.rearrange("(h p t) d -> h t p d", h=HALVES, t=PACK)
         uswt = keep.tile([P, TILES, 2], F32, name="uswt")
         nc.vector.memset(uswt[:, :, 1], -1.0)
@@ -359,10 +373,10 @@ def tile_attend_gsma_q_pl_kernel(
         do_woven = deal(do_raw[0], "do0", DO0_V)
         softmax(0)
         softmax(1)
+        v_codes = pick(vw_win[:].bitcast(U32), "v_codes", U32)
         nc.vector.tensor_tensor(
             uswt[:, :, 0], us_sb[:].rearrange("p h t -> p (h t)"), wt_sb[:].rearrange("p h t -> p (h t)"), ALU.mult
         )
-        v_codes = pick(vw_win[:].bitcast(U32), "v_codes", U32)
         row_factors(0)
         do_mx = [quantise("do0", do_woven, E5M2)]
         value_weights(0)

@@ -37,14 +37,19 @@ OUT0_V = 0
 P0_AT = 8
 OUT1_V = 384
 PIECE = 128
-SHIFT_V = (0, 1, 6, 7)
+SHIFT_V = (0, 1, 5, 6, 7)
 LEAD = 3
 FACT = 2
-PAIRS = 0
+DO1W_AT = 0
+R0_G = 0
+Q0_V = 0
+X_LATE = 2
+PAIRS = 1
 WARM = ()
+WARM_SCORE = ()
 Q1_AT = 0
 DO1_AT = 1
-OUT0_AT = 6
+OUT0_AT = 5
 
 
 def tile_attend_gsma_q_pl_kernel(
@@ -140,23 +145,23 @@ def tile_attend_gsma_q_pl_kernel(
                     nc.tensor.transpose(bank[:, e, u, :], words[:, u, :], ident[:])
             copy(kt_woven[:, :, 2 * pair : 2 * pair + 2, :], bank[:].rearrange("s e u p -> s p e u"))
 
-        def token_rows(window, name):
+        def token_rows(window, name, tag):
             rows = keep.tile([P, PACK, P], F32, name=name + "_rows")
-            nc.scalar.copy(rows[:], pick(window[:], name + "_picked", F32)[:].rearrange("r (s u) -> r u s", u=PACK))
+            nc.scalar.copy(rows[:], pick(window[:], name + "_picked", F32, tag)[:].rearrange("r (s u) -> r u s", u=PACK))
             return rows
 
         gather_keys(0)
-        ts_rows = token_rows(ts_win, "ts")
+        v_scales = pick(vs_win[:], "v_scales", U8)
+        gather_keys(1)
+        ts_rows = token_rows(ts_win, "ts", "k_win1")
+        turn_keys(0, nc.scalar.copy)
         turned = psum.tile([P, PACK, P], F32, name="ts_place_turned", tag="out", bufs=BANKS)
         for u in range(PACK):
             nc.tensor.transpose(turned[:, u, :], ts_rows[:, u, :], ident[:])
         ts_place = keep.tile([P, PACK], F32, name="ts_place")
         nc.scalar.activation(ts_place[:], turned[:, :, 0], ACT.Copy)
-        gather_keys(1)
-        tv_rows = token_rows(tv_win, "tv")[:].rearrange("r u s -> r (u s)")
-        turn_keys(0, nc.scalar.copy)
         gather_keys(2)
-        v_scales = pick(vs_win[:], "v_scales", U8)
+        tv_rows = token_rows(tv_win, "tv", "k_win2")[:].rearrange("r u s -> r (u s)")
         gather_keys(3)
 
         def shares(dst, src, width, on_vector, vpiece):
@@ -190,15 +195,21 @@ def tile_attend_gsma_q_pl_kernel(
         q_dealt = keep.tile([P, PACK, P, PACK], BF16, name="q0_woven", align_bytes=64)
         dealt = q_dealt[:].rearrange("p t m j -> p m j t")
         for i in range(len(q_first)):
+            width = Q0_CUTS[i + 1] - Q0_CUTS[i] - (Q0_V if i == len(q_first) - 1 else 0)
             nc.scalar.copy(
-                dealt[:, Q0_CUTS[i] // PACK : Q0_CUTS[i + 1] // PACK], q_first[i][:].rearrange("p j (m t) -> p m j t", t=PACK)
+                dealt[:, Q0_CUTS[i] // PACK : (Q0_CUTS[i] + width) // PACK],
+                q_first[i][:, :, :width].rearrange("p j (m t) -> p m j t", t=PACK),
             )
         k_codes, k_scales = quantise("k", k_woven, E4M3, pieces=2)
         turn_keys(1, nc.vector.tensor_copy)
+        if Q0_V > 0:
+            nc.vector.tensor_copy(
+                dealt[:, (PASS - Q0_V) // PACK :], q_first[-1][:, :, width:].rearrange("p j (m t) -> p m j t", t=PACK)
+            )
         q_mx = [quantise("q0", q_dealt[:].rearrange("p t m j -> p (t m j)"), E4M3, pieces=PACK)]
         kt_mx = quantise("kt", kt_woven[:].rearrange("s p t u -> s (p t u)").bitcast(BF16), E4M3, tag="q0_woven")
 
-        result = [keep.tile([P, PACK, FEATURES], F32, name=f"result{h}", tag=f"k_win{h}", align_bytes=64) for h in range(HALVES)]
+        result = [keep.tile([P, PACK, FEATURES], F32, name=f"result{h}", tag=f"k_win{3 * h}", align_bytes=64) for h in range(HALVES)]
         out_rows = out_0.rearrange("(h p t) d -> h t p d", h=HALVES, t=PACK)
         uswt = keep.tile([P, TILES, 2], F32, name="uswt")
         nc.vector.memset(uswt[:, :, 1], -1.0)
@@ -229,6 +240,11 @@ def tile_attend_gsma_q_pl_kernel(
             h, t = divmod(n, PACK)
             cols = slice(t * P, (t + 1) * P)
             bank = psum.tile([P, SLOTS], F32, name="score_bank", tag="score", bufs=BANKS)
+            for again in range(WARM_SCORE.count(n)):
+                nc.tensor.matmul_mx(
+                    out=bank[:], lhsT=k_codes[:, :P].bitcast(E4M3), lhsT_scale=k_scales[:, :P],
+                    rhs=k_codes[:].bitcast(E4M3), rhs_scale=k_scales[:], start=True, stop=True,
+                )
             nc.tensor.matmul_mx(
                 out=bank[:], lhsT=q_mx[h][0][:, cols].bitcast(E4M3), lhsT_scale=q_mx[h][1][:, cols],
                 rhs=k_codes[:].bitcast(E4M3), rhs_scale=k_scales[:], start=True, stop=True,
@@ -249,11 +265,11 @@ def tile_attend_gsma_q_pl_kernel(
             z = state[("z", n)][:]
             neg_max = work.tile([P, 1], F32, name="neg_max")
             nc.vector.tensor_reduce(neg_max[:], z, AXIS.X, ALU.max, negate=True)
-            if n == 2:
+            if n == X_LATE:
                 x = keep.tile([P, SLOTS], F32, name="x_late", tag="q_second", align_bytes=64)
             else:
-                x = work.tile([P, SLOTS], F32, name="x", bufs=PACK)
-            total = work.tile([P, 1], F32, name="total", bufs=PACK + 1)
+                x = work.tile([P, SLOTS], F32, name="x", bufs=PACK + 1)
+            total = work.tile([P, 1], F32, name="total", bufs=PACK + 2)
             nc.scalar.activation(x[:], z, ACT.Exp, bias=neg_max[:], accum_out=total[:])
             state[("x", n)] = (x, None, total)
             if n > 1:
@@ -264,7 +280,7 @@ def tile_attend_gsma_q_pl_kernel(
             if n == 0:
                 xv = keep.tile([P, SLOTS], F32, name="xv_first", tag="do0_woven", align_bytes=64)
             else:
-                xv = work.tile([P, SLOTS], F32, name="xv", bufs=PACK)
+                xv = work.tile([P, SLOTS], F32, name="xv", bufs=PACK + 1)
             if n in XV_V:
                 nc.vector.tensor_tensor(xv[:], x[:], tv_rows, ALU.mult)
             else:
@@ -308,7 +324,10 @@ def tile_attend_gsma_q_pl_kernel(
                 )
 
         def gradient(n):
-            g = work.tile([P, P, PACK], BF16, name="g", align_bytes=64)
+            if PAIRS and n == TILES - 1:
+                g = keep.tile([P, P, PACK], BF16, name="g_last", tag="q1_woven", align_bytes=64)
+            else:
+                g = work.tile([P, P, PACK], BF16, name="g", align_bytes=64)
             nc.vector.tensor_tensor(
                 g[:], state[("grad", n)][:].rearrange("s u r -> s r u"),
                 ts_place[:].unsqueeze(1).to_broadcast([P, P, PACK]), ALU.mult,
@@ -329,7 +348,7 @@ def tile_attend_gsma_q_pl_kernel(
                 out=g_codes[:].bitcast(E5M2), scales=g_scales[:], in_=state[("g", n)][:].rearrange("s r u -> s (r u)")
             )
             bank = psum.tile([P, FEATURES], F32, name="out_bank", tag="out", bufs=BANKS)
-            if n in WARM:
+            for again in range(WARM.count(n)):
                 result_pass(bank, *state["last"])
             result_pass(bank, g_codes, g_scales)
             state["last"] = (g_codes, g_scales)
@@ -406,28 +425,26 @@ def tile_attend_gsma_q_pl_kernel(
                 centre(step)
             if step == Q1_AT:
                 q_mx.append(quantise("q1", q_woven, E4M3))
-                do_woven = deal(do_raw[1], "do1", DO1_V)
+                for n in range(PACK, step + LEAD + 1):
+                    score_pass(n)
             if step == OUT0_AT:
                 for piece in range(OUT0_V, PACK):
                     weave_first(piece, nc.scalar.copy)
-            if OUT0_AT <= step and 2 * (step - OUT0_AT) < OUT0_V:
-                weave_first(2 * (step - OUT0_AT), nc.vector.tensor_copy)
-            if step == P0_AT:
-                planes(0, first[:].rearrange("p c t -> p (c t)"))
+            if step == TILES:
+                for piece in range(OUT0_V):
+                    weave_first(piece, nc.vector.tensor_copy)
             if fresh:
                 scores(ahead)
-            if live(step) and step in SHIFT_V and step >= OUT0_AT:
-                centre(step)
             if live(step - 1):
                 gradient(step - 1)
-            if live(step) and step in SHIFT_V and step < OUT0_AT:
+            if live(step) and step in SHIFT_V:
                 centre(step)
-            if OUT0_AT <= step and 2 * (step - OUT0_AT) + 1 < OUT0_V:
-                weave_first(2 * (step - OUT0_AT) + 1, nc.vector.tensor_copy)
             if fresh:
                 softmax(ahead)
             if live(step - 1):
                 query_gradient(step - 1)
+            if step == DO1W_AT:
+                do_woven = deal(do_raw[1], "do1", DO1_V)
             if step == DO1_AT:
                 do_mx.append(quantise("do1", do_woven, E5M2))
             if PACK <= ahead + 1 < TILES:
@@ -439,6 +456,7 @@ def tile_attend_gsma_q_pl_kernel(
             src = result[1][:].rearrange("p t (c i) -> p c t i", i=4)
             dst = last[:].rearrange("p (c i) t -> p c t i", i=4)
             nc.vector.tensor_copy(dst[:, :, :2], src[:, :, :2])
+            planes(0, first[:].rearrange("p c t -> p (c t)"))
             for c in range(0, PASS // 4, PASS // 8):
                 nc.vector.tensor_copy(dst[:, c : c + PASS // 8, 2:], src[:, c : c + PASS // 8, 2:])
         else:

@@ -37,15 +37,28 @@ OUT0_V = 0
 P0_AT = 8
 OUT1_V = 384
 PIECE = 128
-SHIFT_V = (0, 1, 5, 6, 7)
-LEAD = 3
+SHIFT_V = (6, 7)
+LEAD = 4
+Q1_AFTER = 0
+DO0_AFTER = 0
+DEEP = 8
 FACT = 2
+Q1_TAG = "vw_win"
+Z_BUFS = 4
+E_FIRST = 0
+Z_LATE = 9
+XV_LATE = 9
+A_FIRST = 1
+Q1_FIRST = 1
 DO1W_AT = 0
 R0_G = 0
-Q0_V = 0
-X_LATE = 2
+Q0_V = 320
+X_LATE = 9
 PAIRS = 1
-WARM = ()
+WARM = (4, 5, 6, 7)
+WARM_VALUE = (2, 3)
+KT_TAG = "q0_woven"
+WT_EARLY = 1
 WARM_SCORE = ()
 Q1_AT = 0
 DO1_AT = 1
@@ -62,8 +75,6 @@ def tile_attend_gsma_q_pl_kernel(
         psum = ctx.enter_context(tc.psum_pool(name="psum", bufs=2))
 
         k_planes = kT.rearrange("(p t) c -> t p c", t=PACK)
-        q_rows = qT.rearrange("(p j) (h r) -> h p j r", j=PACK, h=HALVES)
-        do_rows = doT.rearrange("(p j) (h r) -> h p j r", j=PACK, h=HALVES)
         offsets = keep.tile([P, SLOTS // 16], U16, name="offsets")
         k_win = [keep.tile([P, TOKENS], F32, name=f"k_win{t}", align_bytes=64) for t in range(PACK)]
         vs_win = keep.tile([P, TOKENS], U8, name="vs_win")
@@ -83,21 +94,16 @@ def tile_attend_gsma_q_pl_kernel(
             )
         for t in range(1, PACK):
             nc.sync.dma_start(k_win[t][:], k_planes[t])
-        q_first = []
-        for i in range(len(Q0_CUTS) - 1):
-            q_first.append(keep.tile([P, PACK, Q0_CUTS[i + 1] - Q0_CUTS[i]], F32, name=f"q_first{i}", align_bytes=64))
-            nc.sync.dma_start(q_first[i][:], q_rows[0][:, :, Q0_CUTS[i] : Q0_CUTS[i + 1]])
+        q_raw = keep.tile([P, PACK, QUERIES], F32, name="q_raw", align_bytes=64)
+        nc.sync.dma_start(q_raw[:], qT.rearrange("(p j) r -> p j r", j=PACK))
         us_sb = keep.tile([P, HALVES, PACK], F32, name="us_sb")
         nc.sync.dma_start(us_sb[:], us.rearrange("(h p t) o -> p h (t o)", h=HALVES, t=PACK))
-        do_raw = [keep.tile([P, PACK, PASS], F32, name=f"do_raw{h}", align_bytes=64) for h in range(HALVES)]
+        do_raw = keep.tile([P, PACK, QUERIES], F32, name="do_raw", align_bytes=64)
         vw_win = keep.tile([P, TOKENS], I32, name="vw_win", align_bytes=64)
-        q_second = keep.tile([P, PACK, PASS], F32, name="q_second", align_bytes=64)
-        nc.sync.dma_start(do_raw[0][:], do_rows[0])
-        nc.sync.dma_start(vw_win[:], vT_words[0].rearrange("p c l -> p (c l)").bitcast(I32))
         wt_sb = keep.tile([P, HALVES, PACK], F32, name="wt_sb")
         nc.sync.dma_start(wt_sb[:], wt.rearrange("(h p t) o -> p h (t o)", h=HALVES, t=PACK))
-        nc.sync.dma_start(q_second[:], q_rows[1])
-        nc.sync.dma_start(do_raw[1][:], do_rows[1])
+        nc.sync.dma_start(do_raw[:], doT.rearrange("(p j) r -> p j r", j=PACK))
+        nc.sync.dma_start(vw_win[:], vT_words[0].rearrange("p c l -> p (c l)").bitcast(I32))
 
         ident = keep.tile([P, P], F32, name="ident")
         ones = keep.tile([P, P], F32, name="ones")
@@ -132,18 +138,19 @@ def tile_attend_gsma_q_pl_kernel(
         fill_window(tv_win, tv_flat, "tv")
 
         k_picked = keep.tile([P, PACK, SLOTS], BF16, name="k_picked", align_bytes=64)
-        kt_woven = keep.tile([P, P, PACK, 2], F32, name="kt_woven", align_bytes=64)
 
         def gather_keys(t):
             nc.vector.tensor_copy(k_picked[:, t, :], k_win[t][:].indirect(offsets[:]))
 
-        def turn_keys(pair, copy):
+        def turn_keys(pair, tag):
             bank = psum.tile([P, 2, 2, P], F32, name=f"kt_bank{pair}", tag="grad", bufs=BANKS)
             for e in range(2):
                 words = k_picked[:, 2 * pair + e, :].bitcast(F32).rearrange("p (s u) -> p u s", u=2)
                 for u in range(2):
                     nc.tensor.transpose(bank[:, e, u, :], words[:, u, :], ident[:])
-            copy(kt_woven[:, :, 2 * pair : 2 * pair + 2, :], bank[:].rearrange("s e u p -> s p e u"))
+            woven = keep.tile([P, P, 2, 2], F32, name=f"kt_woven{pair}", tag=tag, align_bytes=64)
+            nc.scalar.copy(woven[:], bank[:].rearrange("s e u p -> s p e u"))
+            return woven[:].rearrange("s p e u -> s (p e u)").bitcast(BF16)
 
         def token_rows(window, name, tag):
             rows = keep.tile([P, PACK, P], F32, name=name + "_rows")
@@ -154,7 +161,7 @@ def tile_attend_gsma_q_pl_kernel(
         v_scales = pick(vs_win[:], "v_scales", U8)
         gather_keys(1)
         ts_rows = token_rows(ts_win, "ts", "k_win1")
-        turn_keys(0, nc.scalar.copy)
+        kt_woven = [turn_keys(0, "")]
         turned = psum.tile([P, PACK, P], F32, name="ts_place_turned", tag="out", bufs=BANKS)
         for u in range(PACK):
             nc.tensor.transpose(turned[:, u, :], ts_rows[:, u, :], ident[:])
@@ -192,22 +199,23 @@ def tile_attend_gsma_q_pl_kernel(
             return codes, scales
 
         k_woven = weave(k_picked, "k", PASS, PASS // 2)
-        q_dealt = keep.tile([P, PACK, P, PACK], BF16, name="q0_woven", align_bytes=64)
-        dealt = q_dealt[:].rearrange("p t m j -> p m j t")
-        for i in range(len(q_first)):
-            width = Q0_CUTS[i + 1] - Q0_CUTS[i] - (Q0_V if i == len(q_first) - 1 else 0)
-            nc.scalar.copy(
-                dealt[:, Q0_CUTS[i] // PACK : (Q0_CUTS[i] + width) // PACK],
-                q_first[i][:, :, :width].rearrange("p j (m t) -> p m j t", t=PACK),
-            )
         k_codes, k_scales = quantise("k", k_woven, E4M3, pieces=2)
-        turn_keys(1, nc.vector.tensor_copy)
-        if Q0_V > 0:
-            nc.vector.tensor_copy(
-                dealt[:, (PASS - Q0_V) // PACK :], q_first[-1][:, :, width:].rearrange("p j (m t) -> p m j t", t=PACK)
-            )
-        q_mx = [quantise("q0", q_dealt[:].rearrange("p t m j -> p (t m j)"), E4M3, pieces=PACK)]
-        kt_mx = quantise("kt", kt_woven[:].rearrange("s p t u -> s (p t u)").bitcast(BF16), E4M3, tag="q0_woven")
+        kt_woven.append(turn_keys(1, ""))
+
+        def deal(raw, h, name, on_vector):
+            woven = keep.tile([P, PACK, P, PACK], BF16, name=name + "_woven", align_bytes=64)
+            half = raw[:, :, h * PASS : (h + 1) * PASS]
+            shares(woven[:].rearrange("p t m j -> p m j t"), half.rearrange("p j (m t) -> p m j t", t=PACK), PASS, on_vector, PASS)
+            return woven[:].rearrange("p t m j -> p (t m j)")
+
+        q_mx = [quantise("q0", deal(q_raw, 0, "q0", Q0_V), E4M3, pieces=PACK)]
+        kt_mx = (
+            keep.tile([P, 2, FEATURES // 2], U32, name="kt_codes", tag=KT_TAG, align_bytes=64),
+            keep.tile([P, 2, FEATURES // 2], U8, name="kt_scales", align_bytes=64),
+        )
+        for pair in range(2):
+            nc.vector.quantize_mx(out=kt_mx[0][:, pair].bitcast(E4M3), scales=kt_mx[1][:, pair], in_=kt_woven[pair])
+
 
         result = [keep.tile([P, PACK, FEATURES], F32, name=f"result{h}", tag=f"k_win{3 * h}", align_bytes=64) for h in range(HALVES)]
         out_rows = out_0.rearrange("(h p t) d -> h t p d", h=HALVES, t=PACK)
@@ -219,16 +227,12 @@ def tile_attend_gsma_q_pl_kernel(
             h, t = divmod(n, PACK)
             cols = slice(t * P, (t + 1) * P)
             bank = psum.tile([P, SLOTS], F32, name="b_bank", tag="value", bufs=BANKS)
-            nc.tensor.matmul_mx(
-                out=bank[:], lhsT=do_mx[h][0][:, cols].bitcast(E5M2), lhsT_scale=do_mx[h][1][:, cols],
-                rhs=v_codes[:].bitcast(E4M3), rhs_scale=v_scales[:], start=True, stop=True,
-            )
+            for again in range(1 + WARM_VALUE.count(n)):
+                nc.tensor.matmul_mx(
+                    out=bank[:], lhsT=do_mx[h][0][:, cols].bitcast(E5M2), lhsT_scale=do_mx[h][1][:, cols],
+                    rhs=v_codes[:].bitcast(E4M3), rhs_scale=v_scales[:], start=True, stop=True,
+                )
             state[("b", n)] = bank
-
-        def deal(raw, name, on_vector):
-            woven = keep.tile([P, PACK, P, PACK], BF16, name=name + "_woven", align_bytes=64)
-            shares(woven[:].rearrange("p t m j -> p m j t"), raw[:].rearrange("p j (m t) -> p m j t", t=PACK), PASS, on_vector, PASS)
-            return woven[:].rearrange("p t m j -> p (t m j)")
 
         def by_place(view):
             return view.rearrange("r (s u) -> r u s", u=PACK)
@@ -253,9 +257,9 @@ def tile_attend_gsma_q_pl_kernel(
 
         def scores(n):
             h, t = divmod(n, PACK)
-            if n == 2:
+            if n == Z_LATE:
                 state["z_late"] = keep.tile([P, 2, SLOTS], F32, name="z_late", tag="vw_win", align_bytes=64)
-            z = state["z_late"][:, n - 2] if n in (2, 3) else work.tile([P, SLOTS], F32, name="z", bufs=2)
+            z = state["z_late"][:, n - Z_LATE] if Z_LATE <= n < PACK else work.tile([P, SLOTS], F32, name="z", bufs=Z_BUFS)
             nc.vector.scalar_tensor_tensor(
                 as_laid(z), by_place(state[("a", n)][:]), us_sb[:, h, t : t + 1], ts_rows[:], ALU.mult, ALU.mult
             )
@@ -268,19 +272,18 @@ def tile_attend_gsma_q_pl_kernel(
             if n == X_LATE:
                 x = keep.tile([P, SLOTS], F32, name="x_late", tag="q_second", align_bytes=64)
             else:
-                x = work.tile([P, SLOTS], F32, name="x", bufs=PACK + 1)
-            total = work.tile([P, 1], F32, name="total", bufs=PACK + 2)
+                x = work.tile([P, SLOTS], F32, name="x", bufs=DEEP)
+            total = work.tile([P, 1], F32, name="total", bufs=DEEP)
             nc.scalar.activation(x[:], z, ACT.Exp, bias=neg_max[:], accum_out=total[:])
             state[("x", n)] = (x, None, total)
-            if n > 1:
-                value_weights(n)
+            value_weights(n)
 
         def value_weights(n):
             x, none, total = state[("x", n)]
-            if n == 0:
+            if n == XV_LATE:
                 xv = keep.tile([P, SLOTS], F32, name="xv_first", tag="do0_woven", align_bytes=64)
             else:
-                xv = work.tile([P, SLOTS], F32, name="xv", bufs=PACK + 1)
+                xv = work.tile([P, SLOTS], F32, name="xv", bufs=DEEP)
             if n in XV_V:
                 nc.vector.tensor_tensor(xv[:], x[:], tv_rows, ALU.mult)
             else:
@@ -337,7 +340,8 @@ def tile_attend_gsma_q_pl_kernel(
         def result_pass(bank, codes, scales):
             nc.tensor.matmul_mx(
                 out=bank[:], lhsT=codes[:].bitcast(E5M2), lhsT_scale=scales[:],
-                rhs=kt_mx[0][:].bitcast(E4M3), rhs_scale=kt_mx[1][:], start=True, stop=True,
+                rhs=kt_mx[0][:].rearrange("s a c -> s (a c)").bitcast(E4M3), rhs_scale=kt_mx[1][:].rearrange("s a c -> s (a c)"),
+                start=True, stop=True,
             )
 
         def query_gradient(n):
@@ -352,11 +356,11 @@ def tile_attend_gsma_q_pl_kernel(
                 result_pass(bank, *state["last"])
             result_pass(bank, g_codes, g_scales)
             state["last"] = (g_codes, g_scales)
-            if n == TILES - 1:
-                nc.scalar.copy(result[h][:, t, : PASS // 2], bank[:, : PASS // 2])
-                nc.scalar.copy(result[h][:, t, PASS // 2 :], bank[:, PASS // 2 :])
-            else:
-                nc.scalar.copy(result[h][:, t, :], bank[:])
+            features = result[h][:, t, :].rearrange("r (p a e) -> r p a e", a=2, e=2)
+            columns = bank[:].rearrange("r (a p e) -> r p a e", a=2, e=2)
+            pieces = 2 if n == TILES - 1 else 1
+            for c in range(0, P, P // pieces):
+                nc.scalar.copy(features[:, c : c + P // pieces], columns[:, c : c + P // pieces])
             nc.sync.dma_start(out_rows[h, t], result[h][:, t, :])
 
         plane_scales = keep.tile([P, HALVES, FEATURES], U8, name="plane_scales", align_bytes=64)
@@ -384,31 +388,29 @@ def tile_attend_gsma_q_pl_kernel(
             return 0 <= n < TILES
 
         score_pass(0)
-        score_pass(1)
-        scores(0)
-        scores(1)
-        score_pass(2)
-        score_pass(3)
-        do_woven = deal(do_raw[0], "do0", DO0_V)
-        softmax(0)
-        softmax(1)
-        v_codes = pick(vw_win[:].bitcast(U32), "v_codes", U32)
         nc.vector.tensor_tensor(
             uswt[:, :, 0], us_sb[:].rearrange("p h t -> p (h t)"), wt_sb[:].rearrange("p h t -> p (h t)"), ALU.mult
         )
-        row_factors(0)
+        score_pass(1)
+        q_woven = deal(q_raw, 1, "q1", Q1_V)
+        for n in range(0, LEAD, 2):
+            scores(n)
+            scores(n + 1)
+            if n == Q1_AFTER:
+                q_mx.append(quantise("q1", q_woven, E4M3))
+            for later in range(n + 2, min(n + 4, LEAD + 1, TILES)):
+                score_pass(later)
+            softmax(n)
+            softmax(n + 1)
+            if n == DO0_AFTER:
+                do_woven = deal(do_raw, 0, "do0", DO0_V)
+        v_codes = pick(vw_win[:].bitcast(U32), "v_codes", U32)
         do_mx = [quantise("do0", do_woven, E5M2)]
-        value_weights(0)
-        value_weights(1)
         values_pass(0)
         values_pass(1)
+        row_factors(0)
         row_factors(1)
-        scores(2)
-        scores(3)
-        q_woven = deal(q_second, "q1", Q1_V)
-        softmax(2)
-        softmax(3)
-        first = keep.tile([P, PASS, PACK], BF16, name="result0_woven", align_bytes=64, tag="k_woven")
+        first = keep.tile([P, PASS, PACK], BF16, name="result0_woven", align_bytes=64, tag="k_picked")
 
         def weave_first(piece, copy):
             part = slice(piece * PIECE // 4, (piece + 1) * PIECE // 4)
@@ -416,20 +418,22 @@ def tile_attend_gsma_q_pl_kernel(
 
         for step in range(TILES + 1):
             ahead = step + LEAD
-            fresh = PACK <= ahead < TILES
+            fresh = ahead < TILES
             if live(step):
                 row_sum(step)
             if 2 <= step + FACT < TILES:
                 row_factors(step + FACT)
             if live(step) and step not in SHIFT_V:
                 centre(step)
-            if step == Q1_AT:
-                q_mx.append(quantise("q1", q_woven, E4M3))
-                for n in range(PACK, step + LEAD + 1):
-                    score_pass(n)
             if step == OUT0_AT:
                 for piece in range(OUT0_V, PACK):
-                    weave_first(piece, nc.scalar.copy)
+                    if piece >= PACK - R0_G:
+                        cols = slice(piece * PIECE, (piece + 1) * PIECE)
+                        nc.gpsimd.tensor_scalar(
+                            first[:, cols], result[0][:, :, cols].rearrange("p t c -> p c t"), 1.0, 0.0, ALU.mult, ALU.add
+                        )
+                    else:
+                        weave_first(piece, nc.scalar.copy)
             if step == TILES:
                 for piece in range(OUT0_V):
                     weave_first(piece, nc.vector.tensor_copy)
@@ -444,10 +448,10 @@ def tile_attend_gsma_q_pl_kernel(
             if live(step - 1):
                 query_gradient(step - 1)
             if step == DO1W_AT:
-                do_woven = deal(do_raw[1], "do1", DO1_V)
+                do_woven = deal(do_raw, 1, "do1", DO1_V)
             if step == DO1_AT:
                 do_mx.append(quantise("do1", do_woven, E5M2))
-            if PACK <= ahead + 1 < TILES:
+            if ahead + 1 < TILES:
                 score_pass(ahead + 1)
             if live(step + 2):
                 values_pass(step + 2)

@@ -54,7 +54,6 @@ DO1W_AT = 0
 R0_G = 0
 Q0_V = 320
 X_LATE = 9
-PAIRS = 1
 WARM = (4, 5, 6, 7)
 WARM_VALUE = (2, 3)
 KT_TAG = "q0_woven"
@@ -327,10 +326,7 @@ def tile_attend_gsma_q_pl_kernel(
                 )
 
         def gradient(n):
-            if PAIRS and n == TILES - 1:
-                g = keep.tile([P, P, PACK], BF16, name="g_last", tag="q1_woven", align_bytes=64)
-            else:
-                g = work.tile([P, P, PACK], BF16, name="g", align_bytes=64)
+            g = work.tile([P, P, PACK], BF16, name="g", align_bytes=64)
             nc.vector.tensor_tensor(
                 g[:], state[("grad", n)][:].rearrange("s u r -> s r u"),
                 ts_place[:].unsqueeze(1).to_broadcast([P, P, PACK]), ALU.mult,
@@ -435,8 +431,7 @@ def tile_attend_gsma_q_pl_kernel(
                     else:
                         weave_first(piece, nc.scalar.copy)
             if step == TILES:
-                for piece in range(OUT0_V):
-                    weave_first(piece, nc.vector.tensor_copy)
+                planes(0, first[:].rearrange("p c t -> p (c t)"))
             if fresh:
                 scores(ahead)
             if live(step - 1):
@@ -456,14 +451,9 @@ def tile_attend_gsma_q_pl_kernel(
             if live(step + 2):
                 values_pass(step + 2)
         last = keep.tile([P, PASS, PACK], BF16, name="result1_woven", align_bytes=64, tag="q1_woven")
-        if PAIRS:
-            src = result[1][:].rearrange("p t (c i) -> p c t i", i=4)
-            dst = last[:].rearrange("p (c i) t -> p c t i", i=4)
-            nc.vector.tensor_copy(dst[:, :, :2], src[:, :, :2])
-            planes(0, first[:].rearrange("p c t -> p (c t)"))
-            for c in range(0, PASS // 4, PASS // 8):
-                nc.vector.tensor_copy(dst[:, c : c + PASS // 8, 2:], src[:, c : c + PASS // 8, 2:])
-        else:
-            shares(last[:].rearrange("p (c i) t -> p c t i", i=4), result[1][:].rearrange("p t (c i) -> p c t i", i=4), PASS, OUT1_V, PASS // 2)
+        shares(
+            last[:].rearrange("p (c i) t -> p c t i", i=4), result[1][:].rearrange("p t (c i) -> p c t i", i=4),
+            PASS, OUT1_V, PASS // 2,
+        )
         planes(1, last[:].rearrange("p c t -> p (c t)"))
         store_scales()

@@ -54,8 +54,8 @@ DO1W_AT = 0
 R0_G = 0
 Q0_V = 320
 X_LATE = 9
-WARM = (4, 5, 6, 7)
-WARM_VALUE = (2, 3)
+WARM = (6,)
+WARM_VALUE = (2, 3, 4, 5, 6)
 KT_TAG = "q0_woven"
 WT_EARLY = 1
 WARM_SCORE = ()

@@ -27,41 +27,26 @@ TILES = QUERIES // P
 FLOPS = 3 * 2 * QUERIES * SLOTS * FEATURES
 
 BANKS = 2
-XV_PIECES = 2
-XV_V = ()
-Q0_CUTS = (0, 256, 512)
-DO0_V = 0
-Q1_V = 0
-DO1_V = 0
-OUT0_V = 0
-P0_AT = 8
-OUT1_V = 384
 PIECE = 128
-SHIFT_V = (6, 7)
-LEAD = 4
-Q1_AFTER = 0
-DO0_AFTER = 0
-DEEP = 8
-FACT = 2
-Q1_TAG = "vw_win"
-Z_BUFS = 4
-E_FIRST = 0
-Z_LATE = 9
-XV_LATE = 9
-A_FIRST = 1
-Q1_FIRST = 1
-DO1W_AT = 0
-R0_G = 0
-Q0_V = 320
-X_LATE = 9
-WARM = (6,)
-WARM_VALUE = (2, 3, 4, 5, 6)
-KT_TAG = "q0_woven"
-WT_EARLY = 1
-WARM_SCORE = ()
-Q1_AT = 0
-DO1_AT = 1
-OUT0_AT = 5
+LOADS = ("q0", "us", "wt", "do0", "q1", "vw", "do1")
+Q0_CUTS = (("V", 0, 288, 512), ("S", 288, 512, 128))
+DO0_CUTS = (("S", 0, 256, 128), ("G", 256, 512, 64))
+Q1_CUTS = (("S", 0, 512, 128),)
+DO1_CUTS = (("S", 0, 512, 128),)
+LAST_V = 384
+MODE = "SSSSSSVV"
+LAG = 1
+P0W = 7
+WARM_OUT = ()
+WARM_VALUE = ()
+AHEAD = ((3,), (4,), (5,), (6,), (7,))
+Z_HOLD = {}
+Q1_FIRST = 4
+K_V = 352
+P0_TAG = "x5"
+DO1W = 0
+Q1Q = 0
+DO1Q = 1
 
 
 def tile_attend_gsma_q_pl_kernel(
@@ -85,24 +70,26 @@ def tile_attend_gsma_q_pl_kernel(
         nc.sync.dma_start(offsets[:], offs)
         nc.scalar.dma_start(ts_flat[:], ts[0 : P * P // TOKENS, :].rearrange("r (j n) -> (r j) n", n=P))
         nc.scalar.dma_start(tv_flat[:], tv[0 : P * P // TOKENS, :].rearrange("r (j n) -> (r j) n", n=P))
-        nc.sync.dma_start(k_win[0][:], k_planes[0])
-        for quad in range(4):
-            nc.sync.dma_start(
-                vs_win[32 * quad : 32 * quad + 4, :].bitcast(I32),
-                vT_scales[0, 4 * quad : 4 * quad + 4, :].bitcast(I32),
-            )
-        for t in range(1, PACK):
+        for row in range(4):
+            nc.scalar.dma_start(vs_win[row:P:32, :].bitcast(I32), vT_scales[0, row:16:4, :].bitcast(I32))
+        for t in range(PACK):
             nc.sync.dma_start(k_win[t][:], k_planes[t])
-        q_raw = keep.tile([P, PACK, QUERIES], F32, name="q_raw", align_bytes=64)
-        nc.sync.dma_start(q_raw[:], qT.rearrange("(p j) r -> p j r", j=PACK))
+        q_raw = [keep.tile([P, PACK, PASS], F32, name=f"q_raw{h}", align_bytes=64) for h in range(HALVES)]
+        do_raw = [keep.tile([P, PACK, PASS], F32, name=f"do_raw{h}", align_bytes=64) for h in range(HALVES)]
         us_sb = keep.tile([P, HALVES, PACK], F32, name="us_sb")
-        nc.sync.dma_start(us_sb[:], us.rearrange("(h p t) o -> p h (t o)", h=HALVES, t=PACK))
-        do_raw = keep.tile([P, PACK, QUERIES], F32, name="do_raw", align_bytes=64)
-        vw_win = keep.tile([P, TOKENS], I32, name="vw_win", align_bytes=64)
         wt_sb = keep.tile([P, HALVES, PACK], F32, name="wt_sb")
-        nc.sync.dma_start(wt_sb[:], wt.rearrange("(h p t) o -> p h (t o)", h=HALVES, t=PACK))
-        nc.sync.dma_start(do_raw[:], doT.rearrange("(p j) r -> p j r", j=PACK))
-        nc.sync.dma_start(vw_win[:], vT_words[0].rearrange("p c l -> p (c l)").bitcast(I32))
+        vw_win = keep.tile([P, TOKENS], I32, name="vw_win", align_bytes=64)
+        q_rows = qT.rearrange("(p j) (h r) -> h p j r", j=PACK, h=HALVES)
+        do_rows = doT.rearrange("(p j) (h r) -> h p j r", j=PACK, h=HALVES)
+        loads = {
+            "q0": (q_raw[0][:], q_rows[0]), "q1": (q_raw[1][:], q_rows[1]),
+            "do0": (do_raw[0][:], do_rows[0]), "do1": (do_raw[1][:], do_rows[1]),
+            "us": (us_sb[:], us.rearrange("(h p t) o -> p h (t o)", h=HALVES, t=PACK)),
+            "wt": (wt_sb[:], wt.rearrange("(h p t) o -> p h (t o)", h=HALVES, t=PACK)),
+            "vw": (vw_win[:], vT_words[0].rearrange("p c l -> p (c l)").bitcast(I32)),
+        }
+        for key in LOADS:
+            nc.sync.dma_start(*loads[key])
 
         ident = keep.tile([P, P], F32, name="ident")
         ones = keep.tile([P, P], F32, name="ones")
@@ -116,8 +103,8 @@ def tile_attend_gsma_q_pl_kernel(
             block = slice(32 * quad, 32 * quad + 32)
             nc.vector.tensor_tensor(ident[block, block], ramp[block, block], ramp_turned[block, block], ALU.is_equal)
 
-        def pick(window, name, dtype, tag=""):
-            picked = keep.tile([P, SLOTS], dtype, name=name, align_bytes=64, tag=tag)
+        def pick(window, name, dtype):
+            picked = keep.tile([P, SLOTS], dtype, name=name, align_bytes=64)
             nc.vector.tensor_copy(picked[:], window.indirect(offsets[:]))
             return picked
 
@@ -142,7 +129,7 @@ def tile_attend_gsma_q_pl_kernel(
             nc.vector.tensor_copy(k_picked[:, t, :], k_win[t][:].indirect(offsets[:]))
 
         def turn_keys(pair, tag):
-            bank = psum.tile([P, 2, 2, P], F32, name=f"kt_bank{pair}", tag="grad", bufs=BANKS)
+            bank = psum.tile([P, 2, 2, P], F32, name=f"kt_bank{pair}", tag=("score", "grad")[pair], bufs=BANKS)
             for e in range(2):
                 words = k_picked[:, 2 * pair + e, :].bitcast(F32).rearrange("p (s u) -> p u s", u=2)
                 for u in range(2):
@@ -151,15 +138,17 @@ def tile_attend_gsma_q_pl_kernel(
             nc.scalar.copy(woven[:], bank[:].rearrange("s e u p -> s p e u"))
             return woven[:].rearrange("s p e u -> s (p e u)").bitcast(BF16)
 
-        def token_rows(window, name, tag):
+        def token_rows(window, name):
             rows = keep.tile([P, PACK, P], F32, name=name + "_rows")
-            nc.scalar.copy(rows[:], pick(window[:], name + "_picked", F32, tag)[:].rearrange("r (s u) -> r u s", u=PACK))
+            picked = pick(window[:], name + "_picked", F32)
+            nc.scalar.copy(rows[:].rearrange("r u s -> r s u"), picked[:].rearrange("r (s u) -> r s u", u=PACK))
             return rows
 
         gather_keys(0)
         v_scales = pick(vs_win[:], "v_scales", U8)
+        ts_rows = token_rows(ts_win, "ts")
         gather_keys(1)
-        ts_rows = token_rows(ts_win, "ts", "k_win1")
+        tv_rows = token_rows(tv_win, "tv")[:].rearrange("r u s -> r (u s)")
         kt_woven = [turn_keys(0, "")]
         turned = psum.tile([P, PACK, P], F32, name="ts_place_turned", tag="out", bufs=BANKS)
         for u in range(PACK):
@@ -167,23 +156,42 @@ def tile_attend_gsma_q_pl_kernel(
         ts_place = keep.tile([P, PACK], F32, name="ts_place")
         nc.scalar.activation(ts_place[:], turned[:, :, 0], ACT.Copy)
         gather_keys(2)
-        tv_rows = token_rows(tv_win, "tv", "k_win2")[:].rearrange("r u s -> r (u s)")
+        kt_mx = (
+            keep.tile([P, 2, FEATURES // 2], U32, name="kt_codes", align_bytes=64),
+            keep.tile([P, 2, FEATURES // 2], U8, name="kt_scales", align_bytes=64),
+        )
+        nc.vector.quantize_mx(out=kt_mx[0][:, 0].bitcast(E4M3), scales=kt_mx[1][:, 0], in_=kt_woven[0])
         gather_keys(3)
 
-        def shares(dst, src, width, on_vector, vpiece):
-            for c in range(0, on_vector, vpiece):
-                part = slice(c // 4, min(c + vpiece, on_vector) // 4)
-                nc.vector.tensor_copy(dst[:, part], src[:, part])
-            for c in range(on_vector, width, PIECE):
-                part = slice(c // 4, min(c + PIECE, width) // 4)
-                nc.scalar.copy(dst[:, part], src[:, part])
+        def by_gpsimd(dst, src):
+            nc.gpsimd.tensor_scalar(dst, src, 1.0, 0.0, ALU.mult, ALU.add)
 
-        def weave(src_tile, name, on_vector, vpiece=PASS, tag=""):
-            woven = keep.tile([P, PASS, PACK], BF16, name=name + "_woven", align_bytes=64, tag=tag)
-            src = src_tile[:].rearrange("p t (c i) -> p c t i", i=4)
-            dst = woven[:].rearrange("p (c i) t -> p c t i", i=4)
-            shares(dst, src, PASS, on_vector, vpiece)
+        def shares(dst, src, cuts):
+            for copy, first, last, piece in cuts:
+                for c in range(first, last, piece):
+                    part = slice(c // 4, min(c + piece, last) // 4)
+                    copy(dst[:, part], src[:, part])
+
+        def weave(woven, planes_tile, cuts):
+            src = planes_tile[:].rearrange("p t (c i) -> p c t i", i=4)
+            shares(woven[:].rearrange("p (c i) t -> p c t i", i=4), src, cuts)
             return woven[:].rearrange("p c t -> p (c t)")
+
+        def deal(raw, name, cuts):
+            woven = keep.tile([P, PACK, P, PACK], BF16, name=name + "_woven", align_bytes=64)
+            parts = []
+            for engine, first, last, piece in cuts:
+                order = "p m t j" if engine == "G" else "p m j t"
+                dst, src = woven[:].rearrange("p t m j -> " + order), raw[:].rearrange("p j (m t) -> " + order, t=PACK)
+                copy = {"V": nc.vector.tensor_copy, "S": nc.scalar.copy, "G": by_gpsimd}[engine]
+                for c in range(first, last, piece):
+                    part = slice(c // 4, min(c + piece, last) // 4)
+                    parts.append((copy, dst[:, part], src[:, part]))
+            return woven[:].rearrange("p t m j -> p (t m j)"), parts
+
+        def run(parts):
+            for copy, dst, src in parts:
+                copy(dst, src)
 
         def quantise(name, source, fmt, pieces=1, tag=""):
             codes = keep.tile([P, PASS], U32, name=name + "_codes", align_bytes=64, tag=tag)
@@ -197,24 +205,12 @@ def tile_attend_gsma_q_pl_kernel(
                 )
             return codes, scales
 
-        k_woven = weave(k_picked, "k", PASS, PASS // 2)
-        k_codes, k_scales = quantise("k", k_woven, E4M3, pieces=2)
-        kt_woven.append(turn_keys(1, ""))
-
-        def deal(raw, h, name, on_vector):
-            woven = keep.tile([P, PACK, P, PACK], BF16, name=name + "_woven", align_bytes=64)
-            half = raw[:, :, h * PASS : (h + 1) * PASS]
-            shares(woven[:].rearrange("p t m j -> p m j t"), half.rearrange("p j (m t) -> p m j t", t=PACK), PASS, on_vector, PASS)
-            return woven[:].rearrange("p t m j -> p (t m j)")
-
-        q_mx = [quantise("q0", deal(q_raw, 0, "q0", Q0_V), E4M3, pieces=PACK)]
-        kt_mx = (
-            keep.tile([P, 2, FEATURES // 2], U32, name="kt_codes", tag=KT_TAG, align_bytes=64),
-            keep.tile([P, 2, FEATURES // 2], U8, name="kt_scales", align_bytes=64),
-        )
-        for pair in range(2):
-            nc.vector.quantize_mx(out=kt_mx[0][:, pair].bitcast(E4M3), scales=kt_mx[1][:, pair], in_=kt_woven[pair])
-
+        on_vector, on_scalar = nc.vector.tensor_copy, nc.scalar.copy
+        k_woven = keep.tile([P, PASS, PACK], BF16, name="k_woven", align_bytes=64)
+        k_codes, k_scales = quantise("k", weave(k_woven, k_picked, [(on_vector, 0, K_V, PASS // 2), (on_scalar, K_V, PASS, PASS)]), E4M3, pieces=2)
+        q_woven, parts = deal(q_raw[0], "q0", Q0_CUTS)
+        run(parts)
+        q_mx = [quantise("q0", q_woven, E4M3, pieces=4)]
 
         result = [keep.tile([P, PACK, FEATURES], F32, name=f"result{h}", tag=f"k_win{3 * h}", align_bytes=64) for h in range(HALVES)]
         out_rows = out_0.rearrange("(h p t) d -> h t p d", h=HALVES, t=PACK)
@@ -243,11 +239,6 @@ def tile_attend_gsma_q_pl_kernel(
             h, t = divmod(n, PACK)
             cols = slice(t * P, (t + 1) * P)
             bank = psum.tile([P, SLOTS], F32, name="score_bank", tag="score", bufs=BANKS)
-            for again in range(WARM_SCORE.count(n)):
-                nc.tensor.matmul_mx(
-                    out=bank[:], lhsT=k_codes[:, :P].bitcast(E4M3), lhsT_scale=k_scales[:, :P],
-                    rhs=k_codes[:].bitcast(E4M3), rhs_scale=k_scales[:], start=True, stop=True,
-                )
             nc.tensor.matmul_mx(
                 out=bank[:], lhsT=q_mx[h][0][:, cols].bitcast(E4M3), lhsT_scale=q_mx[h][1][:, cols],
                 rhs=k_codes[:].bitcast(E4M3), rhs_scale=k_scales[:], start=True, stop=True,
@@ -256,9 +247,10 @@ def tile_attend_gsma_q_pl_kernel(
 
         def scores(n):
             h, t = divmod(n, PACK)
-            if n == Z_LATE:
-                state["z_late"] = keep.tile([P, 2, SLOTS], F32, name="z_late", tag="vw_win", align_bytes=64)
-            z = state["z_late"][:, n - Z_LATE] if Z_LATE <= n < PACK else work.tile([P, SLOTS], F32, name="z", bufs=Z_BUFS)
+            if n in Z_HOLD:
+                z = keep.tile([P, SLOTS], F32, name=f"z{n}", tag=Z_HOLD[n], align_bytes=64)
+            else:
+                z = work.tile([P, SLOTS], F32, name=f"z{n}", tag="z", bufs=4)
             nc.vector.scalar_tensor_tensor(
                 as_laid(z), by_place(state[("a", n)][:]), us_sb[:, h, t : t + 1], ts_rows[:], ALU.mult, ALU.mult
             )
@@ -266,67 +258,69 @@ def tile_attend_gsma_q_pl_kernel(
 
         def softmax(n):
             z = state[("z", n)][:]
-            neg_max = work.tile([P, 1], F32, name="neg_max")
+            neg_max = work.tile([P, 1], F32, name=f"neg_max{n}", tag="neg_max")
             nc.vector.tensor_reduce(neg_max[:], z, AXIS.X, ALU.max, negate=True)
-            if n == X_LATE:
-                x = keep.tile([P, SLOTS], F32, name="x_late", tag="q_second", align_bytes=64)
-            else:
-                x = work.tile([P, SLOTS], F32, name="x", bufs=DEEP)
-            total = work.tile([P, 1], F32, name="total", bufs=DEEP)
+            x = keep.tile([P, SLOTS], F32, name=f"x{n}", align_bytes=64)
+            total = work.tile([P, 1], F32, name=f"total{n}", tag="total", bufs=TILES)
             nc.scalar.activation(x[:], z, ACT.Exp, bias=neg_max[:], accum_out=total[:])
-            state[("x", n)] = (x, None, total)
-            value_weights(n)
-
-        def value_weights(n):
-            x, none, total = state[("x", n)]
-            if n == XV_LATE:
-                xv = keep.tile([P, SLOTS], F32, name="xv_first", tag="do0_woven", align_bytes=64)
-            else:
-                xv = work.tile([P, SLOTS], F32, name="xv", bufs=DEEP)
-            if n in XV_V:
-                nc.vector.tensor_tensor(xv[:], x[:], tv_rows, ALU.mult)
-            else:
-                for c in range(0, SLOTS, SLOTS // XV_PIECES):
-                    cols = slice(c, c + SLOTS // XV_PIECES)
-                    nc.gpsimd.tensor_tensor(xv[:, cols], x[:, cols], tv_rows[:, cols], ALU.mult)
+            xv = keep.tile([P, SLOTS], F32, name=f"xv{n}", align_bytes=64)
+            for c in range(0, SLOTS, SLOTS // 2):
+                cols = slice(c, c + SLOTS // 2)
+                nc.gpsimd.tensor_tensor(xv[:, cols], x[:, cols], tv_rows[:, cols], ALU.mult)
             state[("x", n)] = (x, xv, total)
+            if n >= 2:
+                row_factors(n)
 
         def row_factors(n):
-            inverse = work.tile([P, 1], F32, name="inverse", bufs=PACK + 1)
+            inverse = work.tile([P, 1], F32, name=f"inverse{n}", tag="inverse", bufs=TILES)
             nc.vector.reciprocal(inverse[:], state[("x", n)][2][:])
-            gate = work.tile([P, 2], F32, name="gate", bufs=PACK + 1)
+            gate = work.tile([P, 2], F32, name=f"gate{n}", tag="gate", bufs=TILES)
             nc.scalar.activation(gate[:], uswt[:, n, :], ACT.Copy, scale=inverse[:])
             state[("rows", n)] = (gate[:, 0:1], gate[:, 1:2])
 
         def row_sum(n):
-            pdp = work.tile([P, SLOTS], F32, name="pdp")
-            delta = work.tile([P, 1], F32, name="delta")
+            pdp = work.tile([P, SLOTS], F32, name=f"pdp{n}", tag="pdp")
+            delta = work.tile([P, 1], F32, name=f"delta{n}", tag="delta")
             nc.vector.scalar_tensor_tensor(
                 as_laid(pdp), by_place(state[("b", n)][:]), state[("rows", n)][0], as_laid(state[("x", n)][1]),
                 ALU.mult, ALU.mult, accum_out=delta[:],
             )
-            grad = psum.tile([P, PACK, P], F32, name="grad_bank", tag="grad", bufs=BANKS)
-            for u in range(PACK):
-                nc.tensor.matmul(grad[:, u, :], pdp[:, u * P : (u + 1) * P], ident[:], start=u == 0, stop=False, is_transpose=True)
-            state[("grad", n)] = grad
             state[("delta", n)] = delta
+            state[("pdp", n)] = pdp
+            if MODE[n] in "SV":
+                turn(n, pdp, True, False)
 
-        def centre(n):
-            delta = state[("delta", n)]
-            shift = work.tile([P, SLOTS], F32, name="shift")
-            if n in SHIFT_V:
-                nc.vector.tensor_scalar(shift[:], state[("x", n)][0][:], delta[:], state[("rows", n)][1], ALU.mult, ALU.mult)
-            else:
-                factor = work.tile([P, 1], F32, name="factor")
-                nc.scalar.activation(factor[:], delta[:], ACT.Copy, scale=state[("rows", n)][1])
-                nc.scalar.activation(shift[:], state[("x", n)][0][:], ACT.Copy, scale=factor[:])
+        def turn(n, tile, opens, closes):
+            if opens:
+                state[("grad", n)] = psum.tile([P, PACK, P], F32, name=f"grad_bank{n}_", tag="grad", bufs=BANKS)
             for u in range(PACK):
                 nc.tensor.matmul(
-                    state[("grad", n)][:, u, :], shift[:, u * P : (u + 1) * P], ident[:], start=False, stop=u == PACK - 1, is_transpose=True
+                    state[("grad", n)][:, u, :], tile[:, u * P : (u + 1) * P], ident[:],
+                    start=opens and u == 0, stop=closes and u == PACK - 1, is_transpose=True,
                 )
 
+        def centre(n):
+            delta, x = state[("delta", n)], state[("x", n)][0]
+            shift = work.tile([P, SLOTS], F32, name=f"shift{n}", tag="shift")
+            if MODE[n] == "V":
+                nc.vector.tensor_scalar(shift[:], x[:], delta[:], state[("rows", n)][1], ALU.mult, ALU.mult)
+                return turn(n, shift, False, True)
+            factor = work.tile([P, 1], F32, name=f"factor{n}", tag="factor")
+            nc.scalar.activation(factor[:], delta[:], ACT.Copy, scale=state[("rows", n)][1])
+            if MODE[n] == "U":
+                nc.vector.scalar_tensor_tensor(shift[:], x[:], factor[:], state[("pdp", n)][:], ALU.mult, ALU.add)
+                return turn(n, shift, True, True)
+            nc.scalar.activation(shift[:], x[:], ACT.Copy, scale=factor[:])
+            if MODE[n] == "S":
+                return turn(n, shift, False, True)
+            centred = work.tile([P, SLOTS], F32, name=f"centred{n}", tag="centred")
+            for c in range(0, SLOTS, SLOTS // 2):
+                cols = slice(c, c + SLOTS // 2)
+                nc.gpsimd.tensor_tensor(centred[:, cols], shift[:, cols], state[("pdp", n)][:, cols], ALU.add)
+            turn(n, centred, True, True)
+
         def gradient(n):
-            g = work.tile([P, P, PACK], BF16, name="g", align_bytes=64)
+            g = work.tile([P, P, PACK], BF16, name=f"g{n}", tag="g", align_bytes=64)
             nc.vector.tensor_tensor(
                 g[:], state[("grad", n)][:].rearrange("s u r -> s r u"),
                 ts_place[:].unsqueeze(1).to_broadcast([P, P, PACK]), ALU.mult,
@@ -342,13 +336,13 @@ def tile_attend_gsma_q_pl_kernel(
 
         def query_gradient(n):
             h, t = divmod(n, PACK)
-            g_codes = work.tile([P, P], U32, name="g_codes", align_bytes=64)
-            g_scales = work.tile([P, P], U8, name="g_scales", align_bytes=64)
+            g_codes = work.tile([P, P], U32, name=f"g_codes{n}", tag="g_codes", align_bytes=64)
+            g_scales = work.tile([P, P], U8, name=f"g_scales{n}", tag="g_scales", align_bytes=64)
             nc.vector.quantize_mx(
                 out=g_codes[:].bitcast(E5M2), scales=g_scales[:], in_=state[("g", n)][:].rearrange("s r u -> s (r u)")
             )
-            bank = psum.tile([P, FEATURES], F32, name="out_bank", tag="out", bufs=BANKS)
-            for again in range(WARM.count(n)):
+            bank = psum.tile([P, FEATURES], F32, name=f"out_bank{n}", tag="out", bufs=BANKS)
+            for again in range(WARM_OUT.count(n)):
                 result_pass(bank, *state["last"])
             result_pass(bank, g_codes, g_scales)
             state["last"] = (g_codes, g_scales)
@@ -375,85 +369,77 @@ def tile_attend_gsma_q_pl_kernel(
                 )
 
         def store_scales():
-            rows = out_2.rearrange("h f c -> f h c").bitcast(I32)
-            for quad in range(4):
-                queue = nc.scalar if quad % 2 == 0 else nc.sync
-                queue.dma_start(rows[4 * quad : 4 * quad + 4], plane_scales[32 * quad : 32 * quad + 4].bitcast(I32))
+            rows = out_2.rearrange("h (q r) c -> r q h c", r=4).bitcast(I32)
+            for row in range(4):
+                nc.scalar.dma_start(rows[row], plane_scales[row:P:32].bitcast(I32))
 
         def live(n):
             return 0 <= n < TILES
 
         score_pass(0)
+        score_pass(1)
+        kt_woven.append(turn_keys(1, "q_raw0"))
+        do_woven, parts = deal(do_raw[0], "do0", DO0_CUTS)
+        run(parts)
         nc.vector.tensor_tensor(
             uswt[:, :, 0], us_sb[:].rearrange("p h t -> p (h t)"), wt_sb[:].rearrange("p h t -> p (h t)"), ALU.mult
         )
-        score_pass(1)
-        q_woven = deal(q_raw, 1, "q1", Q1_V)
-        for n in range(0, LEAD, 2):
-            scores(n)
-            scores(n + 1)
-            if n == Q1_AFTER:
-                q_mx.append(quantise("q1", q_woven, E4M3))
-            for later in range(n + 2, min(n + 4, LEAD + 1, TILES)):
-                score_pass(later)
-            softmax(n)
-            softmax(n + 1)
-            if n == DO0_AFTER:
-                do_woven = deal(do_raw, 0, "do0", DO0_V)
-        v_codes = pick(vw_win[:].bitcast(U32), "v_codes", U32)
+        nc.vector.quantize_mx(out=kt_mx[0][:, 1].bitcast(E4M3), scales=kt_mx[1][:, 1], in_=kt_woven[1])
+        scores(0)
+        score_pass(2)
+        scores(1)
+        score_pass(3)
+        softmax(0)
+        softmax(1)
         do_mx = [quantise("do0", do_woven, E5M2)]
+        v_codes = pick(vw_win[:].bitcast(U32), "v_codes", U32)
         values_pass(0)
         values_pass(1)
         row_factors(0)
+        scores(2)
         row_factors(1)
-        first = keep.tile([P, PASS, PACK], BF16, name="result0_woven", align_bytes=64, tag="k_picked")
-
-        def weave_first(piece, copy):
-            part = slice(piece * PIECE // 4, (piece + 1) * PIECE // 4)
-            copy(first[:].rearrange("p (c i) t -> p c t i", i=4)[:, part], result[0][:].rearrange("p t (c i) -> p c t i", i=4)[:, part])
-
-        for step in range(TILES + 1):
-            ahead = step + LEAD
-            fresh = ahead < TILES
+        softmax(2)
+        q_woven, q_parts = deal(q_raw[1], "q1", Q1_CUTS)
+        do_woven, do_parts = deal(do_raw[1], "do1", DO1_CUTS)
+        run(q_parts[:Q1_FIRST])
+        for step in range(TILES + LAG):
+            ahead = AHEAD[step] if step < len(AHEAD) else ()
             if live(step):
                 row_sum(step)
-            if 2 <= step + FACT < TILES:
-                row_factors(step + FACT)
-            if live(step) and step not in SHIFT_V:
+            if live(step) and MODE[step] in "SG":
                 centre(step)
-            if step == OUT0_AT:
-                for piece in range(OUT0_V, PACK):
-                    if piece >= PACK - R0_G:
-                        cols = slice(piece * PIECE, (piece + 1) * PIECE)
-                        nc.gpsimd.tensor_scalar(
-                            first[:, cols], result[0][:, :, cols].rearrange("p t c -> p c t"), 1.0, 0.0, ALU.mult, ALU.add
-                        )
-                    else:
-                        weave_first(piece, nc.scalar.copy)
-            if step == TILES:
-                planes(0, first[:].rearrange("p c t -> p (c t)"))
-            if fresh:
-                scores(ahead)
-            if live(step - 1):
-                gradient(step - 1)
-            if live(step) and step in SHIFT_V:
-                centre(step)
-            if fresh:
-                softmax(ahead)
-            if live(step - 1):
-                query_gradient(step - 1)
-            if step == DO1W_AT:
-                do_woven = deal(do_raw, 1, "do1", DO1_V)
-            if step == DO1_AT:
-                do_mx.append(quantise("do1", do_woven, E5M2))
-            if ahead + 1 < TILES:
-                score_pass(ahead + 1)
             if live(step + 2):
                 values_pass(step + 2)
+            for n in ahead[:1]:
+                scores(n)
+            if live(step - LAG):
+                gradient(step - LAG)
+            if live(step) and MODE[step] in "UV":
+                centre(step)
+            for n in ahead[1:]:
+                scores(n)
+            for n in ahead:
+                softmax(n)
+            if step == 0:
+                run(q_parts[Q1_FIRST:])
+            if step == DO1W:
+                run(do_parts)
+            if live(step - LAG):
+                query_gradient(step - LAG)
+            if step == Q1Q:
+                q_mx.append(quantise("q1", q_woven, E4M3))
+                score_pass(4)
+                score_pass(5)
+            if step == DO1Q:
+                do_mx.append(quantise("do1", do_woven, E5M2))
+            for n in ahead:
+                if 6 <= n + 2 < TILES:
+                    score_pass(n + 2)
+            if step == P0W:
+                first = keep.tile([P, PASS, PACK], BF16, name="result0_woven", align_bytes=64, tag=P0_TAG)
+                first_woven = weave(first, result[0], [(on_scalar, 0, PASS, PIECE)])
+        planes(0, first_woven)
         last = keep.tile([P, PASS, PACK], BF16, name="result1_woven", align_bytes=64, tag="q1_woven")
-        shares(
-            last[:].rearrange("p (c i) t -> p c t i", i=4), result[1][:].rearrange("p t (c i) -> p c t i", i=4),
-            PASS, OUT1_V, PASS // 2,
-        )
-        planes(1, last[:].rearrange("p c t -> p (c t)"))
+        last_woven = weave(last, result[1], [(on_vector, 0, LAST_V, PASS // 2), (on_scalar, LAST_V, PASS, PIECE)])
+        planes(1, last_woven)
         store_scales()

@@ -37,8 +37,8 @@ LAST_V = 384
 MODE = "SSSSSSVV"
 LAG = 1
 P0W = 7
-WARM_OUT = ()
-WARM_VALUE = ()
+WARM_OUT = (5,)
+WARM_VALUE = (3, 4, 5, 6, 7)
 AHEAD = ((3,), (4,), (5,), (6,), (7,))
 Z_HOLD = {}
 Q1_FIRST = 4

@@ -26,11 +26,10 @@ TILES = QUERIES // P
 
 FLOPS = 3 * 2 * QUERIES * SLOTS * FEATURES
 
-BANKS = 2
 PIECE = 128
-LOADS = ("q0", "us", "wt", "do0", "q1", "vw", "do1")
-Q0_CUTS = (("V", 0, 288, 512), ("S", 288, 512, 128))
-DO0_CUTS = (("S", 0, 256, 128), ("G", 256, 512, 64))
+LOADS = ("q", "us", "wt", "do", "vw")
+Q0_CUTS = (("V", 0, 352, 512), ("S", 352, 512, 160))
+DO0_CUTS = (("S", 0, 512, 128),)
 Q1_CUTS = (("S", 0, 512, 128),)
 DO1_CUTS = (("S", 0, 512, 128),)
 LAST_V = 384
@@ -39,13 +38,20 @@ LAG = 1
 P0W = 7
 WARM_OUT = (5,)
 WARM_VALUE = (3, 4, 5, 6, 7)
-AHEAD = ((3,), (4,), (5,), (6,), (7,))
-Z_HOLD = {}
-Q1_FIRST = 4
-K_V = 352
+AHEAD = ((4,), (5,), (6,), (7,))
+Z_HOLD = {4: 8192, 5: 10240}
+K_V = 512
 P0_TAG = "x5"
 DO1W = 0
-Q1Q = 0
+LEAD = 4
+STORE = (4, 2)
+PAIRS = 0
+P0Q_TAG = "g_last"
+LATE = 6
+P0_G = 0
+Q1_AT = 2
+DO0_AT = 2
+DO0_PIECES = 1
 DO1Q = 1
 
 
@@ -56,7 +62,8 @@ def tile_attend_gsma_q_pl_kernel(
     with ExitStack() as ctx:
         keep = ctx.enter_context(tc.tile_pool(name="keep", bufs=1))
         work = ctx.enter_context(tc.tile_pool(name="work", bufs=3))
-        psum = ctx.enter_context(tc.psum_pool(name="psum", bufs=2))
+        spent = ctx.enter_context(tc.tile_pool(name="spent", bufs=1))
+        psum = ctx.enter_context(tc.psum_pool(name="psum", bufs=1))
 
         k_planes = kT.rearrange("(p t) c -> t p c", t=PACK)
         offsets = keep.tile([P, SLOTS // 16], U16, name="offsets")
@@ -74,16 +81,14 @@ def tile_attend_gsma_q_pl_kernel(
             nc.scalar.dma_start(vs_win[row:P:32, :].bitcast(I32), vT_scales[0, row:16:4, :].bitcast(I32))
         for t in range(PACK):
             nc.sync.dma_start(k_win[t][:], k_planes[t])
-        q_raw = [keep.tile([P, PACK, PASS], F32, name=f"q_raw{h}", align_bytes=64) for h in range(HALVES)]
-        do_raw = [keep.tile([P, PACK, PASS], F32, name=f"do_raw{h}", align_bytes=64) for h in range(HALVES)]
+        q_raw = keep.tile([P, PACK, QUERIES], F32, name="q_raw", align_bytes=64)
+        do_raw = keep.tile([P, PACK, QUERIES], F32, name="do_raw", align_bytes=64)
         us_sb = keep.tile([P, HALVES, PACK], F32, name="us_sb")
         wt_sb = keep.tile([P, HALVES, PACK], F32, name="wt_sb")
-        vw_win = keep.tile([P, TOKENS], I32, name="vw_win", align_bytes=64)
-        q_rows = qT.rearrange("(p j) (h r) -> h p j r", j=PACK, h=HALVES)
-        do_rows = doT.rearrange("(p j) (h r) -> h p j r", j=PACK, h=HALVES)
+        vw_win = spent.tile([P, TOKENS], I32, name="vw_win", align_bytes=64, offset=0)
         loads = {
-            "q0": (q_raw[0][:], q_rows[0]), "q1": (q_raw[1][:], q_rows[1]),
-            "do0": (do_raw[0][:], do_rows[0]), "do1": (do_raw[1][:], do_rows[1]),
+            "q": (q_raw[:], qT.rearrange("(p j) r -> p j r", j=PACK)),
+            "do": (do_raw[:], doT.rearrange("(p j) r -> p j r", j=PACK)),
             "us": (us_sb[:], us.rearrange("(h p t) o -> p h (t o)", h=HALVES, t=PACK)),
             "wt": (wt_sb[:], wt.rearrange("(h p t) o -> p h (t o)", h=HALVES, t=PACK)),
             "vw": (vw_win[:], vT_words[0].rearrange("p c l -> p (c l)").bitcast(I32)),
@@ -108,20 +113,20 @@ def tile_attend_gsma_q_pl_kernel(
             nc.vector.tensor_copy(picked[:], window.indirect(offsets[:]))
             return picked
 
-        def fill_window(window, flat, name):
-            turned = psum.tile([P, P], F32, name=name + "_turned", tag="out", bufs=BANKS)
+        def fill_window(window, flat, name, tag):
+            turned = psum.tile([P, P], F32, name=name + "_turned", tag=tag)
             nc.tensor.transpose(turned[:], flat[:], ident[:])
             columns = keep.tile([P, TOKENS // P], F32, name=name + "_columns")
             nc.scalar.copy(columns[:], turned[:, : TOKENS // P])
             for b in range(TOKENS // PASS):
-                spread = psum.tile([P, PACK, P], F32, name=name + "_spread", tag=("score", "value")[b % 2], bufs=BANKS)
+                spread = psum.tile([P, PACK, P], F32, name=name + "_spread", tag=("score0", "value0", "score1", "value1")[b])
                 for j in range(PACK):
                     column = columns[:, PACK * b + j : PACK * b + j + 1]
                     nc.tensor.transpose(spread[:, j, :], column.to_broadcast([P, P]), ident[:])
                 nc.scalar.copy(window[:, b * PASS : (b + 1) * PASS], spread[:].rearrange("r j n -> r (j n)"))
 
-        fill_window(ts_win, ts_flat, "ts")
-        fill_window(tv_win, tv_flat, "tv")
+        fill_window(ts_win, ts_flat, "ts", "out0")
+        fill_window(tv_win, tv_flat, "tv", "out1")
 
         k_picked = keep.tile([P, PACK, SLOTS], BF16, name="k_picked", align_bytes=64)
 
@@ -129,7 +134,7 @@ def tile_attend_gsma_q_pl_kernel(
             nc.vector.tensor_copy(k_picked[:, t, :], k_win[t][:].indirect(offsets[:]))
 
         def turn_keys(pair, tag):
-            bank = psum.tile([P, 2, 2, P], F32, name=f"kt_bank{pair}", tag=("score", "grad")[pair], bufs=BANKS)
+            bank = psum.tile([P, 2, 2, P], F32, name=f"kt_bank{pair}", tag=("score1", "grad0")[pair])
             for e in range(2):
                 words = k_picked[:, 2 * pair + e, :].bitcast(F32).rearrange("p (s u) -> p u s", u=2)
                 for u in range(2):
@@ -150,7 +155,7 @@ def tile_attend_gsma_q_pl_kernel(
         gather_keys(1)
         tv_rows = token_rows(tv_win, "tv")[:].rearrange("r u s -> r (u s)")
         kt_woven = [turn_keys(0, "")]
-        turned = psum.tile([P, PACK, P], F32, name="ts_place_turned", tag="out", bufs=BANKS)
+        turned = psum.tile([P, PACK, P], F32, name="ts_place_turned", tag="out0")
         for u in range(PACK):
             nc.tensor.transpose(turned[:, u, :], ts_rows[:, u, :], ident[:])
         ts_place = keep.tile([P, PACK], F32, name="ts_place")
@@ -178,11 +183,14 @@ def tile_attend_gsma_q_pl_kernel(
             return woven[:].rearrange("p c t -> p (c t)")
 
         def deal(raw, name, cuts):
-            woven = keep.tile([P, PACK, P, PACK], BF16, name=name + "_woven", align_bytes=64)
+            if name == "do0":
+                woven = spent.tile([P, PACK, P, PACK], BF16, name=name + "_woven", align_bytes=64, offset=4 * TOKENS)
+            else:
+                woven = keep.tile([P, PACK, P, PACK], BF16, name=name + "_woven", align_bytes=64)
             parts = []
             for engine, first, last, piece in cuts:
                 order = "p m t j" if engine == "G" else "p m j t"
-                dst, src = woven[:].rearrange("p t m j -> " + order), raw[:].rearrange("p j (m t) -> " + order, t=PACK)
+                dst, src = woven[:].rearrange("p t m j -> " + order), raw.rearrange("p j (m t) -> " + order, t=PACK)
                 copy = {"V": nc.vector.tensor_copy, "S": nc.scalar.copy, "G": by_gpsimd}[engine]
                 for c in range(first, last, piece):
                     part = slice(c // 4, min(c + piece, last) // 4)
@@ -194,7 +202,10 @@ def tile_attend_gsma_q_pl_kernel(
                 copy(dst, src)
 
         def quantise(name, source, fmt, pieces=1, tag=""):
-            codes = keep.tile([P, PASS], U32, name=name + "_codes", align_bytes=64, tag=tag)
+            if name == "do0":
+                codes = spent.tile([P, PASS], U32, name=name + "_codes", align_bytes=64, offset=0)
+            else:
+                codes = keep.tile([P, PASS], U32, name=name + "_codes", align_bytes=64, tag=tag)
             scales = keep.tile([P, PASS], U8, name=name + "_scales", align_bytes=64)
             width = PASS // pieces
             for i in range(pieces):
@@ -208,12 +219,14 @@ def tile_attend_gsma_q_pl_kernel(
         on_vector, on_scalar = nc.vector.tensor_copy, nc.scalar.copy
         k_woven = keep.tile([P, PASS, PACK], BF16, name="k_woven", align_bytes=64)
         k_codes, k_scales = quantise("k", weave(k_woven, k_picked, [(on_vector, 0, K_V, PASS // 2), (on_scalar, K_V, PASS, PASS)]), E4M3, pieces=2)
-        q_woven, parts = deal(q_raw[0], "q0", Q0_CUTS)
+        kt_woven.append(turn_keys(1, ""))
+        nc.vector.quantize_mx(out=kt_mx[0][:, 1].bitcast(E4M3), scales=kt_mx[1][:, 1], in_=kt_woven[1])
+        q_woven, parts = deal(q_raw[:, :, :PASS], "q0", Q0_CUTS)
         run(parts)
         q_mx = [quantise("q0", q_woven, E4M3, pieces=4)]
 
         result = [keep.tile([P, PACK, FEATURES], F32, name=f"result{h}", tag=f"k_win{3 * h}", align_bytes=64) for h in range(HALVES)]
-        out_rows = out_0.rearrange("(h p t) d -> h t p d", h=HALVES, t=PACK)
+        out_rows = out_0.rearrange("(h p t) d -> h p t d", h=HALVES, t=PACK)
         uswt = keep.tile([P, TILES, 2], F32, name="uswt")
         nc.vector.memset(uswt[:, :, 1], -1.0)
         state = {}
@@ -221,7 +234,7 @@ def tile_attend_gsma_q_pl_kernel(
         def values_pass(n):
             h, t = divmod(n, PACK)
             cols = slice(t * P, (t + 1) * P)
-            bank = psum.tile([P, SLOTS], F32, name="b_bank", tag="value", bufs=BANKS)
+            bank = psum.tile([P, SLOTS], F32, name=f"b_bank{n}", tag=("value", "score")[n >= LATE] + str(n % 2))
             for again in range(1 + WARM_VALUE.count(n)):
                 nc.tensor.matmul_mx(
                     out=bank[:], lhsT=do_mx[h][0][:, cols].bitcast(E5M2), lhsT_scale=do_mx[h][1][:, cols],
@@ -238,7 +251,7 @@ def tile_attend_gsma_q_pl_kernel(
         def score_pass(n):
             h, t = divmod(n, PACK)
             cols = slice(t * P, (t + 1) * P)
-            bank = psum.tile([P, SLOTS], F32, name="score_bank", tag="score", bufs=BANKS)
+            bank = psum.tile([P, SLOTS], F32, name=f"score_bank{n}", tag=f"score{n % 2}")
             nc.tensor.matmul_mx(
                 out=bank[:], lhsT=q_mx[h][0][:, cols].bitcast(E4M3), lhsT_scale=q_mx[h][1][:, cols],
                 rhs=k_codes[:].bitcast(E4M3), rhs_scale=k_scales[:], start=True, stop=True,
@@ -248,7 +261,7 @@ def tile_attend_gsma_q_pl_kernel(
         def scores(n):
             h, t = divmod(n, PACK)
             if n in Z_HOLD:
-                z = keep.tile([P, SLOTS], F32, name=f"z{n}", tag=Z_HOLD[n], align_bytes=64)
+                z = spent.tile([P, SLOTS], F32, name=f"z{n}", align_bytes=64, offset=Z_HOLD[n])
             else:
                 z = work.tile([P, SLOTS], F32, name=f"z{n}", tag="z", bufs=4)
             nc.vector.scalar_tensor_tensor(
@@ -268,7 +281,7 @@ def tile_attend_gsma_q_pl_kernel(
                 cols = slice(c, c + SLOTS // 2)
                 nc.gpsimd.tensor_tensor(xv[:, cols], x[:, cols], tv_rows[:, cols], ALU.mult)
             state[("x", n)] = (x, xv, total)
-            if n >= 2:
+            if n >= LEAD:
                 row_factors(n)
 
         def row_factors(n):
@@ -279,8 +292,8 @@ def tile_attend_gsma_q_pl_kernel(
             state[("rows", n)] = (gate[:, 0:1], gate[:, 1:2])
 
         def row_sum(n):
-            pdp = work.tile([P, SLOTS], F32, name=f"pdp{n}", tag="pdp")
-            delta = work.tile([P, 1], F32, name=f"delta{n}", tag="delta")
+            pdp = work.tile([P, SLOTS], F32, name=f"pdp{n}", tag="pdp", bufs=4)
+            delta = work.tile([P, 1], F32, name=f"delta{n}", tag="delta", bufs=4)
             nc.vector.scalar_tensor_tensor(
                 as_laid(pdp), by_place(state[("b", n)][:]), state[("rows", n)][0], as_laid(state[("x", n)][1]),
                 ALU.mult, ALU.mult, accum_out=delta[:],
@@ -292,7 +305,7 @@ def tile_attend_gsma_q_pl_kernel(
 
         def turn(n, tile, opens, closes):
             if opens:
-                state[("grad", n)] = psum.tile([P, PACK, P], F32, name=f"grad_bank{n}_", tag="grad", bufs=BANKS)
+                state[("grad", n)] = psum.tile([P, PACK, P], F32, name=f"grad_bank{n}_", tag=("grad", "value")[n >= LATE] + str(n % 2))
             for u in range(PACK):
                 nc.tensor.matmul(
                     state[("grad", n)][:, u, :], tile[:, u * P : (u + 1) * P], ident[:],
@@ -301,7 +314,7 @@ def tile_attend_gsma_q_pl_kernel(
 
         def centre(n):
             delta, x = state[("delta", n)], state[("x", n)][0]
-            shift = work.tile([P, SLOTS], F32, name=f"shift{n}", tag="shift")
+            shift = work.tile([P, SLOTS], F32, name=f"shift{n}", tag="shift", bufs=4)
             if MODE[n] == "V":
                 nc.vector.tensor_scalar(shift[:], x[:], delta[:], state[("rows", n)][1], ALU.mult, ALU.mult)
                 return turn(n, shift, False, True)
@@ -320,7 +333,10 @@ def tile_attend_gsma_q_pl_kernel(
             turn(n, centred, True, True)
 
         def gradient(n):
-            g = work.tile([P, P, PACK], BF16, name=f"g{n}", tag="g", align_bytes=64)
+            if n == TILES - 1:
+                g = keep.tile([P, P, PACK], BF16, name="g_last", align_bytes=64)
+            else:
+                g = work.tile([P, P, PACK], BF16, name=f"g{n}", tag="g", align_bytes=64)
             nc.vector.tensor_tensor(
                 g[:], state[("grad", n)][:].rearrange("s u r -> s r u"),
                 ts_place[:].unsqueeze(1).to_broadcast([P, P, PACK]), ALU.mult,
@@ -341,7 +357,7 @@ def tile_attend_gsma_q_pl_kernel(
             nc.vector.quantize_mx(
                 out=g_codes[:].bitcast(E5M2), scales=g_scales[:], in_=state[("g", n)][:].rearrange("s r u -> s (r u)")
             )
-            bank = psum.tile([P, FEATURES], F32, name=f"out_bank{n}", tag="out", bufs=BANKS)
+            bank = psum.tile([P, FEATURES], F32, name=f"out_bank{n}", tag=f"out{n % 2}")
             for again in range(WARM_OUT.count(n)):
                 result_pass(bank, *state["last"])
             result_pass(bank, g_codes, g_scales)
@@ -351,12 +367,14 @@ def tile_attend_gsma_q_pl_kernel(
             pieces = 2 if n == TILES - 1 else 1
             for c in range(0, P, P // pieces):
                 nc.scalar.copy(features[:, c : c + P // pieces], columns[:, c : c + P // pieces])
-            nc.sync.dma_start(out_rows[h, t], result[h][:, t, :])
+            group = STORE[h]
+            if t % group == group - 1:
+                nc.sync.dma_start(out_rows[h, :, t + 1 - group : t + 1], result[h][:, t + 1 - group : t + 1, :])
 
         plane_scales = keep.tile([P, HALVES, FEATURES], U8, name="plane_scales", align_bytes=64)
 
         def planes(h, woven):
-            codes = keep.tile([P, FEATURES], U32, name=f"plane{h}_codes", align_bytes=64)
+            codes = keep.tile([P, FEATURES], U32, name=f"plane{h}_codes", tag=(P0Q_TAG, "")[h], align_bytes=64)
             width = FEATURES // (1 + h)
             for c in range(0, FEATURES, width):
                 nc.vector.quantize_mx(
@@ -378,35 +396,49 @@ def tile_attend_gsma_q_pl_kernel(
 
         score_pass(0)
         score_pass(1)
-        kt_woven.append(turn_keys(1, "q_raw0"))
-        do_woven, parts = deal(do_raw[0], "do0", DO0_CUTS)
-        run(parts)
         nc.vector.tensor_tensor(
             uswt[:, :, 0], us_sb[:].rearrange("p h t -> p (h t)"), wt_sb[:].rearrange("p h t -> p (h t)"), ALU.mult
         )
-        nc.vector.quantize_mx(out=kt_mx[0][:, 1].bitcast(E4M3), scales=kt_mx[1][:, 1], in_=kt_woven[1])
-        scores(0)
-        score_pass(2)
-        scores(1)
-        score_pass(3)
-        softmax(0)
-        softmax(1)
-        do_mx = [quantise("do0", do_woven, E5M2)]
+        q_woven, parts = deal(q_raw[:, :, PASS:], "q1", Q1_CUTS)
+        run(parts)
+        for n in range(0, LEAD, 2):
+            if n == Q1_AT:
+                q_mx.append(quantise("q1", q_woven, E4M3))
+            if n == 4:
+                score_pass(4)
+                score_pass(5)
+            if n == DO0_AT:
+                do_woven, parts = deal(do_raw[:, :, :PASS], "do0", DO0_CUTS)
+                run(parts)
+            scores(n)
+            if n + 2 != 4:
+                score_pass(n + 2)
+            scores(n + 1)
+            if n + 2 != 4:
+                score_pass(n + 3)
+            softmax(n)
+            softmax(n + 1)
+        if LEAD == 4:
+            score_pass(4)
+            score_pass(5)
         v_codes = pick(vw_win[:].bitcast(U32), "v_codes", U32)
+        row_factors(0)
+        row_factors(1)
+        do_mx = [quantise("do0", do_woven, E5M2, pieces=DO0_PIECES)]
         values_pass(0)
         values_pass(1)
-        row_factors(0)
-        scores(2)
-        row_factors(1)
-        softmax(2)
-        q_woven, q_parts = deal(q_raw[1], "q1", Q1_CUTS)
-        do_woven, do_parts = deal(do_raw[1], "do1", DO1_CUTS)
-        run(q_parts[:Q1_FIRST])
+        for n in range(2, LEAD):
+            row_factors(n)
+        do_woven, do_parts = deal(do_raw[:, :, PASS:], "do1", DO1_CUTS)
         for step in range(TILES + LAG):
             ahead = AHEAD[step] if step < len(AHEAD) else ()
-            if live(step):
+            if step < TILES - 1:
                 row_sum(step)
-            if live(step) and MODE[step] in "SG":
+            if step == TILES - 2:
+                row_sum(step + 1)
+                centre(step)
+                centre(step + 1)
+            if step < TILES - 2 and MODE[step] in "SG":
                 centre(step)
             if live(step + 2):
                 values_pass(step + 2)
@@ -414,30 +446,32 @@ def tile_attend_gsma_q_pl_kernel(
                 scores(n)
             if live(step - LAG):
                 gradient(step - LAG)
-            if live(step) and MODE[step] in "UV":
+            if step < TILES - 2 and MODE[step] in "UV":
                 centre(step)
             for n in ahead[1:]:
                 scores(n)
             for n in ahead:
                 softmax(n)
-            if step == 0:
-                run(q_parts[Q1_FIRST:])
             if step == DO1W:
                 run(do_parts)
             if live(step - LAG):
                 query_gradient(step - LAG)
-            if step == Q1Q:
-                q_mx.append(quantise("q1", q_woven, E4M3))
-                score_pass(4)
-                score_pass(5)
             if step == DO1Q:
                 do_mx.append(quantise("do1", do_woven, E5M2))
             for n in ahead:
-                if 6 <= n + 2 < TILES:
+                if n + 2 < TILES:
                     score_pass(n + 2)
-            if step == P0W:
+            if PAIRS and step in (1 + LAG, 3 + LAG):
+                if step == 1 + LAG:
+                    first = keep.tile([P, PASS, PACK], BF16, name="result0_woven", align_bytes=64, tag=P0_TAG)
+                    first_woven = first[:].rearrange("p c t -> p (c t)")
+                pair = slice(step - LAG - 1, step - LAG + 1)
+                for c in range(0, PASS, PASS // PAIRS):
+                    cols = slice(c, c + PASS // PAIRS)
+                    nc.scalar.copy(first[:, cols, pair], result[0][:, pair, cols].rearrange("p t c -> p c t"))
+            if step == P0W and not PAIRS:
                 first = keep.tile([P, PASS, PACK], BF16, name="result0_woven", align_bytes=64, tag=P0_TAG)
-                first_woven = weave(first, result[0], [(on_scalar, 0, PASS, PIECE)])
+                first_woven = weave(first, result[0], [(by_gpsimd, 0, P0_G, 64), (on_scalar, P0_G, PASS, PIECE)])
         planes(0, first_woven)
         last = keep.tile([P, PASS, PACK], BF16, name="result1_woven", align_bytes=64, tag="q1_woven")
         last_woven = weave(last, result[1], [(on_vector, 0, LAST_V, PASS // 2), (on_scalar, LAST_V, PASS, PIECE)])

@@ -33,26 +33,18 @@ DO0_CUTS = (("S", 0, 512, 128),)
 Q1_CUTS = (("S", 0, 512, 128),)
 DO1_CUTS = (("S", 0, 512, 128),)
 LAST_V = 384
-MODE = "SSSSSSVV"
-LAG = 1
-P0W = 7
-WARM_OUT = (5,)
-WARM_VALUE = (3, 4, 5, 6, 7)
-AHEAD = ((4,), (5,), (6,), (7,))
-Z_HOLD = {4: 8192, 5: 10240}
-K_V = 512
-P0_TAG = "x5"
-DO1W = 0
-LEAD = 4
+MODE = "SSSSSSSS"
+WARM_OUT = ()
+WARM_VALUE = ()
+K_V = 352
+P0_TAG = "x7"
 STORE = (4, 2)
-PAIRS = 0
-P0Q_TAG = "g_last"
+P0Q_TAG = "g6"
 LATE = 6
-P0_G = 0
-Q1_AT = 2
-DO0_AT = 2
-DO0_PIECES = 1
-DO1Q = 1
+K_PIECES = 1
+XV_PIECES = 2
+Q_APART = (4, 6)
+P0_S = 256
 
 
 def tile_attend_gsma_q_pl_kernel(
@@ -133,39 +125,34 @@ def tile_attend_gsma_q_pl_kernel(
         def gather_keys(t):
             nc.vector.tensor_copy(k_picked[:, t, :], k_win[t][:].indirect(offsets[:]))
 
-        def turn_keys(pair, tag):
+        kt_woven = keep.tile([P, 2, P, 2, 2], F32, name="kt_woven", align_bytes=64)
+
+        def turn_keys(pair):
             bank = psum.tile([P, 2, 2, P], F32, name=f"kt_bank{pair}", tag=("score1", "grad0")[pair])
             for e in range(2):
                 words = k_picked[:, 2 * pair + e, :].bitcast(F32).rearrange("p (s u) -> p u s", u=2)
                 for u in range(2):
                     nc.tensor.transpose(bank[:, e, u, :], words[:, u, :], ident[:])
-            woven = keep.tile([P, P, 2, 2], F32, name=f"kt_woven{pair}", tag=tag, align_bytes=64)
-            nc.scalar.copy(woven[:], bank[:].rearrange("s e u p -> s p e u"))
-            return woven[:].rearrange("s p e u -> s (p e u)").bitcast(BF16)
+            nc.scalar.copy(kt_woven[:, pair], bank[:].rearrange("s e u p -> s p e u"))
 
-        def token_rows(window, name):
-            rows = keep.tile([P, PACK, P], F32, name=name + "_rows")
+        def token_rows(window, name, tag):
+            rows = keep.tile([P, PACK, P], F32, name=name + "_rows", tag=tag)
             picked = pick(window[:], name + "_picked", F32)
             nc.scalar.copy(rows[:].rearrange("r u s -> r s u"), picked[:].rearrange("r (s u) -> r s u", u=PACK))
             return rows
 
         gather_keys(0)
         v_scales = pick(vs_win[:], "v_scales", U8)
-        ts_rows = token_rows(ts_win, "ts")
+        ts_rows = token_rows(ts_win, "ts", "tv_columns")
         gather_keys(1)
-        tv_rows = token_rows(tv_win, "tv")[:].rearrange("r u s -> r (u s)")
-        kt_woven = [turn_keys(0, "")]
+        tv_rows = token_rows(tv_win, "tv", "")[:].rearrange("r u s -> r (u s)")
+        turn_keys(0)
         turned = psum.tile([P, PACK, P], F32, name="ts_place_turned", tag="out0")
         for u in range(PACK):
             nc.tensor.transpose(turned[:, u, :], ts_rows[:, u, :], ident[:])
         ts_place = keep.tile([P, PACK], F32, name="ts_place")
         nc.scalar.activation(ts_place[:], turned[:, :, 0], ACT.Copy)
         gather_keys(2)
-        kt_mx = (
-            keep.tile([P, 2, FEATURES // 2], U32, name="kt_codes", align_bytes=64),
-            keep.tile([P, 2, FEATURES // 2], U8, name="kt_scales", align_bytes=64),
-        )
-        nc.vector.quantize_mx(out=kt_mx[0][:, 0].bitcast(E4M3), scales=kt_mx[1][:, 0], in_=kt_woven[0])
         gather_keys(3)
 
         def by_gpsimd(dst, src):
@@ -218,17 +205,19 @@ def tile_attend_gsma_q_pl_kernel(
 
         on_vector, on_scalar = nc.vector.tensor_copy, nc.scalar.copy
         k_woven = keep.tile([P, PASS, PACK], BF16, name="k_woven", align_bytes=64)
-        k_codes, k_scales = quantise("k", weave(k_woven, k_picked, [(on_vector, 0, K_V, PASS // 2), (on_scalar, K_V, PASS, PASS)]), E4M3, pieces=2)
-        kt_woven.append(turn_keys(1, ""))
-        nc.vector.quantize_mx(out=kt_mx[0][:, 1].bitcast(E4M3), scales=kt_mx[1][:, 1], in_=kt_woven[1])
+        k_codes, k_scales = quantise("k", weave(k_woven, k_picked, [(on_vector, 0, K_V, PASS // 2), (on_scalar, K_V, PASS, PASS)]), E4M3, pieces=K_PIECES)
+        turn_keys(1)
         q_woven, parts = deal(q_raw[:, :, :PASS], "q0", Q0_CUTS)
         run(parts)
-        q_mx = [quantise("q0", q_woven, E4M3, pieces=4)]
+        q_mx = [quantise("q0", q_woven, E4M3, pieces=2)]
 
         result = [keep.tile([P, PACK, FEATURES], F32, name=f"result{h}", tag=f"k_win{3 * h}", align_bytes=64) for h in range(HALVES)]
         out_rows = out_0.rearrange("(h p t) d -> h p t d", h=HALVES, t=PACK)
         uswt = keep.tile([P, TILES, 2], F32, name="uswt")
-        nc.vector.memset(uswt[:, :, 1], -1.0)
+        nc.gpsimd.memset(uswt[:, :, 1], -1.0)
+        nc.gpsimd.tensor_tensor(
+            uswt[:, :, 0], us_sb[:].rearrange("p h t -> p (h t)"), wt_sb[:].rearrange("p h t -> p (h t)"), ALU.mult
+        )
         state = {}
 
         def values_pass(n):
@@ -246,7 +235,7 @@ def tile_attend_gsma_q_pl_kernel(
             return view.rearrange("r (s u) -> r u s", u=PACK)
 
         def as_laid(tile):
-            return tile[:].rearrange("r (u s) -> r u s", u=PACK)
+            return tile.rearrange("r (u s) -> r u s", u=PACK)
 
         def score_pass(n):
             h, t = divmod(n, PACK)
@@ -258,44 +247,46 @@ def tile_attend_gsma_q_pl_kernel(
             )
             state[("a", n)] = bank
 
-        def scores(n):
-            h, t = divmod(n, PACK)
-            if n in Z_HOLD:
-                z = spent.tile([P, SLOTS], F32, name=f"z{n}", align_bytes=64, offset=Z_HOLD[n])
+        def scores(first):
+            if first == PACK:
+                z = spent.tile([P, 2, SLOTS], F32, name=f"z{first}", align_bytes=64, offset=4 * TOKENS)
             else:
-                z = work.tile([P, SLOTS], F32, name=f"z{n}", tag="z", bufs=4)
-            nc.vector.scalar_tensor_tensor(
-                as_laid(z), by_place(state[("a", n)][:]), us_sb[:, h, t : t + 1], ts_rows[:], ALU.mult, ALU.mult
-            )
-            state[("z", n)] = z
+                z = work.tile([P, 2, SLOTS], F32, name=f"z{first}", tag="z", bufs=2)
+            for i in range(2):
+                h, t = divmod(first + i, PACK)
+                nc.vector.scalar_tensor_tensor(
+                    as_laid(z[:, i]), by_place(state[("a", first + i)][:]), us_sb[:, h, t : t + 1], ts_rows[:], ALU.mult, ALU.mult
+                )
+            state[("z", first)] = z
 
-        def softmax(n):
-            z = state[("z", n)][:]
-            neg_max = work.tile([P, 1], F32, name=f"neg_max{n}", tag="neg_max")
-            nc.vector.tensor_reduce(neg_max[:], z, AXIS.X, ALU.max, negate=True)
-            x = keep.tile([P, SLOTS], F32, name=f"x{n}", align_bytes=64)
-            total = work.tile([P, 1], F32, name=f"total{n}", tag="total", bufs=TILES)
-            nc.scalar.activation(x[:], z, ACT.Exp, bias=neg_max[:], accum_out=total[:])
-            xv = keep.tile([P, SLOTS], F32, name=f"xv{n}", align_bytes=64)
-            for c in range(0, SLOTS, SLOTS // 2):
-                cols = slice(c, c + SLOTS // 2)
-                nc.gpsimd.tensor_tensor(xv[:, cols], x[:, cols], tv_rows[:, cols], ALU.mult)
-            state[("x", n)] = (x, xv, total)
-            if n >= LEAD:
-                row_factors(n)
+        def softmax(first):
+            z = state[("z", first)]
+            neg_max = work.tile([P, 2], F32, name=f"neg_max{first}", tag="neg_max")
+            nc.vector.tensor_reduce(neg_max[:], z[:], AXIS.X, ALU.max, negate=True)
+            total = work.tile([P, 2], F32, name=f"total{first}", tag="total", bufs=PACK)
+            state[("total", first)] = total
+            for i in range(2):
+                x = keep.tile([P, SLOTS], F32, name=f"x{first + i}", align_bytes=64)
+                nc.scalar.activation(x[:], z[:, i], ACT.Exp, bias=neg_max[:, i : i + 1], accum_out=total[:, i : i + 1])
+                xv = keep.tile([P, SLOTS], F32, name=f"xv{first + i}", align_bytes=64)
+                for c in range(0, SLOTS, SLOTS // XV_PIECES):
+                    cols = slice(c, c + SLOTS // XV_PIECES)
+                    nc.gpsimd.tensor_tensor(xv[:, cols], x[:, cols], tv_rows[:, cols], ALU.mult)
+                state[("x", first + i)] = (x, xv)
 
-        def row_factors(n):
-            inverse = work.tile([P, 1], F32, name=f"inverse{n}", tag="inverse", bufs=TILES)
-            nc.vector.reciprocal(inverse[:], state[("x", n)][2][:])
-            gate = work.tile([P, 2], F32, name=f"gate{n}", tag="gate", bufs=TILES)
-            nc.scalar.activation(gate[:], uswt[:, n, :], ACT.Copy, scale=inverse[:])
-            state[("rows", n)] = (gate[:, 0:1], gate[:, 1:2])
+        def row_factors(first):
+            inverse = work.tile([P, 2], F32, name=f"inverse{first}", tag="inverse", bufs=PACK)
+            nc.vector.reciprocal(inverse[:], state[("total", first)][:])
+            for i in range(2):
+                gate = work.tile([P, 2], F32, name=f"gate{first + i}", tag="gate", bufs=TILES)
+                nc.scalar.activation(gate[:], uswt[:, first + i, :], ACT.Copy, scale=inverse[:, i : i + 1])
+                state[("rows", first + i)] = (gate[:, 0:1], gate[:, 1:2])
 
         def row_sum(n):
             pdp = work.tile([P, SLOTS], F32, name=f"pdp{n}", tag="pdp", bufs=4)
             delta = work.tile([P, 1], F32, name=f"delta{n}", tag="delta", bufs=4)
             nc.vector.scalar_tensor_tensor(
-                as_laid(pdp), by_place(state[("b", n)][:]), state[("rows", n)][0], as_laid(state[("x", n)][1]),
+                as_laid(pdp[:]), by_place(state[("b", n)][:]), state[("rows", n)][0], as_laid(state[("x", n)][1][:]),
                 ALU.mult, ALU.mult, accum_out=delta[:],
             )
             state[("delta", n)] = delta
@@ -332,44 +323,47 @@ def tile_attend_gsma_q_pl_kernel(
                 nc.gpsimd.tensor_tensor(centred[:, cols], shift[:, cols], state[("pdp", n)][:, cols], ALU.add)
             turn(n, centred, True, True)
 
-        def gradient(n):
-            if n == TILES - 1:
-                g = keep.tile([P, P, PACK], BF16, name="g_last", align_bytes=64)
-            else:
-                g = work.tile([P, P, PACK], BF16, name=f"g{n}", tag="g", align_bytes=64)
-            nc.vector.tensor_tensor(
-                g[:], state[("grad", n)][:].rearrange("s u r -> s r u"),
-                ts_place[:].unsqueeze(1).to_broadcast([P, P, PACK]), ALU.mult,
-            )
-            state[("g", n)] = g
+        def gradient(first):
+            g = keep.tile([P, 2, P, PACK], BF16, name=f"g{first}", align_bytes=64)
+            for i in range(2):
+                nc.vector.tensor_tensor(
+                    g[:, i], state[("grad", first + i)][:].rearrange("s u r -> s r u"),
+                    ts_place[:].unsqueeze(1).to_broadcast([P, P, PACK]), ALU.mult,
+                )
+            state[("g", first)] = g
 
         def result_pass(bank, codes, scales):
             nc.tensor.matmul_mx(
-                out=bank[:], lhsT=codes[:].bitcast(E5M2), lhsT_scale=scales[:],
-                rhs=kt_mx[0][:].rearrange("s a c -> s (a c)").bitcast(E4M3), rhs_scale=kt_mx[1][:].rearrange("s a c -> s (a c)"),
-                start=True, stop=True,
+                out=bank[:], lhsT=codes.bitcast(E5M2), lhsT_scale=scales,
+                rhs=kt_mx[0][:].bitcast(E4M3), rhs_scale=kt_mx[1][:], start=True, stop=True,
             )
 
-        def query_gradient(n):
-            h, t = divmod(n, PACK)
-            g_codes = work.tile([P, P], U32, name=f"g_codes{n}", tag="g_codes", align_bytes=64)
-            g_scales = work.tile([P, P], U8, name=f"g_scales{n}", tag="g_scales", align_bytes=64)
-            nc.vector.quantize_mx(
-                out=g_codes[:].bitcast(E5M2), scales=g_scales[:], in_=state[("g", n)][:].rearrange("s r u -> s (r u)")
-            )
-            bank = psum.tile([P, FEATURES], F32, name=f"out_bank{n}", tag=f"out{n % 2}")
-            for again in range(WARM_OUT.count(n)):
+        def query_gradient(first):
+            g_codes = keep.tile([P, 2 * P], U32, name=f"g_codes{first}", align_bytes=64)
+            g_scales = keep.tile([P, 2 * P], U8, name=f"g_scales{first}", align_bytes=64)
+            source = state[("g", first)][:].rearrange("s i r u -> s (i r u)")
+            width = P if first in Q_APART else 2 * P
+            for c in range(0, 2 * P, width):
+                nc.vector.quantize_mx(
+                    out=g_codes[:, c : c + width].bitcast(E5M2), scales=g_scales[:, c : c + width],
+                    in_=source[:, c * PACK : (c + width) * PACK],
+                )
+            for i in range(2):
+                n = first + i
+                h, t = divmod(n, PACK)
+                bank = psum.tile([P, FEATURES], F32, name=f"out_bank{n}", tag=f"out{i}")
+                for again in range(WARM_OUT.count(n)):
+                    result_pass(bank, *state["last"])
+                state["last"] = (g_codes[:, i * P : (i + 1) * P], g_scales[:, i * P : (i + 1) * P])
                 result_pass(bank, *state["last"])
-            result_pass(bank, g_codes, g_scales)
-            state["last"] = (g_codes, g_scales)
-            features = result[h][:, t, :].rearrange("r (p a e) -> r p a e", a=2, e=2)
-            columns = bank[:].rearrange("r (a p e) -> r p a e", a=2, e=2)
-            pieces = 2 if n == TILES - 1 else 1
-            for c in range(0, P, P // pieces):
-                nc.scalar.copy(features[:, c : c + P // pieces], columns[:, c : c + P // pieces])
-            group = STORE[h]
-            if t % group == group - 1:
-                nc.sync.dma_start(out_rows[h, :, t + 1 - group : t + 1], result[h][:, t + 1 - group : t + 1, :])
+                features = result[h][:, t, :].rearrange("r (p a e) -> r p a e", a=2, e=2)
+                columns = bank[:].rearrange("r (a p e) -> r p a e", a=2, e=2)
+                pieces = 2 if n == TILES - 1 else 1
+                for c in range(0, P, P // pieces):
+                    nc.scalar.copy(features[:, c : c + P // pieces], columns[:, c : c + P // pieces])
+                group = STORE[h]
+                if t % group == group - 1:
+                    nc.sync.dma_start(out_rows[h, :, t + 1 - group : t + 1], result[h][:, t + 1 - group : t + 1, :])
 
         plane_scales = keep.tile([P, HALVES, FEATURES], U8, name="plane_scales", align_bytes=64)
 
@@ -391,87 +385,65 @@ def tile_attend_gsma_q_pl_kernel(
             for row in range(4):
                 nc.scalar.dma_start(rows[row], plane_scales[row:P:32].bitcast(I32))
 
-        def live(n):
-            return 0 <= n < TILES
+        def both(step, first):
+            step(first)
+            step(first + 1)
 
-        score_pass(0)
-        score_pass(1)
-        nc.vector.tensor_tensor(
-            uswt[:, :, 0], us_sb[:].rearrange("p h t -> p (h t)"), wt_sb[:].rearrange("p h t -> p (h t)"), ALU.mult
-        )
+        both(score_pass, 0)
+        kt_mx = quantise("kt", kt_woven[:].rearrange("s a p e u -> s (a p e u)").bitcast(BF16), E4M3)
         q_woven, parts = deal(q_raw[:, :, PASS:], "q1", Q1_CUTS)
         run(parts)
-        for n in range(0, LEAD, 2):
-            if n == Q1_AT:
-                q_mx.append(quantise("q1", q_woven, E4M3))
-            if n == 4:
-                score_pass(4)
-                score_pass(5)
-            if n == DO0_AT:
-                do_woven, parts = deal(do_raw[:, :, :PASS], "do0", DO0_CUTS)
-                run(parts)
-            scores(n)
-            if n + 2 != 4:
-                score_pass(n + 2)
-            scores(n + 1)
-            if n + 2 != 4:
-                score_pass(n + 3)
-            softmax(n)
-            softmax(n + 1)
-        if LEAD == 4:
-            score_pass(4)
-            score_pass(5)
+        scores(0)
+        both(score_pass, 2)
+        softmax(0)
+        q_mx.append(quantise("q1", q_woven, E4M3))
+        do_woven, parts = deal(do_raw[:, :, :PASS], "do0", DO0_CUTS)
+        run(parts)
+        scores(2)
+        both(score_pass, 4)
+        softmax(2)
         v_codes = pick(vw_win[:].bitcast(U32), "v_codes", U32)
         row_factors(0)
-        row_factors(1)
-        do_mx = [quantise("do0", do_woven, E5M2, pieces=DO0_PIECES)]
-        values_pass(0)
-        values_pass(1)
-        for n in range(2, LEAD):
-            row_factors(n)
-        do_woven, do_parts = deal(do_raw[:, :, PASS:], "do1", DO1_CUTS)
-        for step in range(TILES + LAG):
-            ahead = AHEAD[step] if step < len(AHEAD) else ()
-            if step < TILES - 1:
-                row_sum(step)
-            if step == TILES - 2:
-                row_sum(step + 1)
-                centre(step)
-                centre(step + 1)
-            if step < TILES - 2 and MODE[step] in "SG":
-                centre(step)
-            if live(step + 2):
-                values_pass(step + 2)
-            for n in ahead[:1]:
-                scores(n)
-            if live(step - LAG):
-                gradient(step - LAG)
-            if step < TILES - 2 and MODE[step] in "UV":
-                centre(step)
-            for n in ahead[1:]:
-                scores(n)
-            for n in ahead:
-                softmax(n)
-            if step == DO1W:
-                run(do_parts)
-            if live(step - LAG):
-                query_gradient(step - LAG)
-            if step == DO1Q:
-                do_mx.append(quantise("do1", do_woven, E5M2))
-            for n in ahead:
-                if n + 2 < TILES:
-                    score_pass(n + 2)
-            if PAIRS and step in (1 + LAG, 3 + LAG):
-                if step == 1 + LAG:
-                    first = keep.tile([P, PASS, PACK], BF16, name="result0_woven", align_bytes=64, tag=P0_TAG)
-                    first_woven = first[:].rearrange("p c t -> p (c t)")
-                pair = slice(step - LAG - 1, step - LAG + 1)
-                for c in range(0, PASS, PASS // PAIRS):
-                    cols = slice(c, c + PASS // PAIRS)
-                    nc.scalar.copy(first[:, cols, pair], result[0][:, pair, cols].rearrange("p t c -> p c t"))
-            if step == P0W and not PAIRS:
-                first = keep.tile([P, PASS, PACK], BF16, name="result0_woven", align_bytes=64, tag=P0_TAG)
-                first_woven = weave(first, result[0], [(by_gpsimd, 0, P0_G, 64), (on_scalar, P0_G, PASS, PIECE)])
+        do_mx = [quantise("do0", do_woven, E5M2)]
+        both(values_pass, 0)
+        row_factors(2)
+        do_woven, parts = deal(do_raw[:, :, PASS:], "do1", DO1_CUTS)
+
+        both(row_sum, 0)
+        both(centre, 0)
+        both(values_pass, 2)
+        scores(4)
+        both(score_pass, 6)
+        softmax(4)
+        run(parts)
+        do_mx.append(quantise("do1", do_woven, E5M2))
+
+        gradient(0)
+        row_sum(2)
+        query_gradient(0)
+        row_sum(3)
+        both(centre, 2)
+        both(values_pass, 4)
+        scores(6)
+        row_factors(4)
+        softmax(6)
+        both(values_pass, 6)
+
+        gradient(2)
+        row_sum(4)
+        query_gradient(2)
+        row_sum(5)
+        both(centre, 4)
+        row_factors(6)
+        both(row_sum, 6)
+        both(centre, 6)
+
+        gradient(4)
+        query_gradient(4)
+        gradient(6)
+        query_gradient(6)
+        first = keep.tile([P, PASS, PACK], BF16, name="result0_woven", align_bytes=64, tag=P0_TAG)
+        first_woven = weave(first, result[0], [(on_scalar, 0, P0_S, PIECE), (on_vector, P0_S, PASS, PASS)])
         planes(0, first_woven)
         last = keep.tile([P, PASS, PACK], BF16, name="result1_woven", align_bytes=64, tag="q1_woven")
         last_woven = weave(last, result[1], [(on_vector, 0, LAST_V, PASS // 2), (on_scalar, LAST_V, PASS, PIECE)])

from contextlib import ExitStack

import concourse.mybir as mybir

F32 = mybir.dt.float32
BF16 = mybir.dt.bfloat16
I32 = mybir.dt.int32
U32 = mybir.dt.uint32
U16 = mybir.dt.uint16
U8 = mybir.dt.uint8
E4M3 = mybir.dt.float8_e4m3fn_x4
E5M2 = mybir.dt.float8_e5m2_x4
ALU = mybir.AluOpType
ACT = mybir.ActivationFunctionType
AXIS = mybir.AxisListType

P = 128
PACK = 4
PASS = P * PACK
TOKENS = 2048
SLOTS = 512
FEATURES = 512
QUERIES = 1024
HALVES = QUERIES // PASS
TILES = QUERIES // P

FLOPS = 3 * 2 * QUERIES * SLOTS * FEATURES

PIECE = 128
LOADS = ("q", "us", "wt", "do", "vw")
Q0_CUTS = (("V", 0, 352, 512), ("S", 352, 512, 160))
DO0_CUTS = (("S", 0, 512, 128),)
Q1_CUTS = (("S", 0, 512, 128),)
DO1_CUTS = (("S", 0, 512, 128),)
LAST_V = 384
MODE = "SSSSSSSS"
WARM_OUT = ()
WARM_VALUE = ()
K_V = 352
P0_TAG = "x7"
STORE = (4, 2)
P0Q_TAG = "g6"
LATE = 6
K_PIECES = 1
XV_PIECES = 2
Q_APART = (4, 6)
P0_S = 256


def tile_attend_gsma_q_pl_kernel(
    tc, qT, kT, doT, vT_words, vT_scales, us, ts, tv, wt, offs, out_0, out_1, out_2
):
    nc = tc.nc
    with ExitStack() as ctx:
        keep = ctx.enter_context(tc.tile_pool(name="keep", bufs=1))
        work = ctx.enter_context(tc.tile_pool(name="work", bufs=3))
        spent = ctx.enter_context(tc.tile_pool(name="spent", bufs=1))
        psum = ctx.enter_context(tc.psum_pool(name="psum", bufs=1))

        k_planes = kT.rearrange("(p t) c -> t p c", t=PACK)
        offsets = keep.tile([P, SLOTS // 16], U16, name="offsets")
        k_win = [keep.tile([P, TOKENS], F32, name=f"k_win{t}", align_bytes=64) for t in range(PACK)]
        vs_win = keep.tile([P, TOKENS], U8, name="vs_win")
        ts_win = keep.tile([P, TOKENS], F32, name="ts_win", align_bytes=64)
        tv_win = keep.tile([P, TOKENS], F32, name="tv_win", align_bytes=64)
        ts_flat = keep.tile([P, P], F32, name="ts_flat")
        tv_flat = keep.tile([P, P], F32, name="tv_flat")
        nc.vector.memset(vs_win[:].bitcast(I32), 0)
        nc.sync.dma_start(offsets[:], offs)
        nc.scalar.dma_start(ts_flat[:], ts[0 : P * P // TOKENS, :].rearrange("r (j n) -> (r j) n", n=P))
        nc.scalar.dma_start(tv_flat[:], tv[0 : P * P // TOKENS, :].rearrange("r (j n) -> (r j) n", n=P))
        for row in range(4):
            nc.scalar.dma_start(vs_win[row:P:32, :].bitcast(I32), vT_scales[0, row:16:4, :].bitcast(I32))
        for t in range(PACK):
            nc.sync.dma_start(k_win[t][:], k_planes[t])
        q_raw = keep.tile([P, PACK, QUERIES], F32, name="q_raw", align_bytes=64)
        do_raw = keep.tile([P, PACK, QUERIES], F32, name="do_raw", align_bytes=64)
        us_sb = keep.tile([P, HALVES, PACK], F32, name="us_sb")
        wt_sb = keep.tile([P, HALVES, PACK], F32, name="wt_sb")
        vw_win = spent.tile([P, TOKENS], I32, name="vw_win", align_bytes=64, offset=0)
        loads = {
            "q": (q_raw[:], qT.rearrange("(p j) r -> p j r", j=PACK)),
            "do": (do_raw[:], doT.rearrange("(p j) r -> p j r", j=PACK)),
            "us": (us_sb[:], us.rearrange("(h p t) o -> p h (t o)", h=HALVES, t=PACK)),
            "wt": (wt_sb[:], wt.rearrange("(h p t) o -> p h (t o)", h=HALVES, t=PACK)),
            "vw": (vw_win[:], vT_words[0].rearrange("p c l -> p (c l)").bitcast(I32)),
        }
        for key in LOADS:
            nc.sync.dma_start(*loads[key])

        ident = keep.tile([P, P], F32, name="ident")
        ones = keep.tile([P, P], F32, name="ones")
        ramp = keep.tile([P, P], F32, name="ramp", align_bytes=64)
        ramp_turned = keep.tile([P, P], F32, name="ramp_turned", align_bytes=64)
        nc.vector.memset(ones[:], 1.0)
        nc.vector.memset(ident[:], 0.0)
        nc.vector.tensor_tensor_scan(ramp[:], ones[:], ones[:], 0.0, ALU.mult, ALU.add)
        nc.vector.transpose(ramp_turned[:], ramp[:])
        for quad in range(4):
            block = slice(32 * quad, 32 * quad + 32)
            nc.vector.tensor_tensor(ident[block, block], ramp[block, block], ramp_turned[block, block], ALU.is_equal)

        def pick(window, name, dtype):
            picked = keep.tile([P, SLOTS], dtype, name=name, align_bytes=64)
            nc.vector.tensor_copy(picked[:], window.indirect(offsets[:]))
            return picked

        def fill_window(window, flat, name, tag):
            turned = psum.tile([P, P], F32, name=name + "_turned", tag=tag)
            nc.tensor.transpose(turned[:], flat[:], ident[:])
            columns = keep.tile([P, TOKENS // P], F32, name=name + "_columns")
            nc.scalar.copy(columns[:], turned[:, : TOKENS // P])
            for b in range(TOKENS // PASS):
                spread = psum.tile([P, PACK, P], F32, name=name + "_spread", tag=("score0", "value0", "score1", "value1")[b])
                for j in range(PACK):
                    column = columns[:, PACK * b + j : PACK * b + j + 1]
                    nc.tensor.transpose(spread[:, j, :], column.to_broadcast([P, P]), ident[:])
                nc.scalar.copy(window[:, b * PASS : (b + 1) * PASS], spread[:].rearrange("r j n -> r (j n)"))

        fill_window(ts_win, ts_flat, "ts", "out0")
        fill_window(tv_win, tv_flat, "tv", "out1")

        k_picked = keep.tile([P, PACK, SLOTS], BF16, name="k_picked", align_bytes=64)

        def gather_keys(t):
            nc.vector.tensor_copy(k_picked[:, t, :], k_win[t][:].indirect(offsets[:]))

        kt_woven = keep.tile([P, 2, P, 2, 2], F32, name="kt_woven", align_bytes=64)

        def turn_keys(pair):
            bank = psum.tile([P, 2, 2, P], F32, name=f"kt_bank{pair}", tag=("score1", "grad0")[pair])
            for e in range(2):
                words = k_picked[:, 2 * pair + e, :].bitcast(F32).rearrange("p (s u) -> p u s", u=2)
                for u in range(2):
                    nc.tensor.transpose(bank[:, e, u, :], words[:, u, :], ident[:])
            nc.scalar.copy(kt_woven[:, pair], bank[:].rearrange("s e u p -> s p e u"))

        def token_rows(window, name, tag):
            rows = keep.tile([P, PACK, P], F32, name=name + "_rows", tag=tag)
            picked = pick(window[:], name + "_picked", F32)
            nc.scalar.copy(rows[:].rearrange("r u s -> r s u"), picked[:].rearrange("r (s u) -> r s u", u=PACK))
            return rows

        gather_keys(0)
        v_scales = pick(vs_win[:], "v_scales", U8)
        ts_rows = token_rows(ts_win, "ts", "tv_columns")
        gather_keys(1)
        tv_rows = token_rows(tv_win, "tv", "")[:].rearrange("r u s -> r (u s)")
        turn_keys(0)
        turned = psum.tile([P, PACK, P], F32, name="ts_place_turned", tag="out0")
        for u in range(PACK):
            nc.tensor.transpose(turned[:, u, :], ts_rows[:, u, :], ident[:])
        ts_place = keep.tile([P, PACK], F32, name="ts_place")
        nc.scalar.activation(ts_place[:], turned[:, :, 0], ACT.Copy)
        gather_keys(2)
        gather_keys(3)

        def by_gpsimd(dst, src):
            nc.gpsimd.tensor_scalar(dst, src, 1.0, 0.0, ALU.mult, ALU.add)

        def shares(dst, src, cuts):
            for copy, first, last, piece in cuts:
                for c in range(first, last, piece):
                    part = slice(c // 4, min(c + piece, last) // 4)
                    copy(dst[:, part], src[:, part])

        def weave(woven, planes_tile, cuts):
            src = planes_tile[:].rearrange("p t (c i) -> p c t i", i=4)
            shares(woven[:].rearrange("p (c i) t -> p c t i", i=4), src, cuts)
            return woven[:].rearrange("p c t -> p (c t)")

        def deal(raw, name, cuts):
            if name == "do0":
                woven = spent.tile([P, PACK, P, PACK], BF16, name=name + "_woven", align_bytes=64, offset=4 * TOKENS)
            else:
                woven = keep.tile([P, PACK, P, PACK], BF16, name=name + "_woven", align_bytes=64)
            parts = []
            for engine, first, last, piece in cuts:
                order = "p m t j" if engine == "G" else "p m j t"
                dst, src = woven[:].rearrange("p t m j -> " + order), raw.rearrange("p j (m t) -> " + order, t=PACK)
                copy = {"V": nc.vector.tensor_copy, "S": nc.scalar.copy, "G": by_gpsimd}[engine]
                for c in range(first, last, piece):
                    part = slice(c // 4, min(c + piece, last) // 4)
                    parts.append((copy, dst[:, part], src[:, part]))
            return woven[:].rearrange("p t m j -> p (t m j)"), parts

        def run(parts):
            for copy, dst, src in parts:
                copy(dst, src)

        def quantise(name, source, fmt, pieces=1, tag=""):
            if name == "do0":
                codes = spent.tile([P, PASS], U32, name=name + "_codes", align_bytes=64, offset=0)
            else:
                codes = keep.tile([P, PASS], U32, name=name + "_codes", align_bytes=64, tag=tag)
            scales = keep.tile([P, PASS], U8, name=name + "_scales", align_bytes=64)
            width = PASS // pieces
            for i in range(pieces):
                cols = slice(i * width, (i + 1) * width)
                nc.vector.quantize_mx(
                    out=codes[:, cols].bitcast(fmt), scales=scales[:, cols],
                    in_=source[:, i * width * PACK : (i + 1) * width * PACK],
                )
            return codes, scales

        on_vector, on_scalar = nc.vector.tensor_copy, nc.scalar.copy
        k_woven = keep.tile([P, PASS, PACK], BF16, name="k_woven", align_bytes=64)
        k_codes, k_scales = quantise("k", weave(k_woven, k_picked, [(on_vector, 0, K_V, PASS // 2), (on_scalar, K_V, PASS, PASS)]), E4M3, pieces=K_PIECES)
        turn_keys(1)
        q_woven, parts = deal(q_raw[:, :, :PASS], "q0", Q0_CUTS)
        run(parts)
        q_mx = [quantise("q0", q_woven, E4M3, pieces=2)]

        result = [keep.tile([P, PACK, FEATURES], F32, name=f"result{h}", tag=f"k_win{3 * h}", align_bytes=64) for h in range(HALVES)]
        out_rows = out_0.rearrange("(h p t) d -> h p t d", h=HALVES, t=PACK)
        uswt = keep.tile([P, TILES, 2], F32, name="uswt")
        nc.gpsimd.memset(uswt[:, :, 1], -1.0)
        nc.gpsimd.tensor_tensor(
            uswt[:, :, 0], us_sb[:].rearrange("p h t -> p (h t)"), wt_sb[:].rearrange("p h t -> p (h t)"), ALU.mult
        )
        state = {}

        def values_pass(n):
            h, t = divmod(n, PACK)
            cols = slice(t * P, (t + 1) * P)
            bank = psum.tile([P, SLOTS], F32, name=f"b_bank{n}", tag=("value", "score")[n >= LATE] + str(n % 2))
            for again in range(1 + WARM_VALUE.count(n)):
                nc.tensor.matmul_mx(
                    out=bank[:], lhsT=do_mx[h][0][:, cols].bitcast(E5M2), lhsT_scale=do_mx[h][1][:, cols],
                    rhs=v_codes[:].bitcast(E4M3), rhs_scale=v_scales[:], start=True, stop=True,
                )
            state[("b", n)] = bank

        def by_place(view):
            return view.rearrange("r (s u) -> r u s", u=PACK)

        def as_laid(tile):
            return tile.rearrange("r (u s) -> r u s", u=PACK)

        def score_pass(n):
            h, t = divmod(n, PACK)
            cols = slice(t * P, (t + 1) * P)
            bank = psum.tile([P, SLOTS], F32, name=f"score_bank{n}", tag=f"score{n % 2}")
            nc.tensor.matmul_mx(
                out=bank[:], lhsT=q_mx[h][0][:, cols].bitcast(E4M3), lhsT_scale=q_mx[h][1][:, cols],
                rhs=k_codes[:].bitcast(E4M3), rhs_scale=k_scales[:], start=True, stop=True,
            )
            state[("a", n)] = bank

        def scores(first):
            if first == PACK:
                z = spent.tile([P, 2, SLOTS], F32, name=f"z{first}", align_bytes=64, offset=4 * TOKENS)
            else:
                z = work.tile([P, 2, SLOTS], F32, name=f"z{first}", tag="z", bufs=2)
            for i in range(2):
                h, t = divmod(first + i, PACK)
                nc.vector.scalar_tensor_tensor(
                    as_laid(z[:, i]), by_place(state[("a", first + i)][:]), us_sb[:, h, t : t + 1], ts_rows[:], ALU.mult, ALU.mult
                )
            state[("z", first)] = z

        def softmax(first):
            z = state[("z", first)]
            neg_max = work.tile([P, 2], F32, name=f"neg_max{first}", tag="neg_max")
            nc.vector.tensor_reduce(neg_max[:], z[:], AXIS.X, ALU.max, negate=True)
            total = work.tile([P, 2], F32, name=f"total{first}", tag="total", bufs=PACK)
            state[("total", first)] = total
            for i in range(2):
                x = keep.tile([P, SLOTS], F32, name=f"x{first + i}", align_bytes=64)
                nc.scalar.activation(x[:], z[:, i], ACT.Exp, bias=neg_max[:, i : i + 1], accum_out=total[:, i : i + 1])
                xv = keep.tile([P, SLOTS], F32, name=f"xv{first + i}", align_bytes=64)
                for c in range(0, SLOTS, SLOTS // XV_PIECES):
                    cols = slice(c, c + SLOTS // XV_PIECES)
                    nc.gpsimd.tensor_tensor(xv[:, cols], x[:, cols], tv_rows[:, cols], ALU.mult)
                state[("x", first + i)] = (x, xv)

        def row_factors(first):
            inverse = work.tile([P, 2], F32, name=f"inverse{first}", tag="inverse", bufs=PACK)
            nc.vector.reciprocal(inverse[:], state[("total", first)][:])
            for i in range(2):
                gate = work.tile([P, 2], F32, name=f"gate{first + i}", tag="gate", bufs=TILES)
                nc.scalar.activation(gate[:], uswt[:, first + i, :], ACT.Copy, scale=inverse[:, i : i + 1])
                state[("rows", first + i)] = (gate[:, 0:1], gate[:, 1:2])

        def row_sum(n):
            pdp = work.tile([P, SLOTS], F32, name=f"pdp{n}", tag="pdp", bufs=4)
            delta = work.tile([P, 1], F32, name=f"delta{n}", tag="delta", bufs=4)
            nc.vector.scalar_tensor_tensor(
                as_laid(pdp[:]), by_place(state[("b", n)][:]), state[("rows", n)][0], as_laid(state[("x", n)][1][:]),
                ALU.mult, ALU.mult, accum_out=delta[:],
            )
            state[("delta", n)] = delta
            state[("pdp", n)] = pdp
            if MODE[n] in "SV":
                turn(n, pdp, True, False)

        def turn(n, tile, opens, closes):
            if opens:
                state[("grad", n)] = psum.tile([P, PACK, P], F32, name=f"grad_bank{n}_", tag=("grad", "value")[n >= LATE] + str(n % 2))
            for u in range(PACK):
                nc.tensor.matmul(
                    state[("grad", n)][:, u, :], tile[:, u * P : (u + 1) * P], ident[:],
                    start=opens and u == 0, stop=closes and u == PACK - 1, is_transpose=True,
                )

        def centre(n):
            delta, x = state[("delta", n)], state[("x", n)][0]
            shift = work.tile([P, SLOTS], F32, name=f"shift{n}", tag="shift", bufs=4)
            if MODE[n] == "V":
                nc.vector.tensor_scalar(shift[:], x[:], delta[:], state[("rows", n)][1], ALU.mult, ALU.mult)
                return turn(n, shift, False, True)
            factor = work.tile([P, 1], F32, name=f"factor{n}", tag="factor")
            nc.scalar.activation(factor[:], delta[:], ACT.Copy, scale=state[("rows", n)][1])
            if MODE[n] == "U":
                nc.vector.scalar_tensor_tensor(shift[:], x[:], factor[:], state[("pdp", n)][:], ALU.mult, ALU.add)
                return turn(n, shift, True, True)
            nc.scalar.activation(shift[:], x[:], ACT.Copy, scale=factor[:])
            if MODE[n] == "S":
                return turn(n, shift, False, True)
            centred = work.tile([P, SLOTS], F32, name=f"centred{n}", tag="centred")
            for c in range(0, SLOTS, SLOTS // 2):
                cols = slice(c, c + SLOTS // 2)
                nc.gpsimd.tensor_tensor(centred[:, cols], shift[:, cols], state[("pdp", n)][:, cols], ALU.add)
            turn(n, centred, True, True)

        def gradient(first):
            g = keep.tile([P, 2, P, PACK], BF16, name=f"g{first}", align_bytes=64)
            for i in range(2):
                nc.vector.tensor_tensor(
                    g[:, i], state[("grad", first + i)][:].rearrange("s u r -> s r u"),
                    ts_place[:].unsqueeze(1).to_broadcast([P, P, PACK]), ALU.mult,
                )
            state[("g", first)] = g

        def result_pass(bank, codes, scales):
            nc.tensor.matmul_mx(
                out=bank[:], lhsT=codes.bitcast(E5M2), lhsT_scale=scales,
                rhs=kt_mx[0][:].bitcast(E4M3), rhs_scale=kt_mx[1][:], start=True, stop=True,
            )

        def query_gradient(first):
            g_codes = keep.tile([P, 2 * P], U32, name=f"g_codes{first}", align_bytes=64)
            g_scales = keep.tile([P, 2 * P], U8, name=f"g_scales{first}", align_bytes=64)
            source = state[("g", first)][:].rearrange("s i r u -> s (i r u)")
            width = P if first in Q_APART else 2 * P
            for c in range(0, 2 * P, width):
                nc.vector.quantize_mx(
                    out=g_codes[:, c : c + width].bitcast(E5M2), scales=g_scales[:, c : c + width],
                    in_=source[:, c * PACK : (c + width) * PACK],
                )
            for i in range(2):
                n = first + i
                h, t = divmod(n, PACK)
                bank = psum.tile([P, FEATURES], F32, name=f"out_bank{n}", tag=f"out{i}")
                for again in range(WARM_OUT.count(n)):
                    result_pass(bank, *state["last"])
                state["last"] = (g_codes[:, i * P : (i + 1) * P], g_scales[:, i * P : (i + 1) * P])
                result_pass(bank, *state["last"])
                features = result[h][:, t, :].rearrange("r (p a e) -> r p a e", a=2, e=2)
                columns = bank[:].rearrange("r (a p e) -> r p a e", a=2, e=2)
                pieces = 2 if n == TILES - 1 else 1
                for c in range(0, P, P // pieces):
                    nc.scalar.copy(features[:, c : c + P // pieces], columns[:, c : c + P // pieces])
                group = STORE[h]
                if t % group == group - 1:
                    nc.sync.dma_start(out_rows[h, :, t + 1 - group : t + 1], result[h][:, t + 1 - group : t + 1, :])

        plane_scales = keep.tile([P, HALVES, FEATURES], U8, name="plane_scales", align_bytes=64)

        def planes(h, woven):
            codes = keep.tile([P, FEATURES], U32, name=f"plane{h}_codes", tag=(P0Q_TAG, "")[h], align_bytes=64)
            width = FEATURES // (1 + h)
            for c in range(0, FEATURES, width):
                nc.vector.quantize_mx(
                    out=codes[:, c : c + width].bitcast(E4M3), scales=plane_scales[:, h, c : c + width],
                    in_=woven[:, c * PACK : (c + width) * PACK],
                )
                nc.sync.dma_start(
                    out_1[h].rearrange("p c l -> p (c l)").bitcast(I32)[:, c : c + width],
                    codes[:, c : c + width].bitcast(I32),
                )

        def store_scales():
            rows = out_2.rearrange("h (q r) c -> r q h c", r=4).bitcast(I32)
            for row in range(4):
                nc.scalar.dma_start(rows[row], plane_scales[row:P:32].bitcast(I32))

        def both(step, first):
            step(first)
            step(first + 1)

        both(score_pass, 0)
        kt_mx = quantise("kt", kt_woven[:].rearrange("s a p e u -> s (a p e u)").bitcast(BF16), E4M3)
        q_woven, parts = deal(q_raw[:, :, PASS:], "q1", Q1_CUTS)
        run(parts)
        scores(0)
        both(score_pass, 2)
        softmax(0)
        q_mx.append(quantise("q1", q_woven, E4M3))
        do_woven, parts = deal(do_raw[:, :, :PASS], "do0", DO0_CUTS)
        run(parts)
        scores(2)
        both(score_pass, 4)
        softmax(2)
        v_codes = pick(vw_win[:].bitcast(U32), "v_codes", U32)
        row_factors(0)
        do_mx = [quantise("do0", do_woven, E5M2)]
        both(values_pass, 0)
        row_factors(2)
        do_woven, parts = deal(do_raw[:, :, PASS:], "do1", DO1_CUTS)

        both(row_sum, 0)
        both(centre, 0)
        both(values_pass, 2)
        scores(4)
        both(score_pass, 6)
        softmax(4)
        run(parts)
        do_mx.append(quantise("do1", do_woven, E5M2))

        gradient(0)
        row_sum(2)
        query_gradient(0)
        row_sum(3)
        both(centre, 2)
        both(values_pass, 4)
        scores(6)
        row_factors(4)
        softmax(6)
        both(values_pass, 6)

        gradient(2)
        row_sum(4)
        query_gradient(2)
        row_sum(5)
        both(centre, 4)
        row_factors(6)
        both(row_sum, 6)
        both(centre, 6)

        gradient(4)
        query_gradient(4)
        gradient(6)
        query_gradient(6)
        first = keep.tile([P, PASS, PACK], BF16, name="result0_woven", align_bytes=64, tag=P0_TAG)
        first_woven = weave(first, result[0], [(on_scalar, 0, P0_S, PIECE), (on_vector, P0_S, PASS, PASS)])
        planes(0, first_woven)
        last = keep.tile([P, PASS, PACK], BF16, name="result1_woven", align_bytes=64, tag="q1_woven")
        last_woven = weave(last, result[1], [(on_vector, 0, LAST_V, PASS // 2), (on_scalar, LAST_V, PASS, PIECE)])
        planes(1, last_woven)
        store_scales()
